import numpy as np
import ml_dtypes


def mxq(x, axis, fmt="e4m3"):
    dtype, down = {"e4m3": (ml_dtypes.float8_e4m3fn, 7), "e5m2": (ml_dtypes.float8_e5m2, 14)}[fmt]
    v = np.moveaxis(np.asarray(x, np.float32).astype(ml_dtypes.bfloat16).astype(np.float64), axis, -1)
    blocks = v.reshape(v.shape[:-1] + (-1, 32))
    amax = np.abs(blocks).max(-1, keepdims=True)
    byte = np.maximum(np.where(amax > 0, np.frexp(amax)[1] - 1 + 127, 0) - down, 1)
    scale = np.exp2(byte - 127.0)
    codes = (blocks / scale).astype(np.float32).astype(dtype).astype(np.float64)
    return np.moveaxis((codes * scale).reshape(v.shape), -1, axis)


WIDE = False


def mx_kscale(k):
    if not WIDE:
        return np.ones(k)
    levels = np.array([10, -10, 5, -5, 0])
    if k % 512:
        return np.exp2(np.random.permutation(np.resize(levels, k // 32))).repeat(32)
    a = np.empty((k // 512, 16))
    for p in range(k // 512):
        a[p, :8] = np.random.permutation(np.resize(levels, 8))
        for g in range(8):
            far = levels[np.abs(levels - a[p, g]) >= 10]
            a[p, g + 8] = far[np.random.randint(len(far))]
    return np.exp2(a.ravel()).repeat(32)


def f64(x):
    return np.asarray(x).astype(np.float64)


def striped(idx):
    return np.tile(idx.reshape(-1, 16).T, (8, 1)).astype(np.uint16)


def unstriped(offs):
    return offs[:16].T.reshape(-1).astype(np.int64)


E2M1 = np.array([0.0, 0.5, 1.0, 1.5, 2.0, 3.0, 4.0, 6.0, -0.0, -0.5, -1.0, -1.5, -2.0, -3.0, -4.0, -6.0])


def pack_weight(w, fmt):
    k, n = w.shape
    w = f64(np.asarray(w, np.float32).astype(ml_dtypes.bfloat16)).reshape(k // 32, 32, n)
    amax = np.abs(w).max(1)
    if fmt == "e4m3":
        byte = np.frexp(amax)[1] - 1 + 127 - 7
    else:
        mant, ex = np.frexp(amax / 6.0)
        byte = np.where(mant > 0.5, ex, ex - 1) + 127
    byte = np.clip(np.where(amax > 0, byte, 1), 1, 254)
    scaled = (w * np.exp2(127.0 - byte)[:, None, :]).reshape(k, n).astype(np.float32)
    by_word = np.ascontiguousarray(scaled.reshape(k // 512, 128, 4, n).transpose(0, 1, 3, 2))
    if fmt == "e4m3":
        words = by_word.astype(ml_dtypes.float8_e4m3fn).view(np.uint8)
    else:
        c = by_word.astype(ml_dtypes.float4_e2m1fn).view(np.uint8) & 0xF
        words = (c[..., 0::2] | (c[..., 1::2] << 4)).reshape(k // 512, 128, 2 * n)
    return np.ascontiguousarray(words), np.ascontiguousarray(byte.astype(np.uint8).reshape(k // 512, 16, n))


def unpack_weight(words, scales, fmt):
    g, _, n = scales.shape
    words = np.ascontiguousarray(words).reshape(g, 128, n, -1)
    if fmt == "e4m3":
        vals = words.view(ml_dtypes.float8_e4m3fn).astype(np.float64)
    else:
        nib = np.empty((g, 128, n, 4), np.uint8)
        nib[..., 0::2] = words & 0xF
        nib[..., 1::2] = words >> 4
        vals = E2M1[nib]
    vals = vals * np.repeat(np.exp2(scales.astype(np.float64) - 127.0), 8, axis=1)[..., None]
    return vals.transpose(0, 1, 3, 2).reshape(g * 512, n)


def gelu(v):
    return 0.5 * v * (1.0 + np.tanh(np.sqrt(2.0 / np.pi) * (v + 0.044715 * v**3)))


K, H, N, T, S, T2 = 512, 1024, 384, 4096, 1024, 2048

def setup_inputs():
    n = np.random.standard_normal
    s, u = mx_kscale(K)[:, None], mx_kscale(H)[:, None]
    tab_words, tab_scales = pack_weight(n((K, T)) * s, "e4m3")
    w1_words, w1_scales = pack_weight(n((K, H)) / np.sqrt(K) / s, "e2m1")
    return {
        "tab_words": tab_words, "tab_scales": tab_scales,
        "offs": striped(np.random.permutation(T)[:S]),
        "offs2": striped(np.random.permutation(T2)[:S]),
        "offs3": striped(np.random.permutation(T2)[:S]),
        "w1_words": w1_words, "w1_scales": w1_scales,
        "w2": (n((K, H)) / np.sqrt(K) / s * u.T).astype(np.float32),
        "wg1": np.exp(0.3 * n((128, S))).astype(np.float32),
        "wg2": np.exp(0.3 * n((128, S))).astype(np.float32),
        "gain": (np.exp(0.3 * n(H)) * u[:, 0]).astype(np.float32),
        "weather": (n((H, T2)) * u).astype(np.float32),
        "w3": (n((H, N)) / np.sqrt(H) / u).astype(np.float32),
    }

def reference(tab_words, tab_scales, offs, offs2, offs3, w1_words, w1_scales, w2, wg1, wg2, gain, weather, w3):
    v = unpack_weight(tab_words, tab_scales, "e4m3")[:, unstriped(offs)]
    pollen = unpack_weight(w1_words, w1_scales, "e2m1").T @ v
    stigma = pollen * (mxq(f64(w2), 0, "e4m3").T @ v)
    pageA = np.zeros((H, T2))
    pageA[:, unstriped(offs2)] = np.tile(f64(wg1), (H // 128, 1)) * pollen
    pageB = np.zeros((H, T2))
    pageB[:, unstriped(offs3)] = np.tile(f64(wg2), (H // 128, 1)) * stigma
    ge = 0.5 * pageA * (1 + np.tanh(np.sqrt(2 / np.pi) * (pageA + 0.044715 * pageA ** 3)))
    z = f64(gain)[:, None] * ge + f64(weather) - pageB
    return mxq(f64(w3), 0, "e4m3").T @ mxq(z, 0, "e4m3")

@@ -1,0 +1,354 @@
+from contextlib import ExitStack
+
+import concourse.mybir as mybir
+from concourse.masks import make_identity
+
+K, H, N, T, S, T2 = 512, 1024, 384, 4096, 1024, 2048
+FLOPS = 2 * (2 * K * H * S + H * N * T2)
+
+F32 = mybir.dt.float32
+BF16 = mybir.dt.bfloat16
+I32 = mybir.dt.int32
+U32 = mybir.dt.uint32
+U16 = mybir.dt.uint16
+U8 = mybir.dt.uint8
+FP8X4 = mybir.dt.float8_e4m3fn_x4
+FP4X4 = mybir.dt.float4_e2m1fn_x4
+MULT = mybir.AluOpType.mult
+ADD = mybir.AluOpType.add
+GELU = mybir.ActivationFunctionType.Gelu_apprx_tanh
+COPY = mybir.ActivationFunctionType.Copy
+
+P = 128
+BANK = 512
+SLICES = H // P
+CHUNKS = T2 // BANK
+NT = N // P
+AT_TAB_S = 2112
+AT_ROWS = (4160, 20544)
+AT_PAGE_B = (12352, 28736)
+AT_TAB_W = 16448
+
+
+def tile_list_cherry_pollination_scores_kernel(
+    tc, tab_words, tab_scales, offs, offs2, offs3, w1_words, w1_scales, w2, wg1, wg2, gain, weather, w3, out
+):
+    nc = tc.nc
+    with ExitStack() as ctx:
+        keep = ctx.enter_context(tc.tile_pool(name="keep", bufs=1))
+        work = ctx.enter_context(tc.tile_pool(name="work", bufs=2))
+        shared = ctx.enter_context(tc.tile_pool(name="shared", bufs=1))
+        psum = ctx.enter_context(tc.psum_pool(name="psum", bufs=1))
+
+        def bank(tag):
+            return psum.tile([P, BANK], F32, name=tag, tag=tag)
+
+        list1 = keep.tile([P, S // 16], U16, name="list1")
+        list2 = keep.tile([P, S // 16], U16, name="list2")
+        list3 = keep.tile([P, S // 16], U16, name="list3")
+        tab_w = shared.tile([P, T], I32, name="tab_w", offset=AT_TAB_W)
+        tab_s = shared.tile([P, T], U8, name="tab_s", offset=AT_TAB_S)
+        w1_w = keep.tile([P, 2 * H], U8, name="w1_w", align_bytes=64)
+        w1_s = keep.tile([P, H], U8, name="w1_s", align_bytes=64)
+        wg1_sb = keep.tile([P, S], F32, name="wg1_sb")
+        ident = keep.tile([P, P], F32, name="ident")
+        page_a = [keep.tile([P, T2], F32, name="page_a%d" % i) for i in range(2)]
+        v_w = [keep.tile([P, BANK], U32, name="v_w%d" % i, align_bytes=64) for i in range(2)]
+        v_s = keep.tile([P, S], U8, name="v_s", align_bytes=64)
+        w2_c = keep.tile([P, H], U32, name="w2_c", align_bytes=64)
+        w2_s = keep.tile([P, H], U8, name="w2_s", align_bytes=64)
+        w3_c = keep.tile([P, 2 * N], U32, name="w3_c", align_bytes=64)
+        w3_s = keep.tile([P, 2 * N], U8, name="w3_s", align_bytes=64)
+        partial = {
+            (c, a): keep.tile([P, BANK], F32, name="partial%d%d" % (c, a)) for c in range(1, CHUNKS) for a in range(2)
+        }
+
+        nc.vector.memset(tab_s[:].bitcast(I32), 0)
+        nc.gpsimd.memset(w1_s[:].bitcast(I32), 0)
+        nc.sync.dma_start(list1[:], offs)
+        nc.sync.dma_start(list2[:], offs2)
+        nc.sync.dma_start(list3[:], offs3)
+        nc.sync.dma_start(tab_w[:], tab_words[0].rearrange("p t i -> p (t i)").bitcast(I32))
+        for q in range(4):
+            nc.scalar.dma_start(
+                tab_s[:].bitcast(I32)[32 * q : 32 * q + 4, :], tab_scales[0, 4 * q : 4 * q + 4, :].bitcast(I32)
+            )
+        for q in range(4):
+            nc.gpsimd.dma_start(
+                w1_s[:].bitcast(I32)[32 * q : 32 * q + 4, :], w1_scales[0, 4 * q : 4 * q + 4, :].bitcast(I32)
+            )
+        nc.sync.dma_start(w1_w[:].bitcast(I32), w1_words[0].bitcast(I32))
+        nc.sync.dma_start(wg1_sb[:], wg1)
+        nc.vector.memset(page_a[0][:], 0.0)
+        nc.vector.memset(page_a[1][:], 0.0)
+
+        def interleave(dst, raw):
+            nc.scalar.copy(
+                dst.rearrange("p (c i t) -> p c t i", i=4, t=4),
+                raw.rearrange("p t (c i) -> p c t i", i=4),
+            )
+
+        nc.vector.tensor_copy(v_s[:], tab_s[:].indirect(list1[:]))
+        for h in range(2):
+            nc.vector.tensor_copy(v_w[h][:], tab_w[:].bitcast(U32).indirect(list1[:, 32 * h : 32 * (h + 1)]))
+
+        w2_raw = [shared.tile([P, 4, BANK], F32, name="w2_raw%d" % h, offset=AT_ROWS[h]) for h in range(2)]
+        for h in range(2):
+            nc.sync.dma_start(w2_raw[h][:], w2[:, h * BANK : (h + 1) * BANK].rearrange("(p j) w -> p j w", j=4))
+        wg2_gain = shared.tile([P, S + SLICES], F32, name="wg2_gain", offset=0)
+        wg2_sb = wg2_gain[:, 0:S]
+        gain_sb = wg2_gain[:, S : S + SLICES]
+        with nc.allow_non_contiguous_dma(reason="one gain for each partition and slice"):
+            nc.sync.dma_start(gain_sb, gain.rearrange("(s p) -> p s", p=P))
+        nc.sync.dma_start(wg2_sb, wg2)
+        w2_bf = [keep.tile([P, 4 * BANK], BF16, name="w2_bf", tag="weather%d" % h, align_bytes=64) for h in range(2)]
+
+        def cast_w2(h):
+            interleave(w2_bf[h][:], w2_raw[h][:])
+
+        def quantize_w2(h):
+            cols = slice(h * BANK, (h + 1) * BANK)
+            nc.vector.quantize_mx(out=w2_c[:, cols].bitcast(FP8X4), scales=w2_s[:, cols], in_=w2_bf[h][:])
+
+        def prepare_w3():
+            w3_bf = keep.tile([P, 2 * N * 4], BF16, name="w3_bf", align_bytes=64)
+            for b in range(2):
+                w3_raw = keep.tile([P, 4, N], F32, name="w3_raw", tag="weather1", align_bytes=64)
+                nc.sync.dma_start(w3_raw[:], w3[b * K : (b + 1) * K, :].rearrange("(p j) w -> p j w", j=4))
+                interleave(w3_bf[:, b * 4 * N : (b + 1) * 4 * N], w3_raw[:])
+            for lo, hi in ((0, 512), (512, 768)):
+                nc.vector.quantize_mx(
+                    out=w3_c[:, lo:hi].bitcast(FP8X4), scales=w3_s[:, lo:hi], in_=w3_bf[:, 4 * lo : 4 * hi]
+                )
+
+        pollen = {}
+        stigma = {}
+        h2 = {}
+        scaled = {}
+        weather_sb = {}
+        z_rows = {}
+
+        def make_pollen(s):
+            pollen[s] = work.tile([P, S], F32, name="pollen", tag="pollen", bufs=3)
+            for h in range(2):
+                acc = bank("p%d" % h)
+                nc.tensor.matmul_mx(
+                    out=acc[:],
+                    lhsT=w1_w[:, 2 * P * s : 2 * P * (s + 1)].bitcast(FP4X4),
+                    lhsT_scale=w1_s[:, P * s : P * (s + 1)],
+                    rhs=v_w[h][:].bitcast(FP8X4),
+                    rhs_scale=v_s[:, BANK * h : BANK * (h + 1)],
+                    start=True,
+                    stop=True,
+                )
+                nc.scalar.copy(pollen[s][:, BANK * h : BANK * (h + 1)], acc[:])
+
+        def make_h2(s):
+            h2[s] = work.tile([P, S], F32, name="h2", tag="h2", bufs=2)
+            for h in range(2):
+                acc = bank("h%d" % h)
+                nc.tensor.matmul_mx(
+                    out=acc[:],
+                    lhsT=w2_c[:, P * s : P * (s + 1)].bitcast(FP8X4),
+                    lhsT_scale=w2_s[:, P * s : P * (s + 1)],
+                    rhs=v_w[h][:].bitcast(FP8X4),
+                    rhs_scale=v_s[:, BANK * h : BANK * (h + 1)],
+                    start=True,
+                    stop=True,
+                )
+                nc.scalar.activation(h2[s][:, BANK * h : BANK * (h + 1)], acc[:], COPY, scale=-1.0)
+
+        def make_stigma(s):
+            stigma[s] = work.tile([P, S], F32, name="stigma", tag="stigma", bufs=2)
+            nc.vector.tensor_tensor(stigma[s][:], h2[s][:], pollen[s][:], MULT)
+
+        def scatter_a(s, parts):
+            n = S // parts
+            for i in range(parts):
+                nc.vector.tensor_tensor(
+                    page_a[s % 2][:].indirect(list2[:, i * n // 16 : (i + 1) * n // 16]),
+                    pollen[s][:, i * n : (i + 1) * n],
+                    wg1_sb[:, i * n : (i + 1) * n],
+                    MULT,
+                )
+
+        def scatter_b(s):
+            nc.vector.tensor_tensor(page_b[s % 2][:].indirect(list3[:]), stigma[s][:], wg2_sb, MULT)
+
+        def load_weather(s):
+            weather_sb[s] = keep.tile([P, T2], F32, name="weather_sb", tag="weather%d" % (s % 2), align_bytes=64)
+            nc.sync.dma_start(weather_sb[s][:], weather[P * s : P * (s + 1), :])
+
+        def gelu_gain(s):
+            scaled[s] = shared.tile([P, T2], F32, name="scaled%d" % (s % 2), offset=AT_ROWS[s % 2])
+            for h in range(2):
+                cols = slice(h * T2 // 2, (h + 1) * T2 // 2)
+                nc.scalar.activation(scaled[s][:, cols], page_a[s % 2][:, cols], GELU)
+            for h in range(2):
+                cols = slice(h * T2 // 2, (h + 1) * T2 // 2)
+                nc.scalar.activation(scaled[s][:, cols], scaled[s][:, cols], COPY, scale=gain_sb[:, s : s + 1])
+
+        def add_term(acc, src, c, start, stop):
+            for mb in range(4):
+                cols = slice(BANK * c + P * mb, BANK * c + P * (mb + 1))
+                nc.tensor.matmul(
+                    acc[:, P * mb : P * (mb + 1)],
+                    src[:, cols],
+                    ident[:],
+                    start=(start and mb == 0),
+                    stop=(stop and mb == 3),
+                    is_transpose=True,
+                )
+
+        def open_sum(s, c, tag):
+            acc = bank(tag)
+            add_term(acc, weather_sb[s], c, True, False)
+            add_term(acc, scaled[s], c, False, False)
+            return acc
+
+        def copy_on(engine, dst, src):
+            if engine == "vector":
+                nc.vector.tensor_copy(dst, src)
+            else:
+                nc.scalar.copy(dst, src)
+
+        def close_sum(s, c, acc, engine):
+            add_term(acc, page_b[s % 2], c, False, True)
+            if s % 4 == 0:
+                z_rows[c] = work.tile([P, 4, 2, P, 2], BF16, name="z_rows", tag="z_rows%d" % c, bufs=1)
+            q = s % 4
+            copy_on(
+                engine,
+                z_rows[c][:, :, :, 32 * q : 32 * (q + 1), :],
+                acc[:].rearrange("m (b p u e) -> m b u p e", b=4, u=2, e=2),
+            )
+
+        def turn_back(c, tags, engines):
+            words = z_rows[c][:].rearrange("m b u p e -> m (b u p e)").bitcast(F32)
+            z_k = work.tile([P, 4 * BANK], BF16, name="z_k", tag="z_k", bufs=4, align_bytes=64)
+            for half in range(2):
+                acc = bank(tags[half])
+                for i in range(4):
+                    src = 4 * half + i
+                    nc.tensor.transpose(acc[:, P * i : P * (i + 1)], words[:, P * src : P * (src + 1)], ident[:])
+                copy_on(
+                    engines[half],
+                    z_k[:].bitcast(F32)[:, BANK * half : BANK * (half + 1)].rearrange("p (b m u) -> p b m u", b=2, u=2),
+                    acc[:].rearrange("p (b u m) -> p b m u", b=2, u=2),
+                )
+            return z_k
+
+        def quantize_z(z_k):
+            z_c = work.tile([P, BANK], U32, name="z_c", tag="z_c", bufs=8, align_bytes=64)
+            z_s = work.tile([P, BANK], U8, name="z_s", tag="z_s", bufs=8, align_bytes=64)
+            nc.vector.quantize_mx(out=z_c[:].bitcast(FP8X4), scales=z_s[:], in_=z_k[:])
+            return z_c, z_s
+
+        def last_product(acc, b, a, z, start, stop):
+            cols = slice(N * b + P * a, N * b + P * (a + 1))
+            nc.tensor.matmul_mx(
+                out=acc[:],
+                lhsT=w3_c[:, cols].bitcast(FP8X4),
+                lhsT_scale=w3_s[:, cols],
+                rhs=z[0][:].bitcast(FP8X4),
+                rhs_scale=z[1][:],
+                start=start,
+                stop=stop,
+            )
+
+        def sum_slice(s):
+            for c in range(CHUNKS):
+                close_sum(s, c, open_sum(s, c, "z%d" % (c % 2)), "scalar")
+
+        def store(c, a, result):
+            nc.sync.dma_start(out[P * a : P * (a + 1), BANK * c : BANK * (c + 1)], result[:])
+
+        make_pollen(0)
+        scatter_a(0, 2)
+        make_pollen(1)
+        scatter_a(1, 1)
+        cast_w2(0)
+        quantize_w2(0)
+        cast_w2(1)
+        quantize_w2(1)
+        load_weather(0)
+        make_identity(nc, ident[:])
+        page_b = [shared.tile([P, T2], F32, name="page_b%d" % i, offset=AT_PAGE_B[i]) for i in range(2)]
+        nc.gpsimd.memset(page_b[0][:], 0.0)
+        nc.gpsimd.memset(page_b[1][:], 0.0)
+        make_pollen(2)
+        gelu_gain(0)
+        scatter_a(2, 1)
+        make_h2(0)
+        make_stigma(0)
+        scatter_b(0)
+        make_h2(1)
+        make_stigma(1)
+        scatter_b(1)
+        prepare_w3()
+        load_weather(1)
+        last = SLICES - 1
+        for i in range(1, last - 1):
+            gelu_gain(i)
+            make_h2(i + 1)
+            make_stigma(i + 1)
+            make_pollen(i + 2)
+            scatter_a(i + 2, 1)
+            sum_slice(i - 1)
+            load_weather(i + 1)
+            scatter_b(i + 1)
+            if i == 4:
+                turned = [turn_back(c, ("x0", "x1"), ("scalar", "scalar")) for c in range(CHUNKS)]
+                z_first = [quantize_z(z_k) for z_k in turned]
+        gelu_gain(last - 1)
+        make_h2(last)
+        make_stigma(last)
+        for c, a in partial:
+            acc = bank("h%d" % a)
+            last_product(acc, 0, a, z_first[c], True, True)
+            nc.scalar.copy(partial[c, a][:], acc[:])
+        sum_slice(last - 2)
+        load_weather(last)
+        opened = [open_sum(last - 1, c, tag) for c, tag in enumerate(("z0", "z1", "x0", "x1"))]
+        gelu_gain(last)
+        for c in range(CHUNKS):
+            close_sum(last - 1, c, opened[c], "scalar")
+        opened = [open_sum(last, c, tag) for c, tag in enumerate(("p0", "p1", "h0", "h1"))]
+        scatter_b(last)
+        out_tags = (("z0", "z1", "x0"), ("z0", "z1", "x0"), ("h0", "h1", "x1"), ("z0", "z1", "x0"))
+        turn_tags = (("x1", "p0"), ("p1", "h0"), ("h1", "x1"), ("p0", "p1"))
+        sums = {}
+
+        def open_out(c):
+            for a in range(NT):
+                sums[c, a] = bank(out_tags[c][a])
+                if (c, a) not in partial:
+                    last_product(sums[c, a], 0, a, z_first[c], True, False)
+
+        def close_out(c, z):
+            for a in range(NT):
+                last_product(sums[c, a], 1, a, z, (c, a) in partial, True)
+
+        def leave(c):
+            for a in range(NT):
+                result = work.tile([P, BANK], F32, name="result", tag="result", bufs=4)
+                if (c, a) in partial:
+                    nc.vector.tensor_tensor(result[:], sums[c, a][:], partial[c, a][:], ADD)
+                else:
+                    copy_on("vector" if (c, a) == (0, 0) else "scalar", result[:], sums[c, a][:])
+                store(c, a, result)
+
+        open_out(0)
+        for c in range(CHUNKS):
+            close_sum(last, c, opened[c], ("scalar", "vector")[c % 2])
+        z_k = {0: turn_back(0, turn_tags[0], ("scalar", "vector"))}
+        z_k[1] = turn_back(1, turn_tags[1], ("scalar", "scalar"))
+        for c in range(CHUNKS):
+            z = quantize_z(z_k[c])
+            if c + 2 < CHUNKS:
+                z_k[c + 2] = turn_back(c + 2, turn_tags[c + 2], ("scalar", "scalar"))
+            if c > 0:
+                leave(c - 1)
+                open_out(c)
+            close_out(c, z)
+        leave(CHUNKS - 1)

@@ -122,7 +122,8 @@ def tile_list_cherry_pollination_scores_kernel(
                 )
 
         pollen = {}
-        stigma = {}
+        to_a = {}
+        to_b = {}
         h2 = {}
         scaled = {}
         weather_sb = {}
@@ -130,8 +131,9 @@ def tile_list_cherry_pollination_scores_kernel(
 
         def make_pollen(s):
             pollen[s] = work.tile([P, S], F32, name="pollen", tag="pollen", bufs=3)
+            to_a[s] = work.tile([P, S], F32, name="to_a", tag="to_a", bufs=2)
             for h in range(2):
-                acc = bank("p%d" % h)
+                acc = bank("s%d" % h)
                 nc.tensor.matmul_mx(
                     out=acc[:],
                     lhsT=w1_w[:, 2 * P * s : 2 * P * (s + 1)].bitcast(FP4X4),
@@ -141,12 +143,16 @@ def tile_list_cherry_pollination_scores_kernel(
                     start=True,
                     stop=True,
                 )
+                if (s, h) == (0, 0):
+                    nc.vector.tensor_tensor(to_a[0][:, 0:BANK], acc[:], wg1_sb[:, 0:BANK], MULT)
                 nc.scalar.copy(pollen[s][:, BANK * h : BANK * (h + 1)], acc[:])
+            cols = slice(BANK if s == 0 else 0, S)
+            nc.gpsimd.tensor_tensor(to_a[s][:, cols], pollen[s][:, cols], wg1_sb[:, cols], MULT)
 
         def make_h2(s):
             h2[s] = work.tile([P, S], F32, name="h2", tag="h2", bufs=2)
             for h in range(2):
-                acc = bank("h%d" % h)
+                acc = bank("s%d" % h)
                 nc.tensor.matmul_mx(
                     out=acc[:],
                     lhsT=w2_c[:, P * s : P * (s + 1)].bitcast(FP8X4),
@@ -159,21 +165,21 @@ def tile_list_cherry_pollination_scores_kernel(
                 nc.scalar.activation(h2[s][:, BANK * h : BANK * (h + 1)], acc[:], COPY, scale=-1.0)
 
         def make_stigma(s):
-            stigma[s] = work.tile([P, S], F32, name="stigma", tag="stigma", bufs=2)
-            nc.vector.tensor_tensor(stigma[s][:], h2[s][:], pollen[s][:], MULT)
+            stigma = work.tile([P, S], F32, name="stigma", tag="stigma", bufs=1)
+            to_b[s] = work.tile([P, S], F32, name="to_b", tag="to_b", bufs=2)
+            nc.gpsimd.tensor_tensor(stigma[:], h2[s][:], pollen[s][:], MULT)
+            nc.gpsimd.tensor_tensor(to_b[s][:], stigma[:], wg2_sb, MULT)
 
         def scatter_a(s, parts):
             n = S // parts
             for i in range(parts):
-                nc.vector.tensor_tensor(
+                nc.vector.tensor_copy(
                     page_a[s % 2][:].indirect(list2[:, i * n // 16 : (i + 1) * n // 16]),
-                    pollen[s][:, i * n : (i + 1) * n],
-                    wg1_sb[:, i * n : (i + 1) * n],
-                    MULT,
+                    to_a[s][:, i * n : (i + 1) * n],
                 )
 
         def scatter_b(s):
-            nc.vector.tensor_tensor(page_b[s % 2][:].indirect(list3[:]), stigma[s][:], wg2_sb, MULT)
+            nc.vector.tensor_copy(page_b[s % 2][:].indirect(list3[:]), to_b[s][:])
 
         def load_weather(s):
             weather_sb[s] = keep.tile([P, T2], F32, name="weather_sb", tag="weather%d" % (s % 2), align_bytes=64)
@@ -223,9 +229,11 @@ def tile_list_cherry_pollination_scores_kernel(
                 acc[:].rearrange("m (b p u e) -> m b u p e", b=4, u=2, e=2),
             )
 
-        def turn_back(c, tags, engines):
+        def new_z_k(chunks):
+            return work.tile([P, chunks * 4 * BANK], BF16, name="z_k", tag="z_k", bufs=2, align_bytes=64)
+
+        def turn_back(c, z_k, tags, engines):
             words = z_rows[c][:].rearrange("m b u p e -> m (b u p e)").bitcast(F32)
-            z_k = work.tile([P, 4 * BANK], BF16, name="z_k", tag="z_k", bufs=4, align_bytes=64)
             for half in range(2):
                 acc = bank(tags[half])
                 for i in range(4):
@@ -233,16 +241,15 @@ def tile_list_cherry_pollination_scores_kernel(
                     nc.tensor.transpose(acc[:, P * i : P * (i + 1)], words[:, P * src : P * (src + 1)], ident[:])
                 copy_on(
                     engines[half],
-                    z_k[:].bitcast(F32)[:, BANK * half : BANK * (half + 1)].rearrange("p (b m u) -> p b m u", b=2, u=2),
+                    z_k.bitcast(F32)[:, BANK * half : BANK * (half + 1)].rearrange("p (b m u) -> p b m u", b=2, u=2),
                     acc[:].rearrange("p (b u m) -> p b m u", b=2, u=2),
                 )
-            return z_k
 
-        def quantize_z(z_k):
-            z_c = work.tile([P, BANK], U32, name="z_c", tag="z_c", bufs=8, align_bytes=64)
-            z_s = work.tile([P, BANK], U8, name="z_s", tag="z_s", bufs=8, align_bytes=64)
+        def quantize_z(z_k, chunks):
+            z_c = work.tile([P, chunks * BANK], U32, name="z_c", tag="z_c%d" % chunks, bufs=4 // chunks, align_bytes=64)
+            z_s = work.tile([P, chunks * BANK], U8, name="z_s", tag="z_s%d" % chunks, bufs=4 // chunks, align_bytes=64)
             nc.vector.quantize_mx(out=z_c[:].bitcast(FP8X4), scales=z_s[:], in_=z_k[:])
-            return z_c, z_s
+            return [(z_c[:, BANK * i : BANK * (i + 1)], z_s[:, BANK * i : BANK * (i + 1)]) for i in range(chunks)]
 
         def last_product(acc, b, a, z, start, stop):
             cols = slice(N * b + P * a, N * b + P * (a + 1))
@@ -250,15 +257,16 @@ def tile_list_cherry_pollination_scores_kernel(
                 out=acc[:],
                 lhsT=w3_c[:, cols].bitcast(FP8X4),
                 lhsT_scale=w3_s[:, cols],
-                rhs=z[0][:].bitcast(FP8X4),
-                rhs_scale=z[1][:],
+                rhs=z[0].bitcast(FP8X4),
+                rhs_scale=z[1],
                 start=start,
                 stop=stop,
             )
 
         def sum_slice(s):
+            opened = [open_sum(s, c, "z%d" % c) for c in range(CHUNKS)]
             for c in range(CHUNKS):
-                close_sum(s, c, open_sum(s, c, "z%d" % (c % 2)), "scalar")
+                close_sum(s, c, opened[c], "scalar")
 
         def store(c, a, result):
             nc.sync.dma_start(out[P * a : P * (a + 1), BANK * c : BANK * (c + 1)], result[:])
@@ -290,33 +298,42 @@ def tile_list_cherry_pollination_scores_kernel(
         last = SLICES - 1
         for i in range(1, last - 1):
             gelu_gain(i)
-            make_h2(i + 1)
-            make_stigma(i + 1)
             make_pollen(i + 2)
             scatter_a(i + 2, 1)
+            make_h2(i + 1)
+            make_stigma(i + 1)
             sum_slice(i - 1)
             load_weather(i + 1)
             scatter_b(i + 1)
             if i == 4:
-                turned = [turn_back(c, ("x0", "x1"), ("scalar", "scalar")) for c in range(CHUNKS)]
-                z_first = [quantize_z(z_k) for z_k in turned]
+                z_first = []
+                for pair in range(2):
+                    z_k = new_z_k(2)
+                    for j in range(2):
+                        part = z_k[:, 4 * BANK * j : 4 * BANK * (j + 1)]
+                        turn_back(2 * pair + j, part, ("x0", "x1"), ("scalar", "scalar"))
+                    z_first.extend(quantize_z(z_k, 2))
         gelu_gain(last - 1)
         make_h2(last)
         make_stigma(last)
-        for c, a in partial:
-            acc = bank("h%d" % a)
+
+        def make_partial(c, a, tag):
+            acc = bank(tag)
             last_product(acc, 0, a, z_first[c], True, True)
             nc.scalar.copy(partial[c, a][:], acc[:])
+
+        for c in range(1, CHUNKS):
+            make_partial(c, 0, "s%d" % (c % 2))
         sum_slice(last - 2)
         load_weather(last)
-        opened = [open_sum(last - 1, c, tag) for c, tag in enumerate(("z0", "z1", "x0", "x1"))]
         gelu_gain(last)
-        for c in range(CHUNKS):
-            close_sum(last - 1, c, opened[c], "scalar")
-        opened = [open_sum(last, c, tag) for c, tag in enumerate(("p0", "p1", "h0", "h1"))]
+        opened = [open_sum(last, c, tag) for c, tag in enumerate(("s0", "s1", "x0", "x1"))]
+        sum_slice(last - 1)
+        for c in range(1, CHUNKS):
+            make_partial(c, 1, "z%d" % (c - 1))
         scatter_b(last)
-        out_tags = (("z0", "z1", "x0"), ("z0", "z1", "x0"), ("h0", "h1", "x1"), ("z0", "z1", "x0"))
-        turn_tags = (("x1", "p0"), ("p1", "h0"), ("h1", "x1"), ("p0", "p1"))
+        out_tags = (("z3", "z0", "z1"), ("z3", "z0", "z1"), ("x0", "x1", "z2"), ("z3", "z0", "z1"))
+        turn_tags = (("z2", "s0"), ("s1", "x0"), ("x1", "z2"), ("s0", "s1"))
         sums = {}
 
         def open_out(c):
@@ -340,13 +357,16 @@ def tile_list_cherry_pollination_scores_kernel(
 
         open_out(0)
         for c in range(CHUNKS):
-            close_sum(last, c, opened[c], ("scalar", "vector")[c % 2])
-        z_k = {0: turn_back(0, turn_tags[0], ("scalar", "vector"))}
-        z_k[1] = turn_back(1, turn_tags[1], ("scalar", "scalar"))
+            close_sum(last, c, opened[c], ("vector", "scalar")[c % 2])
+        z_k = {}
+        for c in range(2):
+            z_k[c] = new_z_k(1)
+            turn_back(c, z_k[c][:], turn_tags[c], ("scalar", ("vector", "scalar")[c]))
         for c in range(CHUNKS):
-            z = quantize_z(z_k[c])
+            z = quantize_z(z_k[c], 1)[0]
             if c + 2 < CHUNKS:
-                z_k[c + 2] = turn_back(c + 2, turn_tags[c + 2], ("scalar", "scalar"))
+                z_k[c + 2] = new_z_k(1)
+                turn_back(c + 2, z_k[c + 2][:], turn_tags[c + 2], ("scalar", "scalar"))
             if c > 0:
                 leave(c - 1)
                 open_out(c)

@@ -15,7 +15,6 @@ U8 = mybir.dt.uint8
 FP8X4 = mybir.dt.float8_e4m3fn_x4
 FP4X4 = mybir.dt.float4_e2m1fn_x4
 MULT = mybir.AluOpType.mult
-ADD = mybir.AluOpType.add
 GELU = mybir.ActivationFunctionType.Gelu_apprx_tanh
 COPY = mybir.ActivationFunctionType.Copy
 
@@ -26,8 +25,13 @@ CHUNKS = T2 // BANK
 NT = N // P
 AT_TAB_S = 2112
 AT_ROWS = (4160, 20544)
-AT_PAGE_B = (12352, 28736)
+AT_PAGE_A1 = 12352
+AT_PAGE_B0 = 28736
 AT_TAB_W = 16448
+AT_WEATHER = (36928, 45120)
+AT_W2_BF = 41024
+AT_TO_B = (53312, 57408)
+AT_LAST_WEATHER = 45184
 
 
 def tile_list_cherry_pollination_scores_kernel(
@@ -52,16 +56,13 @@ def tile_list_cherry_pollination_scores_kernel(
         w1_s = keep.tile([P, H], U8, name="w1_s", align_bytes=64)
         wg1_sb = keep.tile([P, S], F32, name="wg1_sb")
         ident = keep.tile([P, P], F32, name="ident")
-        page_a = [keep.tile([P, T2], F32, name="page_a%d" % i) for i in range(2)]
+        page_a = [keep.tile([P, T2], F32, name="page_a0")]
         v_w = [keep.tile([P, BANK], U32, name="v_w%d" % i, align_bytes=64) for i in range(2)]
         v_s = keep.tile([P, S], U8, name="v_s", align_bytes=64)
         w2_c = keep.tile([P, H], U32, name="w2_c", align_bytes=64)
         w2_s = keep.tile([P, H], U8, name="w2_s", align_bytes=64)
         w3_c = keep.tile([P, 2 * N], U32, name="w3_c", align_bytes=64)
         w3_s = keep.tile([P, 2 * N], U8, name="w3_s", align_bytes=64)
-        partial = {
-            (c, a): keep.tile([P, BANK], F32, name="partial%d%d" % (c, a)) for c in range(1, CHUNKS) for a in range(2)
-        }
 
         nc.vector.memset(tab_s[:].bitcast(I32), 0)
         nc.gpsimd.memset(w1_s[:].bitcast(I32), 0)
@@ -79,8 +80,10 @@ def tile_list_cherry_pollination_scores_kernel(
             )
         nc.sync.dma_start(w1_w[:].bitcast(I32), w1_words[0].bitcast(I32))
         nc.sync.dma_start(wg1_sb[:], wg1)
-        nc.vector.memset(page_a[0][:], 0.0)
-        nc.vector.memset(page_a[1][:], 0.0)
+        nc.vector.memset(page_a[0][:, 0 : T2 // 2 - 1], 0.0)
+        nc.vector.memset(page_a[0][:, T2 // 2 - 1 : T2], 0.0)
+        page_b1 = keep.tile([P, T2], F32, name="page_b1")
+        nc.vector.memset(page_b1[:], 0.0)
 
         def interleave(dst, raw):
             nc.scalar.copy(
@@ -101,19 +104,18 @@ def tile_list_cherry_pollination_scores_kernel(
         with nc.allow_non_contiguous_dma(reason="one gain for each partition and slice"):
             nc.sync.dma_start(gain_sb, gain.rearrange("(s p) -> p s", p=P))
         nc.sync.dma_start(wg2_sb, wg2)
-        w2_bf = [keep.tile([P, 4 * BANK], BF16, name="w2_bf", tag="weather%d" % h, align_bytes=64) for h in range(2)]
+        w2_bf = shared.tile([P, 4 * H], BF16, name="w2_bf", offset=AT_W2_BF, align_bytes=64)
 
         def cast_w2(h):
-            interleave(w2_bf[h][:], w2_raw[h][:])
+            interleave(w2_bf[:, 4 * BANK * h : 4 * BANK * (h + 1)], w2_raw[h][:])
 
-        def quantize_w2(h):
-            cols = slice(h * BANK, (h + 1) * BANK)
-            nc.vector.quantize_mx(out=w2_c[:, cols].bitcast(FP8X4), scales=w2_s[:, cols], in_=w2_bf[h][:])
+        def quantize_w2():
+            nc.vector.quantize_mx(out=w2_c[:].bitcast(FP8X4), scales=w2_s[:], in_=w2_bf[:])
 
         def prepare_w3():
             w3_bf = keep.tile([P, 2 * N * 4], BF16, name="w3_bf", align_bytes=64)
             for b in range(2):
-                w3_raw = keep.tile([P, 4, N], F32, name="w3_raw", tag="weather1", align_bytes=64)
+                w3_raw = shared.tile([P, 4, N], F32, name="w3_raw", offset=AT_WEATHER[1])
                 nc.sync.dma_start(w3_raw[:], w3[b * K : (b + 1) * K, :].rearrange("(p j) w -> p j w", j=4))
                 interleave(w3_bf[:, b * 4 * N : (b + 1) * 4 * N], w3_raw[:])
             for lo, hi in ((0, 512), (512, 768)):
@@ -146,8 +148,9 @@ def tile_list_cherry_pollination_scores_kernel(
                 if (s, h) == (0, 0):
                     nc.vector.tensor_tensor(to_a[0][:, 0:BANK], acc[:], wg1_sb[:, 0:BANK], MULT)
                 nc.scalar.copy(pollen[s][:, BANK * h : BANK * (h + 1)], acc[:])
-            cols = slice(BANK if s == 0 else 0, S)
-            nc.gpsimd.tensor_tensor(to_a[s][:, cols], pollen[s][:, cols], wg1_sb[:, cols], MULT)
+                if (s, h) != (0, 0):
+                    cols = slice(BANK * h, BANK * (h + 1))
+                    nc.gpsimd.tensor_tensor(to_a[s][:, cols], pollen[s][:, cols], wg1_sb[:, cols], MULT)
 
         def make_h2(s):
             h2[s] = work.tile([P, S], F32, name="h2", tag="h2", bufs=2)
@@ -165,10 +168,16 @@ def tile_list_cherry_pollination_scores_kernel(
                 nc.scalar.activation(h2[s][:, BANK * h : BANK * (h + 1)], acc[:], COPY, scale=-1.0)
 
         def make_stigma(s):
-            stigma = work.tile([P, S], F32, name="stigma", tag="stigma", bufs=1)
-            to_b[s] = work.tile([P, S], F32, name="to_b", tag="to_b", bufs=2)
-            nc.gpsimd.tensor_tensor(stigma[:], h2[s][:], pollen[s][:], MULT)
-            nc.gpsimd.tensor_tensor(to_b[s][:], stigma[:], wg2_sb, MULT)
+            if s < 2:
+                stigma = work.tile([P, S], F32, name="stigma", tag="stigma", bufs=1)
+            else:
+                stigma = shared.tile([P, S], F32, name="stigma%d" % (s % 2), offset=AT_WEATHER[s % 2])
+            to_b[s] = shared.tile([P, S], F32, name="to_b%d" % (s % 2), offset=AT_TO_B[s % 2])
+            halves = [slice(BANK * h, BANK * (h + 1)) for h in range(2)]
+            for cols in halves:
+                nc.gpsimd.tensor_tensor(stigma[:, cols], h2[s][:, cols], pollen[s][:, cols], MULT)
+            for cols in halves:
+                nc.gpsimd.tensor_tensor(to_b[s][:, cols], stigma[:, cols], wg2_gain[:, cols], MULT)
 
         def scatter_a(s, parts):
             n = S // parts
@@ -182,8 +191,14 @@ def tile_list_cherry_pollination_scores_kernel(
             nc.vector.tensor_copy(page_b[s % 2][:].indirect(list3[:]), to_b[s][:])
 
         def load_weather(s):
-            weather_sb[s] = keep.tile([P, T2], F32, name="weather_sb", tag="weather%d" % (s % 2), align_bytes=64)
+            weather_sb[s] = shared.tile([P, T2], F32, name="weather%d" % (s % 2), offset=AT_WEATHER[s % 2])
             nc.sync.dma_start(weather_sb[s][:], weather[P * s : P * (s + 1), :])
+
+        def load_last_weather(s):
+            weather_sb[s] = shared.tile([P, T2], F32, name="last_weather", offset=AT_LAST_WEATHER)
+            for c in range(CHUNKS):
+                cols = slice(BANK * c, BANK * (c + 1))
+                nc.sync.dma_start(weather_sb[s][:, cols], weather[P * s : P * (s + 1), cols])
 
         def gelu_gain(s):
             scaled[s] = shared.tile([P, T2], F32, name="scaled%d" % (s % 2), offset=AT_ROWS[s % 2])
@@ -208,8 +223,9 @@ def tile_list_cherry_pollination_scores_kernel(
 
         def open_sum(s, c, tag):
             acc = bank(tag)
-            add_term(acc, weather_sb[s], c, True, False)
-            add_term(acc, scaled[s], c, False, False)
+            add_term(acc, scaled[s], c, True, False)
+            if s < SLICES - 1:
+                add_term(acc, weather_sb[s], c, False, False)
             return acc
 
         def copy_on(engine, dst, src):
@@ -273,17 +289,17 @@ def tile_list_cherry_pollination_scores_kernel(
 
         make_pollen(0)
         scatter_a(0, 2)
+        page_a.append(shared.tile([P, T2], F32, name="page_a1", offset=AT_PAGE_A1))
+        nc.gpsimd.memset(page_a[1][:], 0.0)
         make_pollen(1)
         scatter_a(1, 1)
         cast_w2(0)
-        quantize_w2(0)
         cast_w2(1)
-        quantize_w2(1)
+        quantize_w2()
         load_weather(0)
         make_identity(nc, ident[:])
-        page_b = [shared.tile([P, T2], F32, name="page_b%d" % i, offset=AT_PAGE_B[i]) for i in range(2)]
+        page_b = [shared.tile([P, T2], F32, name="page_b0", offset=AT_PAGE_B0), page_b1]
         nc.gpsimd.memset(page_b[0][:], 0.0)
-        nc.gpsimd.memset(page_b[1][:], 0.0)
         make_pollen(2)
         gelu_gain(0)
         scatter_a(2, 1)
@@ -301,8 +317,8 @@ def tile_list_cherry_pollination_scores_kernel(
             make_pollen(i + 2)
             scatter_a(i + 2, 1)
             make_h2(i + 1)
-            make_stigma(i + 1)
             sum_slice(i - 1)
+            make_stigma(i + 1)
             load_weather(i + 1)
             scatter_b(i + 1)
             if i == 4:
@@ -315,47 +331,33 @@ def tile_list_cherry_pollination_scores_kernel(
                     z_first.extend(quantize_z(z_k, 2))
         gelu_gain(last - 1)
         make_h2(last)
-        make_stigma(last)
-
-        def make_partial(c, a, tag):
-            acc = bank(tag)
-            last_product(acc, 0, a, z_first[c], True, True)
-            nc.scalar.copy(partial[c, a][:], acc[:])
-
-        for c in range(1, CHUNKS):
-            make_partial(c, 0, "s%d" % (c % 2))
         sum_slice(last - 2)
-        load_weather(last)
+        make_stigma(last)
         gelu_gain(last)
         opened = [open_sum(last, c, tag) for c, tag in enumerate(("s0", "s1", "x0", "x1"))]
         sum_slice(last - 1)
-        for c in range(1, CHUNKS):
-            make_partial(c, 1, "z%d" % (c - 1))
+        load_last_weather(last)
         scatter_b(last)
-        out_tags = (("z3", "z0", "z1"), ("z3", "z0", "z1"), ("x0", "x1", "z2"), ("z3", "z0", "z1"))
-        turn_tags = (("z2", "s0"), ("s1", "x0"), ("x1", "z2"), ("s0", "s1"))
+        out_tags = (("z0", "z1", "z2"), ("z3", "z0", "z1"), ("z2", "s0", "s1"), ("z3", "x0", "x1"))
+        turn_tags = (("s0", "s1"), ("x0", "x1"))
         sums = {}
 
-        def open_out(c):
-            for a in range(NT):
-                sums[c, a] = bank(out_tags[c][a])
-                if (c, a) not in partial:
-                    last_product(sums[c, a], 0, a, z_first[c], True, False)
-
-        def close_out(c, z):
-            for a in range(NT):
-                last_product(sums[c, a], 1, a, z, (c, a) in partial, True)
+        def open_out(c, a):
+            sums[c, a] = bank(out_tags[c][a])
+            last_product(sums[c, a], 0, a, z_first[c], True, False)
 
         def leave(c):
             for a in range(NT):
-                result = work.tile([P, BANK], F32, name="result", tag="result", bufs=4)
-                if (c, a) in partial:
-                    nc.vector.tensor_tensor(result[:], sums[c, a][:], partial[c, a][:], ADD)
-                else:
-                    copy_on("vector" if (c, a) == (0, 0) else "scalar", result[:], sums[c, a][:])
+                result = work.tile([P, BANK], F32, name="result", tag="result", bufs=6)
+                on_vector = (a == 1) if c == CHUNKS - 1 else (a != 1)
+                copy_on("vector" if on_vector else "scalar", result[:], sums[c, a][:])
                 store(c, a, result)
 
-        open_out(0)
+        for a in range(NT):
+            open_out(0, a)
+        for c in range(CHUNKS):
+            add_term(opened[c], weather_sb[last], c, False, False)
+        open_out(1, 0)
         for c in range(CHUNKS):
             close_sum(last, c, opened[c], ("vector", "scalar")[c % 2])
         z_k = {}
@@ -366,9 +368,12 @@ def tile_list_cherry_pollination_scores_kernel(
             z = quantize_z(z_k[c], 1)[0]
             if c + 2 < CHUNKS:
                 z_k[c + 2] = new_z_k(1)
-                turn_back(c + 2, z_k[c + 2][:], turn_tags[c + 2], ("scalar", "scalar"))
+                turn_back(c + 2, z_k[c + 2][:], turn_tags[c % 2], ("scalar", "scalar"))
             if c > 0:
                 leave(c - 1)
-                open_out(c)
-            close_out(c, z)
+            for a in range(NT):
+                if (c, a) not in sums:
+                    open_out(c, a)
+            for a in range(NT):
+                last_product(sums[c, a], 1, a, z, False, True)
         leave(CHUNKS - 1)

@@ -15,6 +15,7 @@ U8 = mybir.dt.uint8
 FP8X4 = mybir.dt.float8_e4m3fn_x4
 FP4X4 = mybir.dt.float4_e2m1fn_x4
 MULT = mybir.AluOpType.mult
+ADD = mybir.AluOpType.add
 GELU = mybir.ActivationFunctionType.Gelu_apprx_tanh
 COPY = mybir.ActivationFunctionType.Copy
 
@@ -23,15 +24,28 @@ BANK = 512
 SLICES = H // P
 CHUNKS = T2 // BANK
 NT = N // P
-AT_TAB_S = 2112
-AT_ROWS = (4160, 20544)
-AT_PAGE_A1 = 12352
-AT_PAGE_B0 = 28736
-AT_TAB_W = 16448
-AT_WEATHER = (36928, 45120)
-AT_W2_BF = 41024
-AT_TO_B = (53312, 57408)
-AT_LAST_WEATHER = 45184
+DEALT = {4: 2, 5: 0, 6: 1, 7: 3}
+AT_PAGE_B0 = 0
+AT_TAB_S = 6144
+AT_ROWS = (28736, 36928)
+AT_W2_RAW = (8192, 32832)
+AT_PAGE_A1 = 16384
+AT_TAB_W = 24544
+AT_WG2 = 24576
+AT_Z_K = (45120, 58944)
+AT_W2_BF = 53248
+AT_W1_DEALT = 57408
+AT_LAST_WEATHER = 67136
+AT_WEATHER = (71232, 8192)
+AT_PAIRS = 79424
+AT_WG1 = 95808
+AT_W3_CODES = (53312, AT_WG1)
+AT_Z_CODES = (99904, 104000)
+AT_FIRST_STIGMA = (AT_Z_CODES[0], AT_Z_CODES[1], AT_LAST_WEATHER)
+AT_DEALT_WG = {
+    ("a", 4): AT_W3_CODES[0], ("a", 5): AT_W3_CODES[1], ("a", 6): AT_Z_CODES[0], ("a", 7): AT_Z_CODES[1],
+    ("b", 4): AT_WG2, ("b", 5): AT_LAST_WEATHER, ("b", 6): AT_WG2, ("b", 7): AT_LAST_WEATHER,
+}
 
 
 def tile_list_cherry_pollination_scores_kernel(
@@ -47,6 +61,9 @@ def tile_list_cherry_pollination_scores_kernel(
         def bank(tag):
             return psum.tile([P, BANK], F32, name=tag, tag=tag)
 
+        def chunk(c):
+            return slice(BANK * c, BANK * (c + 1))
+
         list1 = keep.tile([P, S // 16], U16, name="list1")
         list2 = keep.tile([P, S // 16], U16, name="list2")
         list3 = keep.tile([P, S // 16], U16, name="list3")
@@ -54,15 +71,13 @@ def tile_list_cherry_pollination_scores_kernel(
         tab_s = shared.tile([P, T], U8, name="tab_s", offset=AT_TAB_S)
         w1_w = keep.tile([P, 2 * H], U8, name="w1_w", align_bytes=64)
         w1_s = keep.tile([P, H], U8, name="w1_s", align_bytes=64)
-        wg1_sb = keep.tile([P, S], F32, name="wg1_sb")
+        wg1_sb = shared.tile([P, S], F32, name="wg1_sb", offset=AT_WG1)
         ident = keep.tile([P, P], F32, name="ident")
         page_a = [keep.tile([P, T2], F32, name="page_a0")]
         v_w = [keep.tile([P, BANK], U32, name="v_w%d" % i, align_bytes=64) for i in range(2)]
         v_s = keep.tile([P, S], U8, name="v_s", align_bytes=64)
         w2_c = keep.tile([P, H], U32, name="w2_c", align_bytes=64)
         w2_s = keep.tile([P, H], U8, name="w2_s", align_bytes=64)
-        w3_c = keep.tile([P, 2 * N], U32, name="w3_c", align_bytes=64)
-        w3_s = keep.tile([P, 2 * N], U8, name="w3_s", align_bytes=64)
 
         nc.vector.memset(tab_s[:].bitcast(I32), 0)
         nc.gpsimd.memset(w1_s[:].bitcast(I32), 0)
@@ -85,148 +100,324 @@ def tile_list_cherry_pollination_scores_kernel(
         page_b1 = keep.tile([P, T2], F32, name="page_b1")
         nc.vector.memset(page_b1[:], 0.0)
 
+        nc.vector.tensor_copy(v_s[:], tab_s[:].indirect(list1[:]))
+        for h in range(2):
+            nc.vector.tensor_copy(v_w[h][:], tab_w[:].bitcast(U32).indirect(list1[:, 32 * h : 32 * (h + 1)]))
+
+        page_b = [shared.tile([P, T2], F32, name="page_b0", offset=AT_PAGE_B0), page_b1]
+        nc.gpsimd.memset(page_b[0][:], 0.0)
+        w2_raw = [shared.tile([P, 4, BANK], F32, name="w2_raw%d" % h, offset=AT_W2_RAW[h]) for h in range(2)]
+        for h in range(2):
+            nc.sync.dma_start(w2_raw[h][:], w2[:, chunk(h)].rearrange("(p j) w -> p j w", j=4))
+        wg2_sb = shared.tile([P, S], F32, name="wg2_sb", offset=AT_WG2)
+        gain_sb = shared.tile([P, 16], F32, name="gain_sb", offset=AT_WG2 + 4 * S)
+        with nc.allow_non_contiguous_dma(reason="one gain for each partition and slice"):
+            nc.sync.dma_start(gain_sb[:, 0:4], gain[0:K].rearrange("(s p) -> p s", p=P))
+            nc.sync.dma_start(gain_sb[:, 8:12], gain[K:H].rearrange("(p t) -> p t", t=4))
+        nc.sync.dma_start(wg2_sb[:], wg2)
+
         def interleave(dst, raw):
             nc.scalar.copy(
                 dst.rearrange("p (c i t) -> p c t i", i=4, t=4),
                 raw.rearrange("p t (c i) -> p c t i", i=4),
             )
 
-        nc.vector.tensor_copy(v_s[:], tab_s[:].indirect(list1[:]))
-        for h in range(2):
-            nc.vector.tensor_copy(v_w[h][:], tab_w[:].bitcast(U32).indirect(list1[:, 32 * h : 32 * (h + 1)]))
-
-        w2_raw = [shared.tile([P, 4, BANK], F32, name="w2_raw%d" % h, offset=AT_ROWS[h]) for h in range(2)]
-        for h in range(2):
-            nc.sync.dma_start(w2_raw[h][:], w2[:, h * BANK : (h + 1) * BANK].rearrange("(p j) w -> p j w", j=4))
-        wg2_gain = shared.tile([P, S + SLICES], F32, name="wg2_gain", offset=0)
-        wg2_sb = wg2_gain[:, 0:S]
-        gain_sb = wg2_gain[:, S : S + SLICES]
-        with nc.allow_non_contiguous_dma(reason="one gain for each partition and slice"):
-            nc.sync.dma_start(gain_sb, gain.rearrange("(s p) -> p s", p=P))
-        nc.sync.dma_start(wg2_sb, wg2)
-        w2_bf = shared.tile([P, 4 * H], BF16, name="w2_bf", offset=AT_W2_BF, align_bytes=64)
-
-        def cast_w2(h):
-            interleave(w2_bf[:, 4 * BANK * h : 4 * BANK * (h + 1)], w2_raw[h][:])
-
-        def quantize_w2():
+        def prepare_w2():
+            w2_bf = shared.tile([P, 4 * H], BF16, name="w2_bf", offset=AT_W2_BF, align_bytes=64)
+            interleave(w2_bf[:, 0 : 4 * BANK], w2_raw[0][:])
+            nc.scalar.copy(
+                w2_bf[:, 4 * BANK : 8 * BANK].rearrange("p (t q j) -> p q j t", t=4, j=4),
+                w2_raw[1][:].rearrange("p j (q t) -> p q j t", t=4),
+            )
             nc.vector.quantize_mx(out=w2_c[:].bitcast(FP8X4), scales=w2_s[:], in_=w2_bf[:])
 
-        def prepare_w3():
-            w3_bf = keep.tile([P, 2 * N * 4], BF16, name="w3_bf", align_bytes=64)
+        w3_bf = []
+        w3_blocks = []
+
+        def cast_w3():
+            rounded = shared.tile([P, 2 * N * 4], BF16, name="w3_bf", offset=AT_PAIRS, align_bytes=64)
             for b in range(2):
-                w3_raw = shared.tile([P, 4, N], F32, name="w3_raw", offset=AT_WEATHER[1])
+                w3_raw = shared.tile([P, 4, N], F32, name="w3_raw%d" % b, offset=AT_Z_K[b])
                 nc.sync.dma_start(w3_raw[:], w3[b * K : (b + 1) * K, :].rearrange("(p j) w -> p j w", j=4))
-                interleave(w3_bf[:, b * 4 * N : (b + 1) * 4 * N], w3_raw[:])
-            for lo, hi in ((0, 512), (512, 768)):
-                nc.vector.quantize_mx(
-                    out=w3_c[:, lo:hi].bitcast(FP8X4), scales=w3_s[:, lo:hi], in_=w3_bf[:, 4 * lo : 4 * hi]
-                )
+                interleave(rounded[:, b * 4 * N : (b + 1) * 4 * N], w3_raw[:])
+            w3_bf.append(rounded)
 
-        pollen = {}
-        to_a = {}
-        to_b = {}
-        h2 = {}
-        scaled = {}
-        weather_sb = {}
-        z_rows = {}
+        def quantize_w3(i):
+            lo, hi = ((0, 512), (512, 768))[i]
+            codes = shared.tile([P, hi - lo], U32, name="w3_c%d" % i, offset=AT_W3_CODES[i], align_bytes=64)
+            scales = shared.tile([P, hi - lo], U8, name="w3_s%d" % i, offset=AT_W3_CODES[i] + 2048, align_bytes=64)
+            nc.vector.quantize_mx(out=codes[:].bitcast(FP8X4), scales=scales[:], in_=w3_bf[0][:, 4 * lo : 4 * hi])
+            for j in range((hi - lo) // P):
+                w3_blocks.append((codes[:, P * j : P * (j + 1)], scales[:, P * j : P * (j + 1)]))
 
-        def make_pollen(s):
-            pollen[s] = work.tile([P, S], F32, name="pollen", tag="pollen", bufs=3)
-            to_a[s] = work.tile([P, S], F32, name="to_a", tag="to_a", bufs=2)
-            for h in range(2):
-                acc = bank("s%d" % h)
-                nc.tensor.matmul_mx(
-                    out=acc[:],
-                    lhsT=w1_w[:, 2 * P * s : 2 * P * (s + 1)].bitcast(FP4X4),
-                    lhsT_scale=w1_s[:, P * s : P * (s + 1)],
-                    rhs=v_w[h][:].bitcast(FP8X4),
-                    rhs_scale=v_s[:, BANK * h : BANK * (h + 1)],
-                    start=True,
-                    stop=True,
-                )
-                if (s, h) == (0, 0):
-                    nc.vector.tensor_tensor(to_a[0][:, 0:BANK], acc[:], wg1_sb[:, 0:BANK], MULT)
-                nc.scalar.copy(pollen[s][:, BANK * h : BANK * (h + 1)], acc[:])
-                if (s, h) != (0, 0):
-                    cols = slice(BANK * h, BANK * (h + 1))
-                    nc.gpsimd.tensor_tensor(to_a[s][:, cols], pollen[s][:, cols], wg1_sb[:, cols], MULT)
+        w1_dealt = []
 
-        def make_h2(s):
-            h2[s] = work.tile([P, S], F32, name="h2", tag="h2", bufs=2)
-            for h in range(2):
-                acc = bank("s%d" % h)
-                nc.tensor.matmul_mx(
-                    out=acc[:],
-                    lhsT=w2_c[:, P * s : P * (s + 1)].bitcast(FP8X4),
-                    lhsT_scale=w2_s[:, P * s : P * (s + 1)],
-                    rhs=v_w[h][:].bitcast(FP8X4),
-                    rhs_scale=v_s[:, BANK * h : BANK * (h + 1)],
-                    start=True,
-                    stop=True,
-                )
-                nc.scalar.activation(h2[s][:, BANK * h : BANK * (h + 1)], acc[:], COPY, scale=-1.0)
+        def deal_w1():
+            words = shared.tile([P, 4, P, 2], U8, name="w1_dealt_w", offset=AT_W1_DEALT, align_bytes=64)
+            scales = shared.tile([P, 4, P], U8, name="w1_dealt_s", offset=AT_W1_DEALT + H, align_bytes=64)
+            src_w = w1_w[:, H : 2 * H].rearrange("p (q t b) -> p t q b", t=4, b=2)
+            src_s = w1_s[:, K:H].rearrange("p (q t) -> p t q", t=4)
+            for s in range(4, SLICES):
+                t = DEALT[s]
+                nc.gpsimd.tensor_copy(words[:, t, :, :], src_w[:, t, :, :])
+                nc.gpsimd.tensor_copy(scales[:, t, :], src_s[:, t, :])
+            w1_dealt.extend([words, scales])
 
-        def make_stigma(s):
-            if s < 2:
-                stigma = work.tile([P, S], F32, name="stigma", tag="stigma", bufs=1)
+        pollen, h2, placed, scaled, weather_sb, sums, z_rows, dealt_wg = {}, {}, {}, {}, {}, {}, {}, {}
+
+        def column_block(s):
+            return s if s < 4 else 4 + DEALT[s]
+
+        def first_products(kind, s):
+            made = work.tile([P, S], F32, name="made", tag="made_" + kind, bufs=3 if kind == "a" else 2)
+            j = column_block(s)
+            if kind == "b":
+                codes, scales = w2_c[:, P * j : P * (j + 1)].bitcast(FP8X4), w2_s[:, P * j : P * (j + 1)]
+            elif s < 4:
+                codes, scales = w1_w[:, 2 * P * j : 2 * P * (j + 1)].bitcast(FP4X4), w1_s[:, P * j : P * (j + 1)]
             else:
-                stigma = shared.tile([P, S], F32, name="stigma%d" % (s % 2), offset=AT_WEATHER[s % 2])
-            to_b[s] = shared.tile([P, S], F32, name="to_b%d" % (s % 2), offset=AT_TO_B[s % 2])
-            halves = [slice(BANK * h, BANK * (h + 1)) for h in range(2)]
-            for cols in halves:
-                nc.gpsimd.tensor_tensor(stigma[:, cols], h2[s][:, cols], pollen[s][:, cols], MULT)
-            for cols in halves:
-                nc.gpsimd.tensor_tensor(to_b[s][:, cols], stigma[:, cols], wg2_gain[:, cols], MULT)
-
-        def scatter_a(s, parts):
-            n = S // parts
-            for i in range(parts):
-                nc.vector.tensor_copy(
-                    page_a[s % 2][:].indirect(list2[:, i * n // 16 : (i + 1) * n // 16]),
-                    to_a[s][:, i * n : (i + 1) * n],
+                codes = w1_dealt[0][:, j - 4, :, :].rearrange("p q b -> p (q b)").bitcast(FP4X4)
+                scales = w1_dealt[1][:, j - 4, :]
+            for h in range(2):
+                acc = bank("s%d" % h)
+                nc.tensor.matmul_mx(
+                    out=acc[:], lhsT=codes, lhsT_scale=scales, rhs=v_w[h][:].bitcast(FP8X4),
+                    rhs_scale=v_s[:, chunk(h)], start=True, stop=True,
                 )
+                if (kind, s, h) == ("a", 0, 0):
+                    placed[kind, s] = work.tile([P, S], F32, name="placed", tag="placed", bufs=3)
+                    nc.vector.tensor_tensor(placed[kind, s][:, chunk(0)], acc[:], wg1_sb[:, chunk(0)], MULT)
+                if kind == "a":
+                    nc.scalar.copy(made[:, chunk(h)], acc[:])
+                else:
+                    nc.scalar.activation(made[:, chunk(h)], acc[:], COPY, scale=-1.0)
+            (pollen if kind == "a" else h2)[s] = made
 
-        def scatter_b(s):
-            nc.vector.tensor_copy(page_b[s % 2][:].indirect(list3[:]), to_b[s][:])
+        def load_dealt_wg(kind, s):
+            tile = shared.tile([P, S], F32, name="dealt_wg_%s%d" % (kind, s), offset=AT_DEALT_WG[kind, s])
+            rows = (wg1 if kind == "a" else wg2).rearrange("(q t) j -> t q j", t=4)[DEALT[s]]
+            for g in range(4):
+                nc.sync.dma_start(tile[32 * g : 32 * (g + 1), :], rows)
+            dealt_wg[kind, s] = tile
+
+        def weigh(kind, s):
+            if s >= 4:
+                wg = dealt_wg[kind, s]
+            else:
+                wg = wg1_sb if kind == "a" else wg2_sb
+            halves = [chunk(0), chunk(1)]
+            if (kind, s) == ("a", 0):
+                halves = [chunk(1)]
+            else:
+                placed[kind, s] = work.tile([P, S], F32, name="placed", tag="placed", bufs=3)
+            src = pollen[s]
+            if kind == "b":
+                if s < 3:
+                    src = shared.tile([P, S], F32, name="stigma%d" % s, offset=AT_FIRST_STIGMA[s])
+                else:
+                    src = work.tile([P, S], F32, name="stigma", tag="stigma", bufs=1)
+            for cols in halves:
+                if kind == "b":
+                    nc.gpsimd.tensor_tensor(src[:, cols], h2[s][:, cols], pollen[s][:, cols], MULT)
+                nc.gpsimd.tensor_tensor(placed[kind, s][:, cols], src[:, cols], wg[:, cols], MULT)
+
+        def scatter(kind, s):
+            page, offsets = (page_a[s % 2], list2) if kind == "a" else (page_b[s % 2], list3)
+            if s == 0:
+                for h in range(2):
+                    nc.vector.tensor_copy(
+                        page[:].indirect(offsets[:, 32 * h : 32 * (h + 1)]), placed[kind, s][:, chunk(h)]
+                    )
+            else:
+                nc.vector.tensor_copy(page[:].indirect(offsets[:]), placed[kind, s][:])
 
         def load_weather(s):
-            weather_sb[s] = shared.tile([P, T2], F32, name="weather%d" % (s % 2), offset=AT_WEATHER[s % 2])
-            nc.sync.dma_start(weather_sb[s][:], weather[P * s : P * (s + 1), :])
-
-        def load_last_weather(s):
-            weather_sb[s] = shared.tile([P, T2], F32, name="last_weather", offset=AT_LAST_WEATHER)
-            for c in range(CHUNKS):
-                cols = slice(BANK * c, BANK * (c + 1))
-                nc.sync.dma_start(weather_sb[s][:, cols], weather[P * s : P * (s + 1), cols])
+            weather_sb[s] = shared.tile([P, T2], F32, name="weather%d" % s, offset=AT_WEATHER[s % 2])
+            if s < 4:
+                rows = weather[P * s : P * (s + 1), :]
+            else:
+                rows = weather[K:H, :].rearrange("(p t) m -> t p m", t=4)[DEALT[s]]
+            nc.sync.dma_start(weather_sb[s][:], rows)
 
         def gelu_gain(s):
             scaled[s] = shared.tile([P, T2], F32, name="scaled%d" % (s % 2), offset=AT_ROWS[s % 2])
+            j = s if s < 4 else 8 + DEALT[s]
+            if s < SLICES - 1:
+                nc.scalar.activation(scaled[s][:], page_a[s % 2][:], GELU)
             for h in range(2):
                 cols = slice(h * T2 // 2, (h + 1) * T2 // 2)
-                nc.scalar.activation(scaled[s][:, cols], page_a[s % 2][:, cols], GELU)
-            for h in range(2):
-                cols = slice(h * T2 // 2, (h + 1) * T2 // 2)
-                nc.scalar.activation(scaled[s][:, cols], scaled[s][:, cols], COPY, scale=gain_sb[:, s : s + 1])
+                if s == SLICES - 1:
+                    nc.scalar.activation(scaled[s][:, cols], page_a[s % 2][:, cols], GELU)
+                nc.scalar.activation(scaled[s][:, cols], scaled[s][:, cols], COPY, scale=gain_sb[:, j : j + 1])
+
+        summed = {}
+
+        def add_weather(s, c):
+            tag = "stigma" if c == 0 else "z_rows%d" % (c - 1)
+            summed[c] = work.tile([P, BANK], F32, name="summed", tag=tag, bufs=1)
+            nc.gpsimd.tensor_tensor(summed[c][:], scaled[s][:, chunk(c)], weather_sb[s][:, chunk(c)], ADD)
+
+        def pair_half(s, c):
+            t = DEALT[s]
+            return pairs[c][:, t // 2, :].bitcast(BF16).rearrange("p (m e) -> p m e", e=2)[:, :, t % 2]
+
+        def add_in_place(engine, s, c):
+            engine.tensor_tensor(pair_half(s, c), summed[c][:], page_b[s % 2][:, chunk(c)], ADD)
 
         def add_term(acc, src, c, start, stop):
             for mb in range(4):
                 cols = slice(BANK * c + P * mb, BANK * c + P * (mb + 1))
                 nc.tensor.matmul(
-                    acc[:, P * mb : P * (mb + 1)],
-                    src[:, cols],
-                    ident[:],
-                    start=(start and mb == 0),
-                    stop=(stop and mb == 3),
-                    is_transpose=True,
+                    acc[:, P * mb : P * (mb + 1)], src[:, cols], ident[:],
+                    start=(start and mb == 0), stop=(stop and mb == 3), is_transpose=True,
                 )
 
-        def open_sum(s, c, tag):
+        def open_sums(s):
+            for c in range(CHUNKS):
+                sums[s, c] = bank("z%d" % c)
+                add_term(sums[s, c], weather_sb[s], c, True, False)
+                if c < CHUNKS - 1 or s == 6:
+                    add_term(sums[s, c], scaled[s], c, False, False)
+
+        def close_sum(s, c):
+            acc = sums[s, c]
+            if c == CHUNKS - 1 and s < 6:
+                add_term(acc, scaled[s], c, False, False)
+            add_term(acc, page_b[s % 2], c, False, True)
+            if s < 4:
+                if s == 0:
+                    z_rows[c] = work.tile([P, 4, 2, P, 2], BF16, name="z_rows", tag="z_rows%d" % c, bufs=1)
+                nc.scalar.copy(
+                    z_rows[c][:, :, :, 32 * s : 32 * (s + 1), :],
+                    acc[:].rearrange("m (b p u e) -> m b u p e", b=4, u=2, e=2),
+                )
+            elif s == 4:
+                z_rows[c] = work.tile([P, BANK], F32, name="z_rows", tag="z_rows%d" % c, bufs=1)
+                nc.scalar.copy(z_rows[c][:], acc[:])
+                nc.scalar.copy(pair_half(s, c), turn_back(z_rows[c][:], "x%d" % (c % 2))[:])
+            else:
+                if DEALT[s] == 0:
+                    z_rows[c] = work.tile([P, BANK, 2], BF16, name="z_rows", tag="z_rows%d" % c, bufs=1)
+                nc.scalar.copy(z_rows[c][:, :, DEALT[s]], acc[:])
+
+        def turn_back(words, tag):
             acc = bank(tag)
-            add_term(acc, scaled[s], c, True, False)
-            if s < SLICES - 1:
-                add_term(acc, weather_sb[s], c, False, False)
+            for i in range(4):
+                nc.tensor.transpose(acc[:, P * i : P * (i + 1)], words[:, P * i : P * (i + 1)], ident[:])
             return acc
+
+        def new_z_k(chunks, i):
+            return shared.tile([P, chunks * 4 * BANK], BF16, name="z_k%d_%d" % (chunks, i % 2), offset=AT_Z_K[i % 2], align_bytes=64)
+
+        def quantize_z(z_k, chunks, i):
+            if chunks == 2:
+                z_c = shared.tile([P, 2 * BANK], U32, name="z_first%d" % i, offset=AT_Z_CODES[i], align_bytes=64)
+            else:
+                z_c = work.tile([P, BANK], U32, name="z_c", tag="z_c", bufs=4, align_bytes=64)
+            z_s = work.tile([P, chunks * BANK], U8, name="z_s", tag="z_s%d" % chunks, bufs=4 // chunks, align_bytes=64)
+            nc.vector.quantize_mx(out=z_c[:].bitcast(FP8X4), scales=z_s[:], in_=z_k[:])
+            return [(z_c[:, chunk(i)], z_s[:, chunk(i)]) for i in range(chunks)]
+
+        z_first = []
+        z_turned = []
+
+        def finish_first_pass():
+            for pair in range(2):
+                z_k = new_z_k(2, pair)
+                for j in range(2):
+                    words = z_rows[2 * pair + j][:].rearrange("m b u p e -> m (b u p e)").bitcast(F32)
+                    for half in range(2):
+                        acc = turn_back(words[:, chunk(half)], "x%d" % half)
+                        nc.scalar.copy(
+                            z_k[:].bitcast(F32)[:, chunk(2 * j + half)].rearrange("p (b m u) -> p b m u", b=2, u=2),
+                            acc[:].rearrange("p (b u m) -> p b m u", b=2, u=2),
+                        )
+                z_turned.append(z_k)
+
+        def after(kind, s):
+            if kind == "a":
+                gelu_gain(s)
+                if s == SLICES - 1:
+                    add_weather(s, 0)
+                if s == 1:
+                    open_sums(0)
+                    load_weather(2)
+                return
+            for c in range(CHUNKS):
+                close_sum(s, c)
+                if s == 6:
+                    words = z_rows[c][:].rearrange("m x e -> m (x e)").bitcast(F32)
+                    acc = turn_back(words, "x%d" % (c % 2))
+                    nc.scalar.copy(pairs[c][:, 0, :], acc[:])
+                    if c + 1 < CHUNKS:
+                        add_weather(s + 1, c + 1)
+            if s == 3:
+                finish_first_pass()
+            if s + 1 < SLICES - 1:
+                open_sums(s + 1)
+                if s + 3 < SLICES:
+                    load_weather(s + 3)
+
+        order = [("a", 0), ("a", 1), ("a", 2), ("b", 0), ("b", 1)]
+        for s in range(3, SLICES):
+            order.extend([("a", s), ("b", s - 1)])
+        order.append(("b", SLICES - 1))
+
+        def ahead(n):
+            if n < len(order):
+                if order[n][1] >= 4:
+                    load_dealt_wg(*order[n])
+                first_products(*order[n])
+
+        first_products("a", 0)
+        weigh("a", 0)
+        scatter("a", 0)
+        page_a.append(shared.tile([P, T2], F32, name="page_a1", offset=AT_PAGE_A1))
+        nc.gpsimd.memset(page_a[1][:], 0.0)
+        first_products("a", 1)
+        weigh("a", 1)
+        scatter("a", 1)
+        prepare_w2()
+        load_weather(0)
+        load_weather(1)
+        make_identity(nc, ident[:])
+        first_products("a", 2)
+        weigh("a", 2)
+        ahead(3)
+        ahead(4)
+        weigh(*order[3])
+        ahead(5)
+        weigh(*order[4])
+        after("a", 0)
+        after("a", 1)
+        cast_w3()
+        pairs = [shared.tile([P, 2, BANK], F32, name="pairs%d" % c, offset=AT_PAIRS + 4096 * c) for c in range(CHUNKS)]
+        deal_w1()
+        for n in range(2, len(order) - 1):
+            if order[n] in (("a", 4), ("a", 5)):
+                quantize_w3(order[n][1] - 4)
+            if order[n] in (("a", 6), ("a", 7)):
+                z_first.extend(quantize_z(z_turned[order[n][1] - 6], 2, order[n][1] - 6))
+            scatter(*order[n])
+            if n + 3 < len(order):
+                weigh(*order[n + 3])
+            ahead(n + 4)
+            after(*order[n])
+        last = SLICES - 1
+        scatter("b", last)
+
+        out_tags = (("s0", "s1", "z0"), ("z1", "z2", "z3"), ("x0", "x1", "s0"), ("s1", "z0", "z1"))
+        outs = {}
+
+        def last_product(c, b, z):
+            for a in range(NT):
+                if b == 0:
+                    outs[c, a] = bank(out_tags[c][a])
+                codes, scales = w3_blocks[NT * b + a]
+                nc.tensor.matmul_mx(
+                    out=outs[c, a][:], lhsT=codes.bitcast(FP8X4), lhsT_scale=scales,
+                    rhs=z[0].bitcast(FP8X4), rhs_scale=z[1], start=(b == 0), stop=(b == 1),
+                )
 
         def copy_on(engine, dst, src):
             if engine == "vector":
@@ -234,146 +425,29 @@ def tile_list_cherry_pollination_scores_kernel(
             else:
                 nc.scalar.copy(dst, src)
 
-        def close_sum(s, c, acc, engine):
-            add_term(acc, page_b[s % 2], c, False, True)
-            if s % 4 == 0:
-                z_rows[c] = work.tile([P, 4, 2, P, 2], BF16, name="z_rows", tag="z_rows%d" % c, bufs=1)
-            q = s % 4
-            copy_on(
-                engine,
-                z_rows[c][:, :, :, 32 * q : 32 * (q + 1), :],
-                acc[:].rearrange("m (b p u e) -> m b u p e", b=4, u=2, e=2),
-            )
-
-        def new_z_k(chunks):
-            return work.tile([P, chunks * 4 * BANK], BF16, name="z_k", tag="z_k", bufs=2, align_bytes=64)
-
-        def turn_back(c, z_k, tags, engines):
-            words = z_rows[c][:].rearrange("m b u p e -> m (b u p e)").bitcast(F32)
-            for half in range(2):
-                acc = bank(tags[half])
-                for i in range(4):
-                    src = 4 * half + i
-                    nc.tensor.transpose(acc[:, P * i : P * (i + 1)], words[:, P * src : P * (src + 1)], ident[:])
-                copy_on(
-                    engines[half],
-                    z_k.bitcast(F32)[:, BANK * half : BANK * (half + 1)].rearrange("p (b m u) -> p b m u", b=2, u=2),
-                    acc[:].rearrange("p (b u m) -> p b m u", b=2, u=2),
-                )
-
-        def quantize_z(z_k, chunks):
-            z_c = work.tile([P, chunks * BANK], U32, name="z_c", tag="z_c%d" % chunks, bufs=4 // chunks, align_bytes=64)
-            z_s = work.tile([P, chunks * BANK], U8, name="z_s", tag="z_s%d" % chunks, bufs=4 // chunks, align_bytes=64)
-            nc.vector.quantize_mx(out=z_c[:].bitcast(FP8X4), scales=z_s[:], in_=z_k[:])
-            return [(z_c[:, BANK * i : BANK * (i + 1)], z_s[:, BANK * i : BANK * (i + 1)]) for i in range(chunks)]
-
-        def last_product(acc, b, a, z, start, stop):
-            cols = slice(N * b + P * a, N * b + P * (a + 1))
-            nc.tensor.matmul_mx(
-                out=acc[:],
-                lhsT=w3_c[:, cols].bitcast(FP8X4),
-                lhsT_scale=w3_s[:, cols],
-                rhs=z[0].bitcast(FP8X4),
-                rhs_scale=z[1],
-                start=start,
-                stop=stop,
-            )
-
-        def sum_slice(s):
-            opened = [open_sum(s, c, "z%d" % c) for c in range(CHUNKS)]
-            for c in range(CHUNKS):
-                close_sum(s, c, opened[c], "scalar")
-
-        def store(c, a, result):
-            nc.sync.dma_start(out[P * a : P * (a + 1), BANK * c : BANK * (c + 1)], result[:])
-
-        make_pollen(0)
-        scatter_a(0, 2)
-        page_a.append(shared.tile([P, T2], F32, name="page_a1", offset=AT_PAGE_A1))
-        nc.gpsimd.memset(page_a[1][:], 0.0)
-        make_pollen(1)
-        scatter_a(1, 1)
-        cast_w2(0)
-        cast_w2(1)
-        quantize_w2()
-        load_weather(0)
-        make_identity(nc, ident[:])
-        page_b = [shared.tile([P, T2], F32, name="page_b0", offset=AT_PAGE_B0), page_b1]
-        nc.gpsimd.memset(page_b[0][:], 0.0)
-        make_pollen(2)
-        gelu_gain(0)
-        scatter_a(2, 1)
-        make_h2(0)
-        make_stigma(0)
-        scatter_b(0)
-        make_h2(1)
-        make_stigma(1)
-        scatter_b(1)
-        prepare_w3()
-        load_weather(1)
-        last = SLICES - 1
-        for i in range(1, last - 1):
-            gelu_gain(i)
-            make_pollen(i + 2)
-            scatter_a(i + 2, 1)
-            make_h2(i + 1)
-            sum_slice(i - 1)
-            make_stigma(i + 1)
-            load_weather(i + 1)
-            scatter_b(i + 1)
-            if i == 4:
-                z_first = []
-                for pair in range(2):
-                    z_k = new_z_k(2)
-                    for j in range(2):
-                        part = z_k[:, 4 * BANK * j : 4 * BANK * (j + 1)]
-                        turn_back(2 * pair + j, part, ("x0", "x1"), ("scalar", "scalar"))
-                    z_first.extend(quantize_z(z_k, 2))
-        gelu_gain(last - 1)
-        make_h2(last)
-        sum_slice(last - 2)
-        make_stigma(last)
-        gelu_gain(last)
-        opened = [open_sum(last, c, tag) for c, tag in enumerate(("s0", "s1", "x0", "x1"))]
-        sum_slice(last - 1)
-        load_last_weather(last)
-        scatter_b(last)
-        out_tags = (("z0", "z1", "z2"), ("z3", "z0", "z1"), ("z2", "s0", "s1"), ("z3", "x0", "x1"))
-        turn_tags = (("s0", "s1"), ("x0", "x1"))
-        sums = {}
-
-        def open_out(c, a):
-            sums[c, a] = bank(out_tags[c][a])
-            last_product(sums[c, a], 0, a, z_first[c], True, False)
+        def weave(c, engine):
+            z_k = new_z_k(1, c)
+            copy_on(engine, z_k[:].bitcast(F32).rearrange("p (m u) -> p m u", u=2), pairs[c][:].rearrange("p u m -> p m u"))
+            return z_k
 
         def leave(c):
             for a in range(NT):
                 result = work.tile([P, BANK], F32, name="result", tag="result", bufs=6)
-                on_vector = (a == 1) if c == CHUNKS - 1 else (a != 1)
-                copy_on("vector" if on_vector else "scalar", result[:], sums[c, a][:])
-                store(c, a, result)
+                copy_on("vector" if (c == CHUNKS - 1 and a == 1) else "scalar", result[:], outs[c, a][:])
+                nc.sync.dma_start(out[P * a : P * (a + 1), chunk(c)], result[:])
 
-        for a in range(NT):
-            open_out(0, a)
-        for c in range(CHUNKS):
-            add_term(opened[c], weather_sb[last], c, False, False)
-        open_out(1, 0)
-        for c in range(CHUNKS):
-            close_sum(last, c, opened[c], ("vector", "scalar")[c % 2])
+        for c in range(2):
+            last_product(c, 0, z_first[c])
         z_k = {}
         for c in range(2):
-            z_k[c] = new_z_k(1)
-            turn_back(c, z_k[c][:], turn_tags[c], ("scalar", ("vector", "scalar")[c]))
+            add_in_place(nc.vector, last, c)
+            z_k[c] = weave(c, "vector")
         for c in range(CHUNKS):
-            z = quantize_z(z_k[c], 1)[0]
+            z = quantize_z(z_k[c], 1, c)[0]
             if c + 2 < CHUNKS:
-                z_k[c + 2] = new_z_k(1)
-                turn_back(c + 2, z_k[c + 2][:], turn_tags[c % 2], ("scalar", "scalar"))
-            if c > 0:
-                leave(c - 1)
-            for a in range(NT):
-                if (c, a) not in sums:
-                    open_out(c, a)
-            for a in range(NT):
-                last_product(sums[c, a], 1, a, z, False, True)
-        leave(CHUNKS - 1)
+                add_in_place(nc.vector, last, c + 2)
+                z_k[c + 2] = weave(c + 2, "vector")
+            if c >= 2:
+                last_product(c, 0, z_first[c])
+            last_product(c, 1, z)
+            leave(c)

@@ -34,17 +34,17 @@ AT_TAB_W = 24544
 AT_WG2 = 24576
 AT_Z_K = (45120, 58944)
 AT_W2_BF = 53248
-AT_W1_DEALT = 57408
-AT_LAST_WEATHER = 67136
-AT_WEATHER = (71232, 8192)
+AT_LAST_WEATHER = 67904
+AT_WEATHER = (108864, 8192)
 AT_PAIRS = 79424
 AT_WG1 = 95808
 AT_W3_CODES = (53312, AT_WG1)
-AT_Z_CODES = (99904, 104000)
-AT_FIRST_STIGMA = (AT_Z_CODES[0], AT_Z_CODES[1], AT_LAST_WEATHER)
+AT_Z_CODES = (100288, 104768)
+AT_FIRST_STIGMA = (AT_Z_CODES[0] - 384, AT_Z_CODES[1] - 384, AT_LAST_WEATHER - 768)
+AT_W1_DEALT = {4: AT_FIRST_STIGMA[0], 5: AT_FIRST_STIGMA[1], 6: AT_FIRST_STIGMA[2], 7: AT_FIRST_STIGMA[2] + 384}
 AT_DEALT_WG = {
-    ("a", 4): AT_W3_CODES[0], ("a", 5): AT_W3_CODES[1], ("a", 6): AT_Z_CODES[0], ("a", 7): AT_Z_CODES[1],
-    ("b", 4): AT_WG2, ("b", 5): AT_LAST_WEATHER, ("b", 6): AT_WG2, ("b", 7): AT_LAST_WEATHER,
+    ("a", 4): AT_W3_CODES[0], ("a", 5): AT_W3_CODES[1], ("a", 6): AT_Z_CODES[0], ("a", 7): AT_LAST_WEATHER,
+    ("b", 4): AT_WG2, ("b", 5): AT_LAST_WEATHER, ("b", 6): AT_Z_CODES[1], ("b", 7): AT_LAST_WEATHER,
 }
 
 
@@ -150,18 +150,14 @@ def tile_list_cherry_pollination_scores_kernel(
             for j in range((hi - lo) // P):
                 w3_blocks.append((codes[:, P * j : P * (j + 1)], scales[:, P * j : P * (j + 1)]))
 
-        w1_dealt = []
-
-        def deal_w1():
-            words = shared.tile([P, 4, P, 2], U8, name="w1_dealt_w", offset=AT_W1_DEALT, align_bytes=64)
-            scales = shared.tile([P, 4, P], U8, name="w1_dealt_s", offset=AT_W1_DEALT + H, align_bytes=64)
+        def deal_w1(s):
+            words = shared.tile([P, P, 2], U8, name="w1_dealt_w%d" % s, offset=AT_W1_DEALT[s], align_bytes=64)
+            scales = shared.tile([P, P], U8, name="w1_dealt_s%d" % s, offset=AT_W1_DEALT[s] + 2 * P, align_bytes=64)
             src_w = w1_w[:, H : 2 * H].rearrange("p (q t b) -> p t q b", t=4, b=2)
             src_s = w1_s[:, K:H].rearrange("p (q t) -> p t q", t=4)
-            for s in range(4, SLICES):
-                t = DEALT[s]
-                nc.gpsimd.tensor_copy(words[:, t, :, :], src_w[:, t, :, :])
-                nc.gpsimd.tensor_copy(scales[:, t, :], src_s[:, t, :])
-            w1_dealt.extend([words, scales])
+            nc.gpsimd.tensor_copy(words[:], src_w[:, DEALT[s], :, :])
+            nc.gpsimd.tensor_copy(scales[:], src_s[:, DEALT[s], :])
+            return words[:].rearrange("p q b -> p (q b)").bitcast(FP4X4), scales[:]
 
         pollen, h2, placed, scaled, weather_sb, sums, z_rows, dealt_wg = {}, {}, {}, {}, {}, {}, {}, {}
 
@@ -176,8 +172,7 @@ def tile_list_cherry_pollination_scores_kernel(
             elif s < 4:
                 codes, scales = w1_w[:, 2 * P * j : 2 * P * (j + 1)].bitcast(FP4X4), w1_s[:, P * j : P * (j + 1)]
             else:
-                codes = w1_dealt[0][:, j - 4, :, :].rearrange("p q b -> p (q b)").bitcast(FP4X4)
-                scales = w1_dealt[1][:, j - 4, :]
+                codes, scales = deal_w1(s)
             for h in range(2):
                 acc = bank("s%d" % h)
                 nc.tensor.matmul_mx(
@@ -242,27 +237,29 @@ def tile_list_cherry_pollination_scores_kernel(
         def gelu_gain(s):
             scaled[s] = shared.tile([P, T2], F32, name="scaled%d" % (s % 2), offset=AT_ROWS[s % 2])
             j = s if s < 4 else 8 + DEALT[s]
-            if s < SLICES - 1:
-                nc.scalar.activation(scaled[s][:], page_a[s % 2][:], GELU)
+            nc.scalar.activation(scaled[s][:], page_a[s % 2][:], GELU)
             for h in range(2):
                 cols = slice(h * T2 // 2, (h + 1) * T2 // 2)
-                if s == SLICES - 1:
-                    nc.scalar.activation(scaled[s][:, cols], page_a[s % 2][:, cols], GELU)
                 nc.scalar.activation(scaled[s][:, cols], scaled[s][:, cols], COPY, scale=gain_sb[:, j : j + 1])
 
-        summed = {}
-
-        def add_weather(s, c):
-            tag = "stigma" if c == 0 else "z_rows%d" % (c - 1)
-            summed[c] = work.tile([P, BANK], F32, name="summed", tag=tag, bufs=1)
-            nc.gpsimd.tensor_tensor(summed[c][:], scaled[s][:, chunk(c)], weather_sb[s][:, chunk(c)], ADD)
+        def add_last_page(s):
+            for c in range(CHUNKS):
+                nc.gpsimd.tensor_tensor(
+                    weather_sb[s][:, chunk(c)], weather_sb[s][:, chunk(c)], page_b[s % 2][:, chunk(c)], ADD
+                )
 
         def pair_half(s, c):
             t = DEALT[s]
             return pairs[c][:, t // 2, :].bitcast(BF16).rearrange("p (m e) -> p m e", e=2)[:, :, t % 2]
 
-        def add_in_place(engine, s, c):
-            engine.tensor_tensor(pair_half(s, c), summed[c][:], page_b[s % 2][:, chunk(c)], ADD)
+        def finish_last(s, c):
+            if c == 0:
+                scaled[s] = work.tile([P, T2], F32, name="last_gelu", tag="z_rows3", bufs=1)
+            j = 8 + DEALT[s]
+            nc.scalar.activation(scaled[s][:, chunk(c)], page_a[s % 2][:, chunk(c)], GELU)
+            nc.vector.scalar_tensor_tensor(
+                pair_half(s, c), scaled[s][:, chunk(c)], gain_sb[:, j : j + 1], weather_sb[s][:, chunk(c)], MULT, ADD
+            )
 
         def add_term(acc, src, c, start, stop):
             for mb in range(4):
@@ -337,11 +334,12 @@ def tile_list_cherry_pollination_scores_kernel(
         def after(kind, s):
             if kind == "a":
                 gelu_gain(s)
-                if s == SLICES - 1:
-                    add_weather(s, 0)
                 if s == 1:
                     open_sums(0)
                     load_weather(2)
+                return
+            if s == SLICES - 1:
+                add_last_page(s)
                 return
             for c in range(CHUNKS):
                 close_sum(s, c)
@@ -349,8 +347,6 @@ def tile_list_cherry_pollination_scores_kernel(
                     words = z_rows[c][:].rearrange("m x e -> m (x e)").bitcast(F32)
                     acc = turn_back(words, "x%d" % (c % 2))
                     nc.scalar.copy(pairs[c][:, 0, :], acc[:])
-                    if c + 1 < CHUNKS:
-                        add_weather(s + 1, c + 1)
             if s == 3:
                 finish_first_pass()
             if s + 1 < SLICES - 1:
@@ -359,15 +355,18 @@ def tile_list_cherry_pollination_scores_kernel(
                     load_weather(s + 3)
 
         order = [("a", 0), ("a", 1), ("a", 2), ("b", 0), ("b", 1)]
-        for s in range(3, SLICES):
+        for s in range(3, SLICES - 1):
             order.extend([("a", s), ("b", s - 1)])
-        order.append(("b", SLICES - 1))
+        order.extend([("b", 6), ("b", 7), ("a", 7)])
 
         def ahead(n):
             if n < len(order):
                 if order[n][1] >= 4:
                     load_dealt_wg(*order[n])
-                first_products(*order[n])
+                if order[n] == ("b", 7):
+                    first_products("a", 7)
+                if order[n] != ("a", 7):
+                    first_products(*order[n])
 
         first_products("a", 0)
         weigh("a", 0)
@@ -392,19 +391,19 @@ def tile_list_cherry_pollination_scores_kernel(
         after("a", 1)
         cast_w3()
         pairs = [shared.tile([P, 2, BANK], F32, name="pairs%d" % c, offset=AT_PAIRS + 4096 * c) for c in range(CHUNKS)]
-        deal_w1()
         for n in range(2, len(order) - 1):
             if order[n] in (("a", 4), ("a", 5)):
                 quantize_w3(order[n][1] - 4)
-            if order[n] in (("a", 6), ("a", 7)):
-                z_first.extend(quantize_z(z_turned[order[n][1] - 6], 2, order[n][1] - 6))
+            if order[n][1] == 6:
+                i = len(z_first) // 2
+                z_first.extend(quantize_z(z_turned[i], 2, i))
             scatter(*order[n])
             if n + 3 < len(order):
                 weigh(*order[n + 3])
             ahead(n + 4)
             after(*order[n])
         last = SLICES - 1
-        scatter("b", last)
+        scatter("a", last)
 
         out_tags = (("s0", "s1", "z0"), ("z1", "z2", "z3"), ("x0", "x1", "s0"), ("s1", "z0", "z1"))
         outs = {}
@@ -433,19 +432,19 @@ def tile_list_cherry_pollination_scores_kernel(
         def leave(c):
             for a in range(NT):
                 result = work.tile([P, BANK], F32, name="result", tag="result", bufs=6)
-                copy_on("vector" if (c == CHUNKS - 1 and a == 1) else "scalar", result[:], outs[c, a][:])
+                copy_on("vector" if (c == CHUNKS - 1 and a != 1) else "scalar", result[:], outs[c, a][:])
                 nc.sync.dma_start(out[P * a : P * (a + 1), chunk(c)], result[:])
 
         for c in range(2):
             last_product(c, 0, z_first[c])
         z_k = {}
         for c in range(2):
-            add_in_place(nc.vector, last, c)
+            finish_last(last, c)
             z_k[c] = weave(c, "vector")
         for c in range(CHUNKS):
             z = quantize_z(z_k[c], 1, c)[0]
             if c + 2 < CHUNKS:
-                add_in_place(nc.vector, last, c + 2)
+                finish_last(last, c + 2)
                 z_k[c + 2] = weave(c + 2, "vector")
             if c >= 2:
                 last_product(c, 0, z_first[c])

@@ -24,6 +24,7 @@ BANK = 512
 SLICES = H // P
 CHUNKS = T2 // BANK
 NT = N // P
+EARLY = 1024
 DEALT = {4: 2, 5: 0, 6: 1, 7: 3}
 AT_PAGE_B0 = 0
 AT_TAB_S = 6144
@@ -32,10 +33,10 @@ AT_W2_RAW = (8192, 32832)
 AT_PAGE_A1 = 16384
 AT_TAB_W = 24544
 AT_WG2 = 24576
-AT_Z_K = (45120, 58944)
+AT_Z_K = (45120, 108864)
 AT_W2_BF = 53248
 AT_LAST_WEATHER = 67904
-AT_WEATHER = (108864, 8192)
+AT_WEATHER = (8192, 58944)
 AT_PAIRS = 79424
 AT_WG1 = 95808
 AT_W3_CODES = (53312, AT_WG1)
@@ -84,21 +85,24 @@ def tile_list_cherry_pollination_scores_kernel(
         nc.sync.dma_start(list1[:], offs)
         nc.sync.dma_start(list2[:], offs2)
         nc.sync.dma_start(list3[:], offs3)
-        nc.sync.dma_start(tab_w[:], tab_words[0].rearrange("p t i -> p (t i)").bitcast(I32))
+        table = tab_words[0].rearrange("p t i -> p (t i)").bitcast(I32)
+        nc.sync.dma_start(tab_w[:, 0:EARLY], table[:, 0:EARLY])
         for q in range(4):
-            nc.scalar.dma_start(
+            nc.sync.dma_start(
                 tab_s[:].bitcast(I32)[32 * q : 32 * q + 4, :], tab_scales[0, 4 * q : 4 * q + 4, :].bitcast(I32)
             )
+        nc.sync.dma_start(tab_w[:, EARLY:T], table[:, EARLY:T])
+        nc.sync.dma_start(w1_w[:].bitcast(I32), w1_words[0].bitcast(I32))
         for q in range(4):
             nc.gpsimd.dma_start(
                 w1_s[:].bitcast(I32)[32 * q : 32 * q + 4, :], w1_scales[0, 4 * q : 4 * q + 4, :].bitcast(I32)
             )
-        nc.sync.dma_start(w1_w[:].bitcast(I32), w1_words[0].bitcast(I32))
-        nc.sync.dma_start(wg1_sb[:], wg1)
-        nc.vector.memset(page_a[0][:, 0 : T2 // 2 - 1], 0.0)
-        nc.vector.memset(page_a[0][:, T2 // 2 - 1 : T2], 0.0)
+        for h in range(2):
+            nc.sync.dma_start(wg1_sb[:, chunk(h)], wg1[:, chunk(h)])
         page_b1 = keep.tile([P, T2], F32, name="page_b1")
-        nc.vector.memset(page_b1[:], 0.0)
+        for page in (page_a[0], page_b1):
+            nc.vector.memset(page[:, 0 : T2 // 2 - 1], 0.0)
+            nc.vector.memset(page[:, T2 // 2 - 1 : T2], 0.0)
 
         nc.vector.tensor_copy(v_s[:], tab_s[:].indirect(list1[:]))
         for h in range(2):
@@ -137,7 +141,7 @@ def tile_list_cherry_pollination_scores_kernel(
         def cast_w3():
             rounded = shared.tile([P, 2 * N * 4], BF16, name="w3_bf", offset=AT_PAIRS, align_bytes=64)
             for b in range(2):
-                w3_raw = shared.tile([P, 4, N], F32, name="w3_raw%d" % b, offset=AT_Z_K[b])
+                w3_raw = shared.tile([P, 4, N], F32, name="w3_raw%d" % b, offset=AT_Z_K[0])
                 nc.sync.dma_start(w3_raw[:], w3[b * K : (b + 1) * K, :].rearrange("(p j) w -> p j w", j=4))
                 interleave(rounded[:, b * 4 * N : (b + 1) * 4 * N], w3_raw[:])
             w3_bf.append(rounded)
@@ -200,7 +204,7 @@ def tile_list_cherry_pollination_scores_kernel(
                 wg = dealt_wg[kind, s]
             else:
                 wg = wg1_sb if kind == "a" else wg2_sb
-            halves = [chunk(0), chunk(1)]
+            halves = [slice(0, S)] if s > 0 else [chunk(0), chunk(1)]
             if (kind, s) == ("a", 0):
                 halves = [chunk(1)]
             else:
@@ -304,7 +308,7 @@ def tile_list_cherry_pollination_scores_kernel(
             return acc
 
         def new_z_k(chunks, i):
-            return shared.tile([P, chunks * 4 * BANK], BF16, name="z_k%d_%d" % (chunks, i % 2), offset=AT_Z_K[i % 2], align_bytes=64)
+            return shared.tile([P, chunks * 4 * BANK], BF16, name="z_k%d_%d" % (chunks, i), offset=AT_Z_K[i % 2] + 4096 * (i // 2), align_bytes=64)
 
         def quantize_z(z_k, chunks, i):
             if chunks == 2:
@@ -431,8 +435,10 @@ def tile_list_cherry_pollination_scores_kernel(
 
         def leave(c):
             for a in range(NT):
-                result = work.tile([P, BANK], F32, name="result", tag="result", bufs=6)
-                copy_on("vector" if (c == CHUNKS - 1 and a != 1) else "scalar", result[:], outs[c, a][:])
+                i = NT * c + a
+                at = AT_ROWS[0] + 2048 * i if i < 8 else AT_PAGE_B0 + 2048 * (i - 8)
+                result = shared.tile([P, BANK], F32, name="result%d" % i, offset=at)
+                copy_on("vector" if (c, a) in ((2, 2), (3, 0), (3, 2)) else "scalar", result[:], outs[c, a][:])
                 nc.sync.dma_start(out[P * a : P * (a + 1), chunk(c)], result[:])
 
         for c in range(2):
@@ -440,7 +446,7 @@ def tile_list_cherry_pollination_scores_kernel(
         z_k = {}
         for c in range(2):
             finish_last(last, c)
-            z_k[c] = weave(c, "vector")
+            z_k[c] = weave(c, ("vector", "scalar")[c])
         for c in range(CHUNKS):
             z = quantize_z(z_k[c], 1, c)[0]
             if c + 2 < CHUNKS:

@@ -207,6 +207,8 @@ def tile_list_cherry_pollination_scores_kernel(
             halves = [slice(0, S)] if s > 0 else [chunk(0), chunk(1)]
             if (kind, s) == ("a", 0):
                 halves = [chunk(1)]
+            elif (kind, s) == ("a", SLICES - 1):
+                placed[kind, s] = shared.tile([P, S], F32, name="placed_last", offset=AT_Z_CODES[1])
             else:
                 placed[kind, s] = work.tile([P, S], F32, name="placed", tag="placed", bufs=3)
             src = pollen[s]
@@ -222,7 +224,7 @@ def tile_list_cherry_pollination_scores_kernel(
 
         def scatter(kind, s):
             page, offsets = (page_a[s % 2], list2) if kind == "a" else (page_b[s % 2], list3)
-            if s == 0:
+            if (kind, s) == ("a", 0):
                 for h in range(2):
                     nc.vector.tensor_copy(
                         page[:].indirect(offsets[:, 32 * h : 32 * (h + 1)]), placed[kind, s][:, chunk(h)]
@@ -308,7 +310,8 @@ def tile_list_cherry_pollination_scores_kernel(
             return acc
 
         def new_z_k(chunks, i):
-            return shared.tile([P, chunks * 4 * BANK], BF16, name="z_k%d_%d" % (chunks, i), offset=AT_Z_K[i % 2] + 4096 * (i // 2), align_bytes=64)
+            at = AT_Z_K[i] if chunks == 2 else AT_Z_K[i // 2] + 4096 * (i % 2)
+            return shared.tile([P, chunks * 4 * BANK], BF16, name="z_k%d_%d" % (chunks, i), offset=at, align_bytes=64)
 
         def quantize_z(z_k, chunks, i):
             if chunks == 2:
@@ -398,9 +401,8 @@ def tile_list_cherry_pollination_scores_kernel(
         for n in range(2, len(order) - 1):
             if order[n] in (("a", 4), ("a", 5)):
                 quantize_w3(order[n][1] - 4)
-            if order[n][1] == 6:
-                i = len(z_first) // 2
-                z_first.extend(quantize_z(z_turned[i], 2, i))
+            if order[n] == ("a", 6):
+                z_first.extend(quantize_z(z_turned[0], 2, 0))
             scatter(*order[n])
             if n + 3 < len(order):
                 weigh(*order[n + 3])
@@ -408,6 +410,7 @@ def tile_list_cherry_pollination_scores_kernel(
             after(*order[n])
         last = SLICES - 1
         scatter("a", last)
+        z_first.extend(quantize_z(z_turned[1], 2, 1))
 
         out_tags = (("s0", "s1", "z0"), ("z1", "z2", "z3"), ("x0", "x1", "s0"), ("s1", "z0", "z1"))
         outs = {}

@@ -28,19 +28,20 @@ EARLY = 1024
 DEALT = {4: 2, 5: 0, 6: 1, 7: 3}
 AT_PAGE_B0 = 0
 AT_TAB_S = 6144
-AT_ROWS = (28736, 36928)
-AT_W2_RAW = (8192, 32832)
-AT_PAGE_A1 = 16384
-AT_TAB_W = 24544
-AT_WG2 = 24576
-AT_Z_K = (45120, 108864)
-AT_W2_BF = 53248
-AT_LAST_WEATHER = 67904
-AT_WEATHER = (8192, 58944)
-AT_PAIRS = 79424
-AT_WG1 = 95808
-AT_W3_CODES = (53312, AT_WG1)
-AT_Z_CODES = (100288, 104768)
+AT_PAGE_A1 = 24576
+AT_PAGE_B1 = 16384
+AT_W2_RAW = (8224, 41024)
+AT_TAB_W = 32736
+AT_WG2 = 32768
+AT_ROWS = (36928, 45120)
+AT_Z_K = (53312, 117056)
+AT_W2_BF = 61440
+AT_WEATHER = (8192, 67136)
+AT_LAST_WEATHER = 76096
+AT_PAIRS = 87616
+AT_WG1 = 104000
+AT_W3_CODES = (61504, AT_WG1)
+AT_Z_CODES = (108480, 112960)
 AT_FIRST_STIGMA = (AT_Z_CODES[0] - 384, AT_Z_CODES[1] - 384, AT_LAST_WEATHER - 768)
 AT_W1_DEALT = {4: AT_FIRST_STIGMA[0], 5: AT_FIRST_STIGMA[1], 6: AT_FIRST_STIGMA[2], 7: AT_FIRST_STIGMA[2] + 384}
 AT_DEALT_WG = {
@@ -99,16 +100,14 @@ def tile_list_cherry_pollination_scores_kernel(
             )
         for h in range(2):
             nc.sync.dma_start(wg1_sb[:, chunk(h)], wg1[:, chunk(h)])
-        page_b1 = keep.tile([P, T2], F32, name="page_b1")
-        for page in (page_a[0], page_b1):
-            nc.vector.memset(page[:, 0 : T2 // 2 - 1], 0.0)
-            nc.vector.memset(page[:, T2 // 2 - 1 : T2], 0.0)
+        nc.vector.memset(page_a[0][:, 0 : T2 // 2 - 1], 0.0)
+        nc.vector.memset(page_a[0][:, T2 // 2 - 1 : T2], 0.0)
 
         nc.vector.tensor_copy(v_s[:], tab_s[:].indirect(list1[:]))
         for h in range(2):
             nc.vector.tensor_copy(v_w[h][:], tab_w[:].bitcast(U32).indirect(list1[:, 32 * h : 32 * (h + 1)]))
 
-        page_b = [shared.tile([P, T2], F32, name="page_b0", offset=AT_PAGE_B0), page_b1]
+        page_b = [shared.tile([P, T2], F32, name="page_b0", offset=AT_PAGE_B0)]
         nc.gpsimd.memset(page_b[0][:], 0.0)
         w2_raw = [shared.tile([P, 4, BANK], F32, name="w2_raw%d" % h, offset=AT_W2_RAW[h]) for h in range(2)]
         for h in range(2):
@@ -217,6 +216,10 @@ def tile_list_cherry_pollination_scores_kernel(
                     src = shared.tile([P, S], F32, name="stigma%d" % s, offset=AT_FIRST_STIGMA[s])
                 else:
                     src = work.tile([P, S], F32, name="stigma", tag="stigma", bufs=1)
+            if (kind, s) == ("b", 0):
+                nc.gpsimd.tensor_tensor(src[:], pollen[s][:], wg[:], MULT)
+                nc.gpsimd.tensor_tensor(placed[kind, s][:], src[:], h2[s][:], MULT)
+                return
             for cols in halves:
                 if kind == "b":
                     nc.gpsimd.tensor_tensor(src[:, cols], h2[s][:, cols], pollen[s][:, cols], MULT)
@@ -389,6 +392,8 @@ def tile_list_cherry_pollination_scores_kernel(
         make_identity(nc, ident[:])
         first_products("a", 2)
         weigh("a", 2)
+        page_b.append(shared.tile([P, T2], F32, name="page_b1", offset=AT_PAGE_B1))
+        nc.gpsimd.memset(page_b[1][:], 0.0)
         ahead(3)
         ahead(4)
         weigh(*order[3])

@@ -24,14 +24,14 @@ BANK = 512
 SLICES = H // P
 CHUNKS = T2 // BANK
 NT = N // P
-EARLY = 1024
+EARLY = 1280
 DEALT = {4: 2, 5: 0, 6: 1, 7: 3}
-AT_PAGE_B0 = 0
+AT_PAGE_B0 = 24576
 AT_TAB_S = 6144
-AT_PAGE_A1 = 24576
+AT_PAGE_A1 = 0
 AT_PAGE_B1 = 16384
 AT_W2_RAW = (8224, 41024)
-AT_TAB_W = 32736
+AT_TAB_W = 32768
 AT_WG2 = 32768
 AT_ROWS = (36928, 45120)
 AT_Z_K = (53312, 117056)
@@ -84,10 +84,10 @@ def tile_list_cherry_pollination_scores_kernel(
         nc.vector.memset(tab_s[:].bitcast(I32), 0)
         nc.gpsimd.memset(w1_s[:].bitcast(I32), 0)
         nc.sync.dma_start(list1[:], offs)
-        nc.sync.dma_start(list2[:], offs2)
-        nc.sync.dma_start(list3[:], offs3)
         table = tab_words[0].rearrange("p t i -> p (t i)").bitcast(I32)
         nc.sync.dma_start(tab_w[:, 0:EARLY], table[:, 0:EARLY])
+        nc.sync.dma_start(list2[:], offs2)
+        nc.sync.dma_start(list3[:], offs3)
         for q in range(4):
             nc.sync.dma_start(
                 tab_s[:].bitcast(I32)[32 * q : 32 * q + 4, :], tab_scales[0, 4 * q : 4 * q + 4, :].bitcast(I32)
@@ -102,13 +102,15 @@ def tile_list_cherry_pollination_scores_kernel(
             nc.sync.dma_start(wg1_sb[:, chunk(h)], wg1[:, chunk(h)])
         nc.vector.memset(page_a[0][:, 0 : T2 // 2 - 1], 0.0)
         nc.vector.memset(page_a[0][:, T2 // 2 - 1 : T2], 0.0)
+        page_b = [shared.tile([P, T2], F32, name="page_b0", offset=AT_PAGE_B0)]
+        nc.vector.memset(page_b[0][:], 0.0)
 
         nc.vector.tensor_copy(v_s[:], tab_s[:].indirect(list1[:]))
         for h in range(2):
             nc.vector.tensor_copy(v_w[h][:], tab_w[:].bitcast(U32).indirect(list1[:, 32 * h : 32 * (h + 1)]))
 
-        page_b = [shared.tile([P, T2], F32, name="page_b0", offset=AT_PAGE_B0)]
-        nc.gpsimd.memset(page_b[0][:], 0.0)
+        page_a.append(shared.tile([P, T2], F32, name="page_a1", offset=AT_PAGE_A1))
+        nc.gpsimd.memset(page_a[1][:], 0.0)
         w2_raw = [shared.tile([P, 4, BANK], F32, name="w2_raw%d" % h, offset=AT_W2_RAW[h]) for h in range(2)]
         for h in range(2):
             nc.sync.dma_start(w2_raw[h][:], w2[:, chunk(h)].rearrange("(p j) w -> p j w", j=4))
@@ -381,8 +383,6 @@ def tile_list_cherry_pollination_scores_kernel(
         first_products("a", 0)
         weigh("a", 0)
         scatter("a", 0)
-        page_a.append(shared.tile([P, T2], F32, name="page_a1", offset=AT_PAGE_A1))
-        nc.gpsimd.memset(page_a[1][:], 0.0)
         first_products("a", 1)
         weigh("a", 1)
         scatter("a", 1)

@@ -100,8 +100,7 @@ def tile_list_cherry_pollination_scores_kernel(
             )
         for h in range(2):
             nc.sync.dma_start(wg1_sb[:, chunk(h)], wg1[:, chunk(h)])
-        nc.vector.memset(page_a[0][:, 0 : T2 // 2 - 1], 0.0)
-        nc.vector.memset(page_a[0][:, T2 // 2 - 1 : T2], 0.0)
+        nc.vector.memset(page_a[0][:], 0.0)
         page_b = [shared.tile([P, T2], F32, name="page_b0", offset=AT_PAGE_B0)]
         nc.vector.memset(page_b[0][:], 0.0)
 
@@ -184,9 +183,6 @@ def tile_list_cherry_pollination_scores_kernel(
                     out=acc[:], lhsT=codes, lhsT_scale=scales, rhs=v_w[h][:].bitcast(FP8X4),
                     rhs_scale=v_s[:, chunk(h)], start=True, stop=True,
                 )
-                if (kind, s, h) == ("a", 0, 0):
-                    placed[kind, s] = work.tile([P, S], F32, name="placed", tag="placed", bufs=3)
-                    nc.vector.tensor_tensor(placed[kind, s][:, chunk(0)], acc[:], wg1_sb[:, chunk(0)], MULT)
                 if kind == "a":
                     nc.scalar.copy(made[:, chunk(h)], acc[:])
                 else:
@@ -205,10 +201,8 @@ def tile_list_cherry_pollination_scores_kernel(
                 wg = dealt_wg[kind, s]
             else:
                 wg = wg1_sb if kind == "a" else wg2_sb
-            halves = [slice(0, S)] if s > 0 else [chunk(0), chunk(1)]
-            if (kind, s) == ("a", 0):
-                halves = [chunk(1)]
-            elif (kind, s) == ("a", SLICES - 1):
+            halves = [slice(0, S)]
+            if (kind, s) == ("a", SLICES - 1):
                 placed[kind, s] = shared.tile([P, S], F32, name="placed_last", offset=AT_Z_CODES[1])
             else:
                 placed[kind, s] = work.tile([P, S], F32, name="placed", tag="placed", bufs=3)
@@ -229,13 +223,7 @@ def tile_list_cherry_pollination_scores_kernel(
 
         def scatter(kind, s):
             page, offsets = (page_a[s % 2], list2) if kind == "a" else (page_b[s % 2], list3)
-            if (kind, s) == ("a", 0):
-                for h in range(2):
-                    nc.vector.tensor_copy(
-                        page[:].indirect(offsets[:, 32 * h : 32 * (h + 1)]), placed[kind, s][:, chunk(h)]
-                    )
-            else:
-                nc.vector.tensor_copy(page[:].indirect(offsets[:]), placed[kind, s][:])
+            nc.vector.tensor_copy(page[:].indirect(offsets[:]), placed[kind, s][:])
 
         def load_weather(s):
             weather_sb[s] = shared.tile([P, T2], F32, name="weather%d" % s, offset=AT_WEATHER[s % 2])
@@ -380,12 +368,24 @@ def tile_list_cherry_pollination_scores_kernel(
                 if order[n] != ("a", 7):
                     first_products(*order[n])
 
-        first_products("a", 0)
-        weigh("a", 0)
-        scatter("a", 0)
-        first_products("a", 1)
-        weigh("a", 1)
-        scatter("a", 1)
+        for s in range(2):
+            pollen[s] = work.tile([P, S], F32, name="made", tag="made_a", bufs=3)
+            placed["a", s] = work.tile([P, S], F32, name="placed", tag="placed", bufs=3)
+        for h in range(2):
+            for s in range(2):
+                acc = bank("s%d" % s)
+                nc.tensor.matmul_mx(
+                    out=acc[:], lhsT=w1_w[:, 2 * P * s : 2 * P * (s + 1)].bitcast(FP4X4),
+                    lhsT_scale=w1_s[:, P * s : P * (s + 1)], rhs=v_w[h][:].bitcast(FP8X4),
+                    rhs_scale=v_s[:, chunk(h)], start=True, stop=True,
+                )
+                values = placed["a", s][:, chunk(h)]
+                if (s, h) == (0, 0):
+                    nc.vector.tensor_tensor(values, acc[:], wg1_sb[:, chunk(h)], MULT)
+                nc.scalar.copy(pollen[s][:, chunk(h)], acc[:])
+                if (s, h) != (0, 0):
+                    nc.gpsimd.tensor_tensor(values, pollen[s][:, chunk(h)], wg1_sb[:, chunk(h)], MULT)
+                nc.vector.tensor_copy(page_a[s][:].indirect(list2[:, 32 * h : 32 * (h + 1)]), values)
         prepare_w2()
         load_weather(0)
         load_weather(1)

@@ -27,7 +27,7 @@ NT = N // P
 EARLY = 1280
 DEALT = {4: 2, 5: 0, 6: 1, 7: 3}
 AT_PAGE_B0 = 24576
-AT_TAB_S = 6144
+AT_TAB_S = 8192
 AT_PAGE_A1 = 0
 AT_PAGE_B1 = 16384
 AT_W2_RAW = (8224, 41024)
@@ -83,6 +83,7 @@ def tile_list_cherry_pollination_scores_kernel(
 
         nc.vector.memset(tab_s[:].bitcast(I32), 0)
         nc.gpsimd.memset(w1_s[:].bitcast(I32), 0)
+        make_identity(nc, ident[:])
         nc.sync.dma_start(list1[:], offs)
         table = tab_words[0].rearrange("p t i -> p (t i)").bitcast(I32)
         nc.sync.dma_start(tab_w[:, 0:EARLY], table[:, 0:EARLY])
@@ -100,9 +101,8 @@ def tile_list_cherry_pollination_scores_kernel(
             )
         for h in range(2):
             nc.sync.dma_start(wg1_sb[:, chunk(h)], wg1[:, chunk(h)])
-        nc.vector.memset(page_a[0][:], 0.0)
-        page_b = [shared.tile([P, T2], F32, name="page_b0", offset=AT_PAGE_B0)]
-        nc.vector.memset(page_b[0][:], 0.0)
+        nc.vector.memset(page_a[0][:, 0 : T2 // 2 - 1], 0.0)
+        nc.vector.memset(page_a[0][:, T2 // 2 - 1 : T2], 0.0)
 
         nc.vector.tensor_copy(v_s[:], tab_s[:].indirect(list1[:]))
         for h in range(2):
@@ -110,6 +110,8 @@ def tile_list_cherry_pollination_scores_kernel(
 
         page_a.append(shared.tile([P, T2], F32, name="page_a1", offset=AT_PAGE_A1))
         nc.gpsimd.memset(page_a[1][:], 0.0)
+        page_b = [shared.tile([P, T2], F32, name="page_b0", offset=AT_PAGE_B0)]
+        nc.gpsimd.memset(page_b[0][:], 0.0)
         w2_raw = [shared.tile([P, 4, BANK], F32, name="w2_raw%d" % h, offset=AT_W2_RAW[h]) for h in range(2)]
         for h in range(2):
             nc.sync.dma_start(w2_raw[h][:], w2[:, chunk(h)].rearrange("(p j) w -> p j w", j=4))
@@ -389,7 +391,6 @@ def tile_list_cherry_pollination_scores_kernel(
         prepare_w2()
         load_weather(0)
         load_weather(1)
-        make_identity(nc, ident[:])
         first_products("a", 2)
         weigh("a", 2)
         page_b.append(shared.tile([P, T2], F32, name="page_b1", offset=AT_PAGE_B1))

@@ -117,10 +117,10 @@ def tile_list_cherry_pollination_scores_kernel(
             nc.sync.dma_start(w2_raw[h][:], w2[:, chunk(h)].rearrange("(p j) w -> p j w", j=4))
         wg2_sb = shared.tile([P, S], F32, name="wg2_sb", offset=AT_WG2)
         gain_sb = shared.tile([P, 16], F32, name="gain_sb", offset=AT_WG2 + 4 * S)
+        nc.sync.dma_start(wg2_sb[:], wg2)
         with nc.allow_non_contiguous_dma(reason="one gain for each partition and slice"):
             nc.sync.dma_start(gain_sb[:, 0:4], gain[0:K].rearrange("(s p) -> p s", p=P))
             nc.sync.dma_start(gain_sb[:, 8:12], gain[K:H].rearrange("(p t) -> p t", t=4))
-        nc.sync.dma_start(wg2_sb[:], wg2)
 
         def interleave(dst, raw):
             nc.scalar.copy(
@@ -156,6 +156,8 @@ def tile_list_cherry_pollination_scores_kernel(
             for j in range((hi - lo) // P):
                 w3_blocks.append((codes[:, P * j : P * (j + 1)], scales[:, P * j : P * (j + 1)]))
 
+        w1_dealt = {}
+
         def deal_w1(s):
             words = shared.tile([P, P, 2], U8, name="w1_dealt_w%d" % s, offset=AT_W1_DEALT[s], align_bytes=64)
             scales = shared.tile([P, P], U8, name="w1_dealt_s%d" % s, offset=AT_W1_DEALT[s] + 2 * P, align_bytes=64)
@@ -163,7 +165,7 @@ def tile_list_cherry_pollination_scores_kernel(
             src_s = w1_s[:, K:H].rearrange("p (q t) -> p t q", t=4)
             nc.gpsimd.tensor_copy(words[:], src_w[:, DEALT[s], :, :])
             nc.gpsimd.tensor_copy(scales[:], src_s[:, DEALT[s], :])
-            return words[:].rearrange("p q b -> p (q b)").bitcast(FP4X4), scales[:]
+            w1_dealt[s] = (words[:].rearrange("p q b -> p (q b)").bitcast(FP4X4), scales[:])
 
         pollen, h2, placed, scaled, weather_sb, sums, z_rows, dealt_wg = {}, {}, {}, {}, {}, {}, {}, {}
 
@@ -178,7 +180,7 @@ def tile_list_cherry_pollination_scores_kernel(
             elif s < 4:
                 codes, scales = w1_w[:, 2 * P * j : 2 * P * (j + 1)].bitcast(FP4X4), w1_s[:, P * j : P * (j + 1)]
             else:
-                codes, scales = deal_w1(s)
+                codes, scales = w1_dealt[s]
             for h in range(2):
                 acc = bank("s%d" % h)
                 nc.tensor.matmul_mx(
@@ -412,6 +414,8 @@ def tile_list_cherry_pollination_scores_kernel(
             scatter(*order[n])
             if n + 3 < len(order):
                 weigh(*order[n + 3])
+                if order[n + 3][0] == "a" and order[n + 3][1] < SLICES - 1:
+                    deal_w1(order[n + 3][1] + 1)
             ahead(n + 4)
             after(*order[n])
         last = SLICES - 1

@@ -464,7 +464,7 @@ def tile_list_cherry_pollination_scores_kernel(
             z = quantize_z(z_k[c], 1, c)[0]
             if c + 2 < CHUNKS:
                 finish_last(last, c + 2)
-                z_k[c + 2] = weave(c + 2, "vector")
+                z_k[c + 2] = weave(c + 2, ("scalar", "vector")[c])
             if c >= 2:
                 last_product(c, 0, z_first[c])
             last_product(c, 1, z)

@@ -24,11 +24,13 @@ BANK = 512
 SLICES = H // P
 CHUNKS = T2 // BANK
 NT = N // P
-EARLY = 1280
+FIRST = 256
+EARLY = 768
 DEALT = {4: 2, 5: 0, 6: 1, 7: 3}
 AT_PAGE_B0 = 24576
-AT_TAB_S = 8192
-AT_PAGE_A1 = 0
+AT_TAB_S = 6144
+AT_WG1_LATE = 6144
+AT_PAGE_A1 = 125248
 AT_PAGE_B1 = 16384
 AT_W2_RAW = (8224, 41024)
 AT_TAB_W = 32768
@@ -73,40 +75,47 @@ def tile_list_cherry_pollination_scores_kernel(
         tab_s = shared.tile([P, T], U8, name="tab_s", offset=AT_TAB_S)
         w1_w = keep.tile([P, 2 * H], U8, name="w1_w", align_bytes=64)
         w1_s = keep.tile([P, H], U8, name="w1_s", align_bytes=64)
-        wg1_sb = shared.tile([P, S], F32, name="wg1_sb", offset=AT_WG1)
+        wg1_sb = [
+            shared.tile([P, BANK], F32, name="wg1_early", offset=AT_WG1),
+            shared.tile([P, BANK], F32, name="wg1_late", offset=AT_WG1_LATE),
+        ]
         ident = keep.tile([P, P], F32, name="ident")
         page_a = [keep.tile([P, T2], F32, name="page_a0")]
-        v_w = [keep.tile([P, BANK], U32, name="v_w%d" % i, align_bytes=64) for i in range(2)]
-        v_s = keep.tile([P, S], U8, name="v_s", align_bytes=64)
+        v_w = keep.tile([P, S], U32, name="v_w", align_bytes=64)
+        picked_s = [keep.tile([P, BANK], U8, name="picked_s%d" % h, align_bytes=64) for h in range(2)]
+        v_s = [keep.tile([P, BANK], U8, name="v_s%d" % h, align_bytes=64) for h in range(2)]
         w2_c = keep.tile([P, H], U32, name="w2_c", align_bytes=64)
         w2_s = keep.tile([P, H], U8, name="w2_s", align_bytes=64)
 
         nc.vector.memset(tab_s[:].bitcast(I32), 0)
         nc.gpsimd.memset(w1_s[:].bitcast(I32), 0)
-        make_identity(nc, ident[:])
         nc.sync.dma_start(list1[:], offs)
         table = tab_words[0].rearrange("p t i -> p (t i)").bitcast(I32)
         nc.sync.dma_start(tab_w[:, 0:EARLY], table[:, 0:EARLY])
         nc.sync.dma_start(list2[:], offs2)
         nc.sync.dma_start(list3[:], offs3)
-        for q in range(4):
-            nc.sync.dma_start(
-                tab_s[:].bitcast(I32)[32 * q : 32 * q + 4, :], tab_scales[0, 4 * q : 4 * q + 4, :].bitcast(I32)
-            )
+        nc.sync.dma_start(tab_s[:].bitcast(I32)[0:P:8, :], tab_scales[0].bitcast(I32))
         nc.sync.dma_start(tab_w[:, EARLY:T], table[:, EARLY:T])
         nc.sync.dma_start(w1_w[:].bitcast(I32), w1_words[0].bitcast(I32))
         for q in range(4):
             nc.gpsimd.dma_start(
                 w1_s[:].bitcast(I32)[32 * q : 32 * q + 4, :], w1_scales[0, 4 * q : 4 * q + 4, :].bitcast(I32)
             )
-        for h in range(2):
-            nc.sync.dma_start(wg1_sb[:, chunk(h)], wg1[:, chunk(h)])
+        make_identity(nc, ident[:])
+        nc.sync.dma_start(wg1_sb[0][:], wg1[:, chunk(0)])
         nc.vector.memset(page_a[0][:, 0 : T2 // 2 - 1], 0.0)
         nc.vector.memset(page_a[0][:, T2 // 2 - 1 : T2], 0.0)
 
-        nc.vector.tensor_copy(v_s[:], tab_s[:].indirect(list1[:]))
         for h in range(2):
-            nc.vector.tensor_copy(v_w[h][:], tab_w[:].bitcast(U32).indirect(list1[:, 32 * h : 32 * (h + 1)]))
+            nc.vector.tensor_copy(picked_s[h][:], tab_s[:].indirect(list1[:, 32 * h : 32 * (h + 1)]))
+            nc.vector.tensor_copy(v_s[h][:].bitcast(I32), picked_s[h][:].bitcast(I32))
+            for r in range(1, 4):
+                (nc.scalar, nc.sync)[h].dma_start(
+                    v_s[h][:].bitcast(I32)[r:P:32, :], picked_s[h][:].bitcast(I32)[8 * r : P : 32, :]
+                )
+        nc.sync.dma_start(wg1_sb[1][:], wg1[:, chunk(1)])
+        for lo, hi in ((0, FIRST), (FIRST, S)):
+            nc.vector.tensor_copy(v_w[:, lo:hi], tab_w[:].bitcast(U32).indirect(list1[:, lo // 16 : hi // 16]))
 
         page_a.append(shared.tile([P, T2], F32, name="page_a1", offset=AT_PAGE_A1))
         nc.gpsimd.memset(page_a[1][:], 0.0)
@@ -184,8 +193,8 @@ def tile_list_cherry_pollination_scores_kernel(
             for h in range(2):
                 acc = bank("s%d" % h)
                 nc.tensor.matmul_mx(
-                    out=acc[:], lhsT=codes, lhsT_scale=scales, rhs=v_w[h][:].bitcast(FP8X4),
-                    rhs_scale=v_s[:, chunk(h)], start=True, stop=True,
+                    out=acc[:], lhsT=codes, lhsT_scale=scales, rhs=v_w[:, chunk(h)].bitcast(FP8X4),
+                    rhs_scale=v_s[h][:], start=True, stop=True,
                 )
                 if kind == "a":
                     nc.scalar.copy(made[:, chunk(h)], acc[:])
@@ -204,7 +213,7 @@ def tile_list_cherry_pollination_scores_kernel(
             if s >= 4:
                 wg = dealt_wg[kind, s]
             else:
-                wg = wg1_sb if kind == "a" else wg2_sb
+                wg = wg2_sb
             halves = [slice(0, S)]
             if (kind, s) == ("a", SLICES - 1):
                 placed[kind, s] = shared.tile([P, S], F32, name="placed_last", offset=AT_Z_CODES[1])
@@ -219,6 +228,10 @@ def tile_list_cherry_pollination_scores_kernel(
             if (kind, s) == ("b", 0):
                 nc.gpsimd.tensor_tensor(src[:], pollen[s][:], wg[:], MULT)
                 nc.gpsimd.tensor_tensor(placed[kind, s][:], src[:], h2[s][:], MULT)
+                return
+            if kind == "a" and s < 4:
+                for h in range(2):
+                    nc.gpsimd.tensor_tensor(placed[kind, s][:, chunk(h)], src[:, chunk(h)], wg1_sb[h][:], MULT)
                 return
             for cols in halves:
                 if kind == "b":
@@ -375,21 +388,27 @@ def tile_list_cherry_pollination_scores_kernel(
         for s in range(2):
             pollen[s] = work.tile([P, S], F32, name="made", tag="made_a", bufs=3)
             placed["a", s] = work.tile([P, S], F32, name="placed", tag="placed", bufs=3)
-        for h in range(2):
-            for s in range(2):
-                acc = bank("s%d" % s)
-                nc.tensor.matmul_mx(
-                    out=acc[:], lhsT=w1_w[:, 2 * P * s : 2 * P * (s + 1)].bitcast(FP4X4),
-                    lhsT_scale=w1_s[:, P * s : P * (s + 1)], rhs=v_w[h][:].bitcast(FP8X4),
-                    rhs_scale=v_s[:, chunk(h)], start=True, stop=True,
-                )
-                values = placed["a", s][:, chunk(h)]
-                if (s, h) == (0, 0):
-                    nc.vector.tensor_tensor(values, acc[:], wg1_sb[:, chunk(h)], MULT)
-                nc.scalar.copy(pollen[s][:, chunk(h)], acc[:])
-                if (s, h) != (0, 0):
-                    nc.gpsimd.tensor_tensor(values, pollen[s][:, chunk(h)], wg1_sb[:, chunk(h)], MULT)
-                nc.vector.tensor_copy(page_a[s][:].indirect(list2[:, 32 * h : 32 * (h + 1)]), values)
+
+        def early_values(s, lo, hi, tag):
+            h, at = lo // BANK, lo % BANK
+            acc = bank(tag)
+            nc.tensor.matmul_mx(
+                out=acc[:, 0 : hi - lo], lhsT=w1_w[:, 2 * P * s : 2 * P * (s + 1)].bitcast(FP4X4),
+                lhsT_scale=w1_s[:, P * s : P * (s + 1)], rhs=v_w[:, lo:hi].bitcast(FP8X4),
+                rhs_scale=v_s[h][:, at : at + hi - lo], start=True, stop=True,
+            )
+            nc.scalar.copy(pollen[s][:, lo:hi], acc[:, 0 : hi - lo])
+            nc.gpsimd.tensor_tensor(
+                placed["a", s][:, lo:hi], pollen[s][:, lo:hi], wg1_sb[h][:, at : at + hi - lo], MULT
+            )
+
+        for s in range(2):
+            early_values(s, 0, FIRST, "s%d" % s)
+            nc.vector.tensor_copy(page_a[s][:].indirect(list2[:, 0 : FIRST // 16]), placed["a", s][:, 0:FIRST])
+        for s in range(2):
+            early_values(s, FIRST, BANK, ("x0", "s0")[s])
+            early_values(s, BANK, S, ("x1", "s1")[s])
+            nc.vector.tensor_copy(page_a[s][:].indirect(list2[:, FIRST // 16 : S // 16]), placed["a", s][:, FIRST:S])
         prepare_w2()
         load_weather(0)
         load_weather(1)

@@ -31,6 +31,7 @@ AT_PAGE_B0 = 24576
 AT_TAB_S = 6144
 AT_WG1_LATE = 6144
 AT_PAGE_A1 = 125248
+AT_W1_S_LATE = 133440
 AT_PAGE_B1 = 16384
 AT_W2_RAW = (8224, 41024)
 AT_TAB_W = 32768
@@ -74,7 +75,8 @@ def tile_list_cherry_pollination_scores_kernel(
         tab_w = shared.tile([P, T], I32, name="tab_w", offset=AT_TAB_W)
         tab_s = shared.tile([P, T], U8, name="tab_s", offset=AT_TAB_S)
         w1_w = keep.tile([P, 2 * H], U8, name="w1_w", align_bytes=64)
-        w1_s = keep.tile([P, H], U8, name="w1_s", align_bytes=64)
+        planes = keep.tile([P, BANK + K], U8, name="planes", align_bytes=64)
+        w1_s = planes[:, BANK : BANK + K]
         wg1_sb = [
             shared.tile([P, BANK], F32, name="wg1_early", offset=AT_WG1),
             shared.tile([P, BANK], F32, name="wg1_late", offset=AT_WG1_LATE),
@@ -82,38 +84,43 @@ def tile_list_cherry_pollination_scores_kernel(
         ident = keep.tile([P, P], F32, name="ident")
         page_a = [keep.tile([P, T2], F32, name="page_a0")]
         v_w = keep.tile([P, S], U32, name="v_w", align_bytes=64)
-        picked_s = [keep.tile([P, BANK], U8, name="picked_s%d" % h, align_bytes=64) for h in range(2)]
-        v_s = [keep.tile([P, BANK], U8, name="v_s%d" % h, align_bytes=64) for h in range(2)]
+        picked_s = [
+            keep.tile([P, BANK], U8, name="picked_early", align_bytes=64),
+            shared.tile([P, BANK], U8, name="picked_late", offset=AT_W1_S_LATE, align_bytes=64),
+        ]
+        v_s_late = keep.tile([P, BANK], U8, name="v_s_late", align_bytes=64)
+        v_s = [planes[:, 0:BANK], v_s_late[:]]
         w2_c = keep.tile([P, H], U32, name="w2_c", align_bytes=64)
         w2_s = keep.tile([P, H], U8, name="w2_s", align_bytes=64)
 
         nc.vector.memset(tab_s[:].bitcast(I32), 0)
-        nc.gpsimd.memset(w1_s[:].bitcast(I32), 0)
+        nc.gpsimd.memset(w1_s.bitcast(I32), 0)
         nc.sync.dma_start(list1[:], offs)
         table = tab_words[0].rearrange("p t i -> p (t i)").bitcast(I32)
         nc.sync.dma_start(tab_w[:, 0:EARLY], table[:, 0:EARLY])
+        nc.sync.dma_start(w1_s.bitcast(I32)[0:P:8, :], w1_scales[0, :, 0:K].bitcast(I32))
         nc.sync.dma_start(list2[:], offs2)
         nc.sync.dma_start(list3[:], offs3)
         nc.sync.dma_start(tab_s[:].bitcast(I32)[0:P:8, :], tab_scales[0].bitcast(I32))
         nc.sync.dma_start(tab_w[:, EARLY:T], table[:, EARLY:T])
         nc.sync.dma_start(w1_w[:].bitcast(I32), w1_words[0].bitcast(I32))
-        for q in range(4):
-            nc.gpsimd.dma_start(
-                w1_s[:].bitcast(I32)[32 * q : 32 * q + 4, :], w1_scales[0, 4 * q : 4 * q + 4, :].bitcast(I32)
-            )
-        make_identity(nc, ident[:])
         nc.sync.dma_start(wg1_sb[0][:], wg1[:, chunk(0)])
         nc.vector.memset(page_a[0][:, 0 : T2 // 2 - 1], 0.0)
         nc.vector.memset(page_a[0][:, T2 // 2 - 1 : T2], 0.0)
 
         for h in range(2):
             nc.vector.tensor_copy(picked_s[h][:], tab_s[:].indirect(list1[:, 32 * h : 32 * (h + 1)]))
-            nc.vector.tensor_copy(v_s[h][:].bitcast(I32), picked_s[h][:].bitcast(I32))
+            nc.vector.tensor_copy(v_s[h].bitcast(I32), picked_s[h][:].bitcast(I32))
+            rows = (planes, v_s_late)[h][:].bitcast(I32)
             for r in range(1, 4):
-                (nc.scalar, nc.sync)[h].dma_start(
-                    v_s[h][:].bitcast(I32)[r:P:32, :], picked_s[h][:].bitcast(I32)[8 * r : P : 32, :]
-                )
+                (nc.scalar, nc.sync)[h].dma_start(rows[r:P:32, :], rows[8 * r : P : 32, :])
         nc.sync.dma_start(wg1_sb[1][:], wg1[:, chunk(1)])
+        w1_s_late = shared.tile([P, K], U8, name="w1_s_late", offset=AT_W1_S_LATE, align_bytes=64)
+        nc.gpsimd.memset(w1_s_late[:].bitcast(I32), 0)
+        for q in range(4):
+            nc.sync.dma_start(
+                w1_s_late[:].bitcast(I32)[32 * q : 32 * q + 4, :], w1_scales[0, 4 * q : 4 * q + 4, K:H].bitcast(I32)
+            )
         for lo, hi in ((0, FIRST), (FIRST, S)):
             nc.vector.tensor_copy(v_w[:, lo:hi], tab_w[:].bitcast(U32).indirect(list1[:, lo // 16 : hi // 16]))
 
@@ -121,6 +128,7 @@ def tile_list_cherry_pollination_scores_kernel(
         nc.gpsimd.memset(page_a[1][:], 0.0)
         page_b = [shared.tile([P, T2], F32, name="page_b0", offset=AT_PAGE_B0)]
         nc.gpsimd.memset(page_b[0][:], 0.0)
+        make_identity(nc, ident[:])
         w2_raw = [shared.tile([P, 4, BANK], F32, name="w2_raw%d" % h, offset=AT_W2_RAW[h]) for h in range(2)]
         for h in range(2):
             nc.sync.dma_start(w2_raw[h][:], w2[:, chunk(h)].rearrange("(p j) w -> p j w", j=4))
@@ -171,7 +179,7 @@ def tile_list_cherry_pollination_scores_kernel(
             words = shared.tile([P, P, 2], U8, name="w1_dealt_w%d" % s, offset=AT_W1_DEALT[s], align_bytes=64)
             scales = shared.tile([P, P], U8, name="w1_dealt_s%d" % s, offset=AT_W1_DEALT[s] + 2 * P, align_bytes=64)
             src_w = w1_w[:, H : 2 * H].rearrange("p (q t b) -> p t q b", t=4, b=2)
-            src_s = w1_s[:, K:H].rearrange("p (q t) -> p t q", t=4)
+            src_s = w1_s_late[:].rearrange("p (q t) -> p t q", t=4)
             nc.gpsimd.tensor_copy(words[:], src_w[:, DEALT[s], :, :])
             nc.gpsimd.tensor_copy(scales[:], src_s[:, DEALT[s], :])
             w1_dealt[s] = (words[:].rearrange("p q b -> p (q b)").bitcast(FP4X4), scales[:])
@@ -194,7 +202,7 @@ def tile_list_cherry_pollination_scores_kernel(
                 acc = bank("s%d" % h)
                 nc.tensor.matmul_mx(
                     out=acc[:], lhsT=codes, lhsT_scale=scales, rhs=v_w[:, chunk(h)].bitcast(FP8X4),
-                    rhs_scale=v_s[h][:], start=True, stop=True,
+                    rhs_scale=v_s[h], start=True, stop=True,
                 )
                 if kind == "a":
                     nc.scalar.copy(made[:, chunk(h)], acc[:])

@@ -25,11 +25,13 @@ SLICES = H // P
 CHUNKS = T2 // BANK
 NT = N // P
 FIRST = 256
-EARLY = 768
+EARLY = 512
+ROWS_AT = P - 16
 DEALT = {4: 2, 5: 0, 6: 1, 7: 3}
 AT_PAGE_B0 = 24576
-AT_TAB_S = 6144
-AT_WG1_LATE = 6144
+AT_TAB_S = 4608
+AT_W1_W_LATE = 3136
+AT_WG1_LATE = 5120
 AT_PAGE_A1 = 125248
 AT_W1_S_LATE = 133440
 AT_PAGE_B1 = 16384
@@ -39,6 +41,7 @@ AT_WG2 = 32768
 AT_ROWS = (36928, 45120)
 AT_Z_K = (53312, 117056)
 AT_W2_BF = 61440
+AT_W3_RAW = AT_W2_BF + 32 - 6144
 AT_WEATHER = (8192, 67136)
 AT_LAST_WEATHER = 76096
 AT_PAIRS = 87616
@@ -74,18 +77,19 @@ def tile_list_cherry_pollination_scores_kernel(
         list3 = keep.tile([P, S // 16], U16, name="list3")
         tab_w = shared.tile([P, T], I32, name="tab_w", offset=AT_TAB_W)
         tab_s = shared.tile([P, T], U8, name="tab_s", offset=AT_TAB_S)
-        w1_w = keep.tile([P, 2 * H], U8, name="w1_w", align_bytes=64)
+        w1_early = keep.tile([P, 4 * P], U8, name="w1_early", align_bytes=64)
+        w1_late = shared.tile([P, 2 * H - 4 * P], U8, name="w1_late", offset=AT_W1_W_LATE, align_bytes=64)
         planes = keep.tile([P, BANK + K], U8, name="planes", align_bytes=64)
         w1_s = planes[:, BANK : BANK + K]
         wg1_sb = [
-            shared.tile([P, BANK], F32, name="wg1_early", offset=AT_WG1),
-            shared.tile([P, BANK], F32, name="wg1_late", offset=AT_WG1_LATE),
+            shared.tile([P, FIRST], F32, name="wg1_early", offset=AT_WG1),
+            shared.tile([P, S - FIRST], F32, name="wg1_late", offset=AT_WG1_LATE),
         ]
         ident = keep.tile([P, P], F32, name="ident")
         page_a = [keep.tile([P, T2], F32, name="page_a0")]
         v_w = keep.tile([P, S], U32, name="v_w", align_bytes=64)
         picked_s = [
-            keep.tile([P, BANK], U8, name="picked_early", align_bytes=64),
+            shared.tile([P, BANK], U8, name="picked_early", offset=AT_W1_S_LATE, align_bytes=64),
             shared.tile([P, BANK], U8, name="picked_late", offset=AT_W1_S_LATE, align_bytes=64),
         ]
         v_s_late = keep.tile([P, BANK], U8, name="v_s_late", align_bytes=64)
@@ -93,28 +97,29 @@ def tile_list_cherry_pollination_scores_kernel(
         w2_c = keep.tile([P, H], U32, name="w2_c", align_bytes=64)
         w2_s = keep.tile([P, H], U8, name="w2_s", align_bytes=64)
 
-        nc.vector.memset(tab_s[:].bitcast(I32), 0)
-        nc.gpsimd.memset(w1_s.bitcast(I32), 0)
-        nc.sync.dma_start(list1[:], offs)
+        nc.vector.memset(tab_s[:].bitcast(I32)[0:ROWS_AT, :], 0)
+        nc.gpsimd.memset(w1_s.bitcast(I32)[0:ROWS_AT, :], 0)
         table = tab_words[0].rearrange("p t i -> p (t i)").bitcast(I32)
         nc.sync.dma_start(tab_w[:, 0:EARLY], table[:, 0:EARLY])
-        nc.sync.dma_start(w1_s.bitcast(I32)[0:P:8, :], w1_scales[0, :, 0:K].bitcast(I32))
+        nc.sync.dma_start(tab_s[:].bitcast(I32)[ROWS_AT:P, :], tab_scales[0].bitcast(I32))
+        nc.sync.dma_start(list1[:], offs)
+        nc.sync.dma_start(w1_s.bitcast(I32)[ROWS_AT:P, :], w1_scales[0, :, 0:K].bitcast(I32))
         nc.sync.dma_start(list2[:], offs2)
-        nc.sync.dma_start(list3[:], offs3)
-        nc.sync.dma_start(tab_s[:].bitcast(I32)[0:P:8, :], tab_scales[0].bitcast(I32))
         nc.sync.dma_start(tab_w[:, EARLY:T], table[:, EARLY:T])
-        nc.sync.dma_start(w1_w[:].bitcast(I32), w1_words[0].bitcast(I32))
-        nc.sync.dma_start(wg1_sb[0][:], wg1[:, chunk(0)])
-        nc.vector.memset(page_a[0][:, 0 : T2 // 2 - 1], 0.0)
-        nc.vector.memset(page_a[0][:, T2 // 2 - 1 : T2], 0.0)
+        nc.sync.dma_start(list3[:], offs3)
+        nc.sync.dma_start(w1_early[:].bitcast(I32), w1_words[0, :, 0 : 4 * P].bitcast(I32))
+        nc.sync.dma_start(wg1_sb[0][:], wg1[:, 0:FIRST])
+        nc.vector.memset(page_a[0][:, 0 : T2 // 2], 0.0)
+        nc.gpsimd.memset(page_a[0][:, T2 // 2 : T2], 0.0)
 
         for h in range(2):
             nc.vector.tensor_copy(picked_s[h][:], tab_s[:].indirect(list1[:, 32 * h : 32 * (h + 1)]))
             nc.vector.tensor_copy(v_s[h].bitcast(I32), picked_s[h][:].bitcast(I32))
             rows = (planes, v_s_late)[h][:].bitcast(I32)
-            for r in range(1, 4):
-                (nc.scalar, nc.sync)[h].dma_start(rows[r:P:32, :], rows[8 * r : P : 32, :])
-        nc.sync.dma_start(wg1_sb[1][:], wg1[:, chunk(1)])
+            for r in range(4):
+                (nc.scalar, nc.sync)[h].dma_start(rows[r:P:32, :], rows[ROWS_AT + r : P : 4, :])
+        nc.sync.dma_start(wg1_sb[1][:], wg1[:, FIRST:S])
+        nc.sync.dma_start(w1_late[:].bitcast(I32), w1_words[0, :, 4 * P : 2 * H].bitcast(I32))
         w1_s_late = shared.tile([P, K], U8, name="w1_s_late", offset=AT_W1_S_LATE, align_bytes=64)
         nc.gpsimd.memset(w1_s_late[:].bitcast(I32), 0)
         for q in range(4):
@@ -160,7 +165,7 @@ def tile_list_cherry_pollination_scores_kernel(
         def cast_w3():
             rounded = shared.tile([P, 2 * N * 4], BF16, name="w3_bf", offset=AT_PAIRS, align_bytes=64)
             for b in range(2):
-                w3_raw = shared.tile([P, 4, N], F32, name="w3_raw%d" % b, offset=AT_Z_K[0])
+                w3_raw = shared.tile([P, 4, N], F32, name="w3_raw%d" % b, offset=AT_W3_RAW)
                 nc.sync.dma_start(w3_raw[:], w3[b * K : (b + 1) * K, :].rearrange("(p j) w -> p j w", j=4))
                 interleave(rounded[:, b * 4 * N : (b + 1) * 4 * N], w3_raw[:])
             w3_bf.append(rounded)
@@ -178,7 +183,7 @@ def tile_list_cherry_pollination_scores_kernel(
         def deal_w1(s):
             words = shared.tile([P, P, 2], U8, name="w1_dealt_w%d" % s, offset=AT_W1_DEALT[s], align_bytes=64)
             scales = shared.tile([P, P], U8, name="w1_dealt_s%d" % s, offset=AT_W1_DEALT[s] + 2 * P, align_bytes=64)
-            src_w = w1_w[:, H : 2 * H].rearrange("p (q t b) -> p t q b", t=4, b=2)
+            src_w = w1_late[:, H - 4 * P : 2 * H - 4 * P].rearrange("p (q t b) -> p t q b", t=4, b=2)
             src_s = w1_s_late[:].rearrange("p (q t) -> p t q", t=4)
             nc.gpsimd.tensor_copy(words[:], src_w[:, DEALT[s], :, :])
             nc.gpsimd.tensor_copy(scales[:], src_s[:, DEALT[s], :])
@@ -195,7 +200,7 @@ def tile_list_cherry_pollination_scores_kernel(
             if kind == "b":
                 codes, scales = w2_c[:, P * j : P * (j + 1)].bitcast(FP8X4), w2_s[:, P * j : P * (j + 1)]
             elif s < 4:
-                codes, scales = w1_w[:, 2 * P * j : 2 * P * (j + 1)].bitcast(FP4X4), w1_s[:, P * j : P * (j + 1)]
+                codes, scales = w1_late[:, 2 * P * (j - 2) : 2 * P * (j - 1)].bitcast(FP4X4), w1_s[:, P * j : P * (j + 1)]
             else:
                 codes, scales = w1_dealt[s]
             for h in range(2):
@@ -238,8 +243,8 @@ def tile_list_cherry_pollination_scores_kernel(
                 nc.gpsimd.tensor_tensor(placed[kind, s][:], src[:], h2[s][:], MULT)
                 return
             if kind == "a" and s < 4:
-                for h in range(2):
-                    nc.gpsimd.tensor_tensor(placed[kind, s][:, chunk(h)], src[:, chunk(h)], wg1_sb[h][:], MULT)
+                for cols, part in ((slice(0, FIRST), wg1_sb[0]), (slice(FIRST, S), wg1_sb[1])):
+                    nc.gpsimd.tensor_tensor(placed[kind, s][:, cols], src[:, cols], part[:], MULT)
                 return
             for cols in halves:
                 if kind == "b":
@@ -401,14 +406,13 @@ def tile_list_cherry_pollination_scores_kernel(
             h, at = lo // BANK, lo % BANK
             acc = bank(tag)
             nc.tensor.matmul_mx(
-                out=acc[:, 0 : hi - lo], lhsT=w1_w[:, 2 * P * s : 2 * P * (s + 1)].bitcast(FP4X4),
+                out=acc[:, 0 : hi - lo], lhsT=w1_early[:, 2 * P * s : 2 * P * (s + 1)].bitcast(FP4X4),
                 lhsT_scale=w1_s[:, P * s : P * (s + 1)], rhs=v_w[:, lo:hi].bitcast(FP8X4),
                 rhs_scale=v_s[h][:, at : at + hi - lo], start=True, stop=True,
             )
             nc.scalar.copy(pollen[s][:, lo:hi], acc[:, 0 : hi - lo])
-            nc.gpsimd.tensor_tensor(
-                placed["a", s][:, lo:hi], pollen[s][:, lo:hi], wg1_sb[h][:, at : at + hi - lo], MULT
-            )
+            wg = wg1_sb[0][:] if lo == 0 else wg1_sb[1][:, lo - FIRST : hi - FIRST]
+            nc.gpsimd.tensor_tensor(placed["a", s][:, lo:hi], pollen[s][:, lo:hi], wg, MULT)
 
         for s in range(2):
             early_values(s, 0, FIRST, "s%d" % s)

@@ -45,6 +45,7 @@ AT_W3_RAW = AT_W2_BF + 32 - 6144
 AT_WEATHER = (8192, 67136)
 AT_LAST_WEATHER = 76096
 AT_PAIRS = 87616
+AT_LATE_CODES = 134144
 AT_WG1 = 104000
 AT_W3_CODES = (61504, AT_WG1)
 AT_Z_CODES = (108480, 112960)
@@ -163,7 +164,7 @@ def tile_list_cherry_pollination_scores_kernel(
         w3_blocks = []
 
         def cast_w3():
-            rounded = shared.tile([P, 2 * N * 4], BF16, name="w3_bf", offset=AT_PAIRS, align_bytes=64)
+            rounded = shared.tile([P, 2 * N * 4], BF16, name="w3_bf", offset=AT_LATE_CODES + 12032, align_bytes=64)
             for b in range(2):
                 w3_raw = shared.tile([P, 4, N], F32, name="w3_raw%d" % b, offset=AT_W3_RAW)
                 nc.sync.dma_start(w3_raw[:], w3[b * K : (b + 1) * K, :].rearrange("(p j) w -> p j w", j=4))
@@ -172,8 +173,8 @@ def tile_list_cherry_pollination_scores_kernel(
 
         def quantize_w3(i):
             lo, hi = ((0, 512), (512, 768))[i]
-            codes = shared.tile([P, hi - lo], U32, name="w3_c%d" % i, offset=AT_W3_CODES[i], align_bytes=64)
-            scales = shared.tile([P, hi - lo], U8, name="w3_s%d" % i, offset=AT_W3_CODES[i] + 2048, align_bytes=64)
+            codes = shared.tile([P, hi - lo], U32, name="w3_c%d" % i, offset=AT_LATE_CODES + 4096 + 4 * lo, align_bytes=64)
+            scales = shared.tile([P, hi - lo], U8, name="w3_s%d" % i, offset=AT_LATE_CODES + 11264 + lo, align_bytes=64)
             nc.vector.quantize_mx(out=codes[:].bitcast(FP8X4), scales=scales[:], in_=w3_bf[0][:, 4 * lo : 4 * hi])
             for j in range((hi - lo) // P):
                 w3_blocks.append((codes[:, P * j : P * (j + 1)], scales[:, P * j : P * (j + 1)]))
@@ -230,6 +231,8 @@ def tile_list_cherry_pollination_scores_kernel(
             halves = [slice(0, S)]
             if (kind, s) == ("a", SLICES - 1):
                 placed[kind, s] = shared.tile([P, S], F32, name="placed_last", offset=AT_Z_CODES[1])
+            elif (kind, s) == ("b", 6):
+                placed[kind, s] = shared.tile([P, S], F32, name="placed_b6", offset=AT_LATE_CODES + 4096 - 512)
             else:
                 placed[kind, s] = work.tile([P, S], F32, name="placed", tag="placed", bufs=3)
             src = pollen[s]
@@ -338,7 +341,7 @@ def tile_list_cherry_pollination_scores_kernel(
 
         def quantize_z(z_k, chunks, i):
             if chunks == 2:
-                z_c = shared.tile([P, 2 * BANK], U32, name="z_first%d" % i, offset=AT_Z_CODES[i], align_bytes=64)
+                z_c = shared.tile([P, 2 * BANK], U32, name="z_first%d" % i, offset=(AT_LATE_CODES, AT_Z_CODES[1])[i], align_bytes=64)
             else:
                 z_c = work.tile([P, BANK], U32, name="z_c", tag="z_c", bufs=4, align_bytes=64)
             z_s = work.tile([P, chunks * BANK], U8, name="z_s", tag="z_s%d" % chunks, bufs=4 // chunks, align_bytes=64)
@@ -438,11 +441,11 @@ def tile_list_cherry_pollination_scores_kernel(
         cast_w3()
         pairs = [shared.tile([P, 2, BANK], F32, name="pairs%d" % c, offset=AT_PAIRS + 4096 * c) for c in range(CHUNKS)]
         for n in range(2, len(order) - 1):
-            if order[n] in (("a", 4), ("a", 5)):
-                quantize_w3(order[n][1] - 4)
-            if order[n] == ("a", 6):
-                z_first.extend(quantize_z(z_turned[0], 2, 0))
             scatter(*order[n])
+            if order[n] == ("b", 6):
+                for i in range(2):
+                    quantize_w3(i)
+                z_first.extend(quantize_z(z_turned[0], 2, 0))
             if n + 3 < len(order):
                 weigh(*order[n + 3])
                 if order[n + 3][0] == "a" and order[n + 3][1] < SLICES - 1:

@@ -35,7 +35,7 @@ AT_WG1_LATE = 5120
 AT_PAGE_A1 = 125248
 AT_W1_S_LATE = 133440
 AT_PAGE_B1 = 16384
-AT_W2_RAW = (8224, 41024)
+AT_W2_RAW = (8192, 41024)
 AT_TAB_W = 32768
 AT_WG2 = 32768
 AT_ROWS = (36928, 45120)

@@ -28,23 +28,28 @@ FIRST = 256
 EARLY = 512
 ROWS_AT = P - 16
 DEALT = {4: 2, 5: 0, 6: 1, 7: 3}
-AT_PAGE_B0 = 24576
+AT_PAGE_B0 = 16384
 AT_TAB_S = 4608
 AT_W1_W_LATE = 3136
 AT_WG1_LATE = 5120
 AT_PAGE_A1 = 125248
 AT_W1_S_LATE = 133440
-AT_PAGE_B1 = 16384
-AT_W2_RAW = (8192, 41024)
-AT_TAB_W = 32768
+AT_PAGE_B1 = 67136
+AT_W2_RAW = (8224, 41024)
+AT_TAB_W = 32736
 AT_WG2 = 32768
 AT_ROWS = (36928, 45120)
 AT_Z_K = (53312, 117056)
 AT_W2_BF = 61440
 AT_W3_RAW = AT_W2_BF + 32 - 6144
-AT_WEATHER = (8192, 67136)
+AT_WEATHER = (8192, 24576)
+AT_IDENT = 65600
 AT_LAST_WEATHER = 76096
 AT_PAIRS = 87616
+PIECES = ((0, 256), (256, 512), (512, 1024), (1024, 1536), (1536, 1792), (1792, 2048))
+OUT_BANKS = (("s0", "s1"), ("x0", "x1"), ("z0", "z1", "z2"), ("z3", "s0", "s1"), ("x0", "x1"), ("z0", "z1"))
+AT_WOVEN = (AT_ROWS[1], AT_ROWS[1] + 2048, AT_ROWS[1] + 4096, AT_Z_K[0], AT_Z_K[0] + 4096, AT_Z_K[0] + 6144)
+AT_RESULTS = (AT_ROWS[0], AT_PAGE_B0, AT_WEATHER[0], AT_WG2)
 AT_LATE_CODES = 134144
 AT_WG1 = 104000
 AT_W3_CODES = (61504, AT_WG1)
@@ -86,7 +91,6 @@ def tile_list_cherry_pollination_scores_kernel(
             shared.tile([P, FIRST], F32, name="wg1_early", offset=AT_WG1),
             shared.tile([P, S - FIRST], F32, name="wg1_late", offset=AT_WG1_LATE),
         ]
-        ident = keep.tile([P, P], F32, name="ident")
         page_a = [keep.tile([P, T2], F32, name="page_a0")]
         v_w = keep.tile([P, S], U32, name="v_w", align_bytes=64)
         picked_s = [
@@ -132,9 +136,6 @@ def tile_list_cherry_pollination_scores_kernel(
 
         page_a.append(shared.tile([P, T2], F32, name="page_a1", offset=AT_PAGE_A1))
         nc.gpsimd.memset(page_a[1][:], 0.0)
-        page_b = [shared.tile([P, T2], F32, name="page_b0", offset=AT_PAGE_B0)]
-        nc.gpsimd.memset(page_b[0][:], 0.0)
-        make_identity(nc, ident[:])
         w2_raw = [shared.tile([P, 4, BANK], F32, name="w2_raw%d" % h, offset=AT_W2_RAW[h]) for h in range(2)]
         for h in range(2):
             nc.sync.dma_start(w2_raw[h][:], w2[:, chunk(h)].rearrange("(p j) w -> p j w", j=4))
@@ -284,15 +285,6 @@ def tile_list_cherry_pollination_scores_kernel(
             t = DEALT[s]
             return pairs[c][:, t // 2, :].bitcast(BF16).rearrange("p (m e) -> p m e", e=2)[:, :, t % 2]
 
-        def finish_last(s, c):
-            if c == 0:
-                scaled[s] = work.tile([P, T2], F32, name="last_gelu", tag="z_rows3", bufs=1)
-            j = 8 + DEALT[s]
-            nc.scalar.activation(scaled[s][:, chunk(c)], page_a[s % 2][:, chunk(c)], GELU)
-            nc.vector.scalar_tensor_tensor(
-                pair_half(s, c), scaled[s][:, chunk(c)], gain_sb[:, j : j + 1], weather_sb[s][:, chunk(c)], MULT, ADD
-            )
-
         def add_term(acc, src, c, start, stop):
             for mb in range(4):
                 cols = slice(BANK * c + P * mb, BANK * c + P * (mb + 1))
@@ -378,7 +370,7 @@ def tile_list_cherry_pollination_scores_kernel(
                 close_sum(s, c)
                 if s == 6:
                     words = z_rows[c][:].rearrange("m x e -> m (x e)").bitcast(F32)
-                    acc = turn_back(words, "x%d" % (c % 2))
+                    acc = turn_back(words, ("s0", "s1", "x0", "x1")[c])
                     nc.scalar.copy(pairs[c][:, 0, :], acc[:])
             if s == 3:
                 finish_first_pass()
@@ -429,8 +421,12 @@ def tile_list_cherry_pollination_scores_kernel(
         load_weather(1)
         first_products("a", 2)
         weigh("a", 2)
-        page_b.append(shared.tile([P, T2], F32, name="page_b1", offset=AT_PAGE_B1))
-        nc.gpsimd.memset(page_b[1][:], 0.0)
+        page_b = []
+        for i in range(2):
+            page_b.append(shared.tile([P, T2], F32, name="page_b%d" % i, offset=(AT_PAGE_B0, AT_PAGE_B1)[i]))
+            nc.gpsimd.memset(page_b[i][:], 0.0)
+        ident = shared.tile([P, P], F32, name="ident", offset=AT_IDENT)
+        make_identity(nc, ident[:])
         ahead(3)
         ahead(4)
         weigh(*order[3])
@@ -454,20 +450,33 @@ def tile_list_cherry_pollination_scores_kernel(
             after(*order[n])
         last = SLICES - 1
         scatter("a", last)
-        z_first.extend(quantize_z(z_turned[1], 2, 1))
 
-        out_tags = (("s0", "s1", "z0"), ("z1", "z2", "z3"), ("x0", "x1", "s0"), ("s1", "z0", "z1"))
-        outs = {}
+        gelu_last = {}
+        outs, woven, z_last = {}, {}, {}
 
-        def last_product(c, b, z):
-            for a in range(NT):
-                if b == 0:
-                    outs[c, a] = bank(out_tags[c][a])
-                codes, scales = w3_blocks[NT * b + a]
-                nc.tensor.matmul_mx(
-                    out=outs[c, a][:], lhsT=codes.bitcast(FP8X4), lhsT_scale=scales,
-                    rhs=z[0].bitcast(FP8X4), rhs_scale=z[1], start=(b == 0), stop=(b == 1),
-                )
+        def columns(i):
+            return slice(*PIECES[i])
+
+        def in_chunk(i):
+            lo, hi = PIECES[i]
+            return lo // BANK, slice(lo % BANK, lo % BANK + hi - lo)
+
+        def gelu(i):
+            lo, hi = PIECES[i]
+            if i == 0:
+                gelu_last["early"] = work.tile([P, 2 * BANK], F32, name="last_gelu", tag="z_rows3", bufs=1)
+            if i < 3:
+                gelu_last[i] = gelu_last["early"][:, lo:hi]
+            else:
+                late = shared.tile([P, hi - lo], F32, name="last_gelu%d" % i, offset=AT_PAIRS + 4 * (lo - 2 * BANK))
+                gelu_last[i] = late[:]
+            nc.scalar.activation(gelu_last[i], page_a[last % 2][:, columns(i)], GELU)
+
+        def finish(i):
+            c, cols = in_chunk(i)
+            nc.vector.scalar_tensor_tensor(
+                pair_half(last, c)[:, cols], gelu_last[i], gain_sb[:, 11:12], weather_sb[last][:, columns(i)], MULT, ADD
+            )
 
         def copy_on(engine, dst, src):
             if engine == "vector":
@@ -475,31 +484,92 @@ def tile_list_cherry_pollination_scores_kernel(
             else:
                 nc.scalar.copy(dst, src)
 
-        def weave(c, engine):
-            z_k = new_z_k(1, c)
-            copy_on(engine, z_k[:].bitcast(F32).rearrange("p (m u) -> p m u", u=2), pairs[c][:].rearrange("p u m -> p m u"))
-            return z_k
+        def weave(i, engine):
+            lo, hi = PIECES[i]
+            c, cols = in_chunk(i)
+            woven[i] = shared.tile([P, 4 * (hi - lo)], BF16, name="woven%d" % i, offset=AT_WOVEN[i], align_bytes=64)
+            copy_on(engine, woven[i][:].bitcast(F32).rearrange("p (m u) -> p m u", u=2), pairs[c][:, :, cols].rearrange("p u m -> p m u"))
 
-        def leave(c):
-            for a in range(NT):
-                i = NT * c + a
-                at = AT_ROWS[0] + 2048 * i if i < 8 else AT_PAGE_B0 + 2048 * (i - 8)
-                result = shared.tile([P, BANK], F32, name="result%d" % i, offset=at)
-                copy_on("vector" if (c, a) in ((2, 2), (3, 0), (3, 2)) else "scalar", result[:], outs[c, a][:])
-                nc.sync.dma_start(out[P * a : P * (a + 1), chunk(c)], result[:])
+        def quantize_last(i):
+            lo, hi = PIECES[i]
+            codes = shared.tile([P, hi - lo], U32, name="last_c%d" % i, offset=AT_Z_CODES[0] + 4 * lo, align_bytes=64)
+            scales = keep.tile([P, hi - lo], U8, name="last_s%d" % i, align_bytes=64)
+            nc.vector.quantize_mx(out=codes[:].bitcast(FP8X4), scales=scales[:], in_=woven[i][:])
+            z_last[i] = (codes[:], scales[:])
 
-        for c in range(2):
-            last_product(c, 0, z_first[c])
-        z_k = {}
-        for c in range(2):
-            finish_last(last, c)
-            z_k[c] = weave(c, ("vector", "scalar")[c])
-        for c in range(CHUNKS):
-            z = quantize_z(z_k[c], 1, c)[0]
-            if c + 2 < CHUNKS:
-                finish_last(last, c + 2)
-                z_k[c + 2] = weave(c + 2, ("scalar", "vector")[c])
-            if c >= 2:
-                last_product(c, 0, z_first[c])
-            last_product(c, 1, z)
-            leave(c)
+        def groups(i):
+            lo, hi = PIECES[i]
+            per = BANK // (hi - lo)
+            return [range(a, min(a + per, NT)) for a in range(0, NT, per)]
+
+        def last_product(i, b):
+            lo, hi = PIECES[i]
+            c, cols = in_chunk(i)
+            z = (z_first[c][0][:, cols], z_first[c][1][:, cols]) if b == 0 else z_last[i]
+            for g, blocks in enumerate(groups(i)):
+                if b == 0:
+                    outs[i, g] = bank(OUT_BANKS[i][g])
+                for j, a in enumerate(blocks):
+                    codes, scales = w3_blocks[NT * b + a]
+                    nc.tensor.matmul_mx(
+                        out=outs[i, g][:, j * (hi - lo) : (j + 1) * (hi - lo)], lhsT=codes.bitcast(FP8X4), lhsT_scale=scales,
+                        rhs=z[0].bitcast(FP8X4), rhs_scale=z[1],
+                        start=(b == 0 and j == 0), stop=(b == 1 and j == len(blocks) - 1),
+                    )
+
+        def quantize_first(c):
+            codes = shared.tile([P, BANK], U32, name="z_first%d" % c, offset=AT_PAIRS + 4096 * (c - 1), align_bytes=64)
+            scales = keep.tile([P, BANK], U8, name="z_first_s%d" % c, align_bytes=64)
+            nc.vector.quantize_mx(
+                out=codes[:].bitcast(FP8X4), scales=scales[:], in_=z_turned[1][:, 4 * BANK * (c - 2) : 4 * BANK * (c - 1)]
+            )
+            z_first.append((codes[:], scales[:]))
+
+        stored = []
+
+        def leave(i, engines):
+            lo, hi = PIECES[i]
+            for g, blocks in enumerate(groups(i)):
+                n = len(stored)
+                result = shared.tile([P, len(blocks), hi - lo], F32, name="result%d" % n, offset=AT_RESULTS[n // 4] + 2048 * (n % 4))
+                stored.append(result)
+                copy_on(engines[g], result[:].rearrange("p a m -> p (a m)"), outs[i, g][:, 0 : len(blocks) * (hi - lo)])
+                rows = out[P * blocks[0] : P * (blocks[-1] + 1), columns(i)]
+                nc.sync.dma_start(rows.rearrange("(a p) m -> p a m", p=P), result[:])
+
+        for i in range(3):
+            last_product(i, 0)
+        for i in range(3):
+            gelu(i)
+            finish(i)
+        weave(0, "scalar")
+        weave(1, "scalar")
+        for i in range(3, 6):
+            gelu(i)
+        quantize_last(0)
+        weave(2, "vector")
+        quantize_last(1)
+        quantize_last(2)
+        for i in range(3):
+            last_product(i, 1)
+            leave(i, ("scalar",) * 3)
+        finish(3)
+        quantize_first(2)
+        last_product(3, 0)
+        weave(3, "vector")
+        finish(4)
+        quantize_last(3)
+        finish(5)
+        weave(4, "scalar")
+        quantize_first(3)
+        weave(5, "vector")
+        last_product(3, 1)
+        last_product(4, 0)
+        last_product(5, 0)
+        quantize_last(4)
+        quantize_last(5)
+        leave(3, ("scalar",) * 3)
+        last_product(4, 1)
+        last_product(5, 1)
+        leave(4, ("vector", "vector"))
+        leave(5, ("scalar", "vector"))

@@ -114,8 +114,9 @@ def tile_list_cherry_pollination_scores_kernel(
         nc.sync.dma_start(list3[:], offs3)
         nc.sync.dma_start(w1_early[:].bitcast(I32), w1_words[0, :, 0 : 4 * P].bitcast(I32))
         nc.sync.dma_start(wg1_sb[0][:], wg1[:, 0:FIRST])
-        nc.vector.memset(page_a[0][:, 0 : T2 // 2], 0.0)
-        nc.gpsimd.memset(page_a[0][:, T2 // 2 : T2], 0.0)
+        page_a.append(shared.tile([P, T2], F32, name="page_a1", offset=AT_PAGE_A1))
+        for page in page_a:
+            nc.vector.memset(page[:], 0.0)
 
         for h in range(2):
             nc.vector.tensor_copy(picked_s[h][:], tab_s[:].indirect(list1[:, 32 * h : 32 * (h + 1)]))
@@ -134,8 +135,6 @@ def tile_list_cherry_pollination_scores_kernel(
         for lo, hi in ((0, FIRST), (FIRST, S)):
             nc.vector.tensor_copy(v_w[:, lo:hi], tab_w[:].bitcast(U32).indirect(list1[:, lo // 16 : hi // 16]))
 
-        page_a.append(shared.tile([P, T2], F32, name="page_a1", offset=AT_PAGE_A1))
-        nc.gpsimd.memset(page_a[1][:], 0.0)
         w2_raw = [shared.tile([P, 4, BANK], F32, name="w2_raw%d" % h, offset=AT_W2_RAW[h]) for h in range(2)]
         for h in range(2):
             nc.sync.dma_start(w2_raw[h][:], w2[:, chunk(h)].rearrange("(p j) w -> p j w", j=4))

@@ -25,15 +25,16 @@ SLICES = H // P
 CHUNKS = T2 // BANK
 NT = N // P
 FIRST = 256
-EARLY = 512
+EARLY = 1024
 ROWS_AT = P - 16
 DEALT = {4: 2, 5: 0, 6: 1, 7: 3}
 AT_PAGE_B0 = 16384
 AT_TAB_S = 4608
 AT_W1_W_LATE = 3136
 AT_WG1_LATE = 5120
-AT_PAGE_A1 = 125248
-AT_W1_S_LATE = 133440
+AT_PAGE_A1 = 125280
+AT_PICKED = 133440
+AT_W1_S_LATE = AT_PICKED + 64
 AT_PAGE_B1 = 67136
 AT_W2_RAW = (8224, 41024)
 AT_TAB_W = 32736
@@ -94,8 +95,8 @@ def tile_list_cherry_pollination_scores_kernel(
         page_a = [keep.tile([P, T2], F32, name="page_a0")]
         v_w = keep.tile([P, S], U32, name="v_w", align_bytes=64)
         picked_s = [
-            shared.tile([P, BANK], U8, name="picked_early", offset=AT_W1_S_LATE, align_bytes=64),
-            shared.tile([P, BANK], U8, name="picked_late", offset=AT_W1_S_LATE, align_bytes=64),
+            shared.tile([P, BANK], U8, name="picked_early", offset=AT_PICKED, align_bytes=64),
+            shared.tile([P, BANK], U8, name="picked_late", offset=AT_PICKED, align_bytes=64),
         ]
         v_s_late = keep.tile([P, BANK], U8, name="v_s_late", align_bytes=64)
         v_s = [planes[:, 0:BANK], v_s_late[:]]
@@ -105,18 +106,15 @@ def tile_list_cherry_pollination_scores_kernel(
         nc.vector.memset(tab_s[:].bitcast(I32)[0:ROWS_AT, :], 0)
         nc.gpsimd.memset(w1_s.bitcast(I32)[0:ROWS_AT, :], 0)
         table = tab_words[0].rearrange("p t i -> p (t i)").bitcast(I32)
-        nc.sync.dma_start(tab_w[:, 0:EARLY], table[:, 0:EARLY])
         nc.sync.dma_start(tab_s[:].bitcast(I32)[ROWS_AT:P, :], tab_scales[0].bitcast(I32))
         nc.sync.dma_start(list1[:], offs)
         nc.sync.dma_start(w1_s.bitcast(I32)[ROWS_AT:P, :], w1_scales[0, :, 0:K].bitcast(I32))
+        nc.sync.dma_start(tab_w[:, 0:EARLY], table[:, 0:EARLY])
         nc.sync.dma_start(list2[:], offs2)
-        nc.sync.dma_start(tab_w[:, EARLY:T], table[:, EARLY:T])
-        nc.sync.dma_start(list3[:], offs3)
         nc.sync.dma_start(w1_early[:].bitcast(I32), w1_words[0, :, 0 : 4 * P].bitcast(I32))
         nc.sync.dma_start(wg1_sb[0][:], wg1[:, 0:FIRST])
-        page_a.append(shared.tile([P, T2], F32, name="page_a1", offset=AT_PAGE_A1))
-        for page in page_a:
-            nc.vector.memset(page[:], 0.0)
+        nc.sync.dma_start(tab_w[:, EARLY:T], table[:, EARLY:T])
+        nc.vector.memset(page_a[0][:], 0.0)
 
         for h in range(2):
             nc.vector.tensor_copy(picked_s[h][:], tab_s[:].indirect(list1[:, 32 * h : 32 * (h + 1)]))
@@ -132,6 +130,8 @@ def tile_list_cherry_pollination_scores_kernel(
             nc.sync.dma_start(
                 w1_s_late[:].bitcast(I32)[32 * q : 32 * q + 4, :], w1_scales[0, 4 * q : 4 * q + 4, K:H].bitcast(I32)
             )
+        page_a.append(shared.tile([P, T2], F32, name="page_a1", offset=AT_PAGE_A1))
+        nc.vector.memset(page_a[1][:], 0.0)
         for lo, hi in ((0, FIRST), (FIRST, S)):
             nc.vector.tensor_copy(v_w[:, lo:hi], tab_w[:].bitcast(U32).indirect(list1[:, lo // 16 : hi // 16]))
 
@@ -141,6 +141,7 @@ def tile_list_cherry_pollination_scores_kernel(
         wg2_sb = shared.tile([P, S], F32, name="wg2_sb", offset=AT_WG2)
         gain_sb = shared.tile([P, 16], F32, name="gain_sb", offset=AT_WG2 + 4 * S)
         nc.sync.dma_start(wg2_sb[:], wg2)
+        nc.sync.dma_start(list3[:], offs3)
         with nc.allow_non_contiguous_dma(reason="one gain for each partition and slice"):
             nc.sync.dma_start(gain_sb[:, 0:4], gain[0:K].rearrange("(s p) -> p s", p=P))
             nc.sync.dma_start(gain_sb[:, 8:12], gain[K:H].rearrange("(p t) -> p t", t=4))
@@ -406,10 +407,11 @@ def tile_list_cherry_pollination_scores_kernel(
             )
             nc.scalar.copy(pollen[s][:, lo:hi], acc[:, 0 : hi - lo])
             wg = wg1_sb[0][:] if lo == 0 else wg1_sb[1][:, lo - FIRST : hi - FIRST]
-            nc.gpsimd.tensor_tensor(placed["a", s][:, lo:hi], pollen[s][:, lo:hi], wg, MULT)
+            (nc.vector if lo == 0 else nc.gpsimd).tensor_tensor(placed["a", s][:, lo:hi], pollen[s][:, lo:hi], wg, MULT)
 
         for s in range(2):
             early_values(s, 0, FIRST, "s%d" % s)
+        for s in range(2):
             nc.vector.tensor_copy(page_a[s][:].indirect(list2[:, 0 : FIRST // 16]), placed["a", s][:, 0:FIRST])
         for s in range(2):
             early_values(s, FIRST, BANK, ("x0", "s0")[s])

@@ -276,10 +276,8 @@ def tile_list_cherry_pollination_scores_kernel(
                 nc.scalar.activation(scaled[s][:, cols], scaled[s][:, cols], COPY, scale=gain_sb[:, j : j + 1])
 
         def add_last_page(s):
-            for c in range(CHUNKS):
-                nc.gpsimd.tensor_tensor(
-                    weather_sb[s][:, chunk(c)], weather_sb[s][:, chunk(c)], page_b[s % 2][:, chunk(c)], ADD
-                )
+            for cols in (slice(0, BANK), slice(BANK, 3 * BANK)):
+                nc.gpsimd.tensor_tensor(weather_sb[s][:, cols], weather_sb[s][:, cols], page_b[s % 2][:, cols], ADD)
 
         def pair_half(s, c):
             t = DEALT[s]
@@ -451,6 +449,8 @@ def tile_list_cherry_pollination_scores_kernel(
             after(*order[n])
         last = SLICES - 1
         scatter("a", last)
+        rest = shared.tile([P, BANK], F32, name="last_sum", offset=AT_Z_CODES[1] + 2048)
+        nc.vector.tensor_tensor(rest[:], weather_sb[last][:, chunk(3)], page_b[last % 2][:, chunk(3)], ADD)
 
         gelu_last = {}
         outs, woven, z_last = {}, {}, {}
@@ -476,7 +476,7 @@ def tile_list_cherry_pollination_scores_kernel(
         def finish(i):
             c, cols = in_chunk(i)
             nc.vector.scalar_tensor_tensor(
-                pair_half(last, c)[:, cols], gelu_last[i], gain_sb[:, 11:12], weather_sb[last][:, columns(i)], MULT, ADD
+                pair_half(last, c)[:, cols], gelu_last[i], gain_sb[:, 11:12], rest[:, cols] if c == 3 else weather_sb[last][:, columns(i)], MULT, ADD
             )
 
         def copy_on(engine, dst, src):
@@ -493,7 +493,7 @@ def tile_list_cherry_pollination_scores_kernel(
 
         def quantize_last(i):
             lo, hi = PIECES[i]
-            codes = shared.tile([P, hi - lo], U32, name="last_c%d" % i, offset=AT_Z_CODES[0] + 4 * lo, align_bytes=64)
+            codes = shared.tile([P, hi - lo], U32, name="last_c%d" % i, offset=(AT_Z_CODES[0] if i < 4 else AT_LATE_CODES + 12032 - 6144) + 4 * lo, align_bytes=64)
             scales = keep.tile([P, hi - lo], U8, name="last_s%d" % i, align_bytes=64)
             nc.vector.quantize_mx(out=codes[:].bitcast(FP8X4), scales=scales[:], in_=woven[i][:])
             z_last[i] = (codes[:], scales[:])

@@ -34,7 +34,8 @@ AT_W1_W_LATE = 3136
 AT_WG1_LATE = 5120
 AT_PAGE_A1 = 125280
 AT_PICKED = 133440
-AT_W1_S_LATE = AT_PICKED + 64
+AT_W1_DEALT = 66112
+AT_TURNED = 152320
 AT_PAGE_B1 = 67136
 AT_W2_RAW = (8224, 41024)
 AT_TAB_W = 32736
@@ -48,7 +49,7 @@ AT_IDENT = 65600
 AT_LAST_WEATHER = 76096
 AT_PAIRS = 87616
 PIECES = ((0, 256), (256, 512), (512, 1024), (1024, 1536), (1536, 1792), (1792, 2048))
-OUT_BANKS = (("s0", "s1"), ("x0", "x1"), ("z0", "z1", "z2"), ("z3", "s0", "s1"), ("x0", "x1"), ("z0", "z1"))
+OUT_BANKS = (("s0", "s1"), ("x0", "x1"), ("z0", "z1", "s0"), ("z2", "s1", "x0"), ("x1", "z3"), ("z0", "z1"))
 AT_WOVEN = (AT_ROWS[1], AT_ROWS[1] + 2048, AT_ROWS[1] + 4096, AT_Z_K[0], AT_Z_K[0] + 4096, AT_Z_K[0] + 6144)
 AT_RESULTS = (AT_ROWS[0], AT_PAGE_B0, AT_WEATHER[0], AT_WG2)
 AT_LATE_CODES = 134144
@@ -56,7 +57,6 @@ AT_WG1 = 104000
 AT_W3_CODES = (61504, AT_WG1)
 AT_Z_CODES = (108480, 112960)
 AT_FIRST_STIGMA = (AT_Z_CODES[0] - 384, AT_Z_CODES[1] - 384, AT_LAST_WEATHER - 768)
-AT_W1_DEALT = {4: AT_FIRST_STIGMA[0], 5: AT_FIRST_STIGMA[1], 6: AT_FIRST_STIGMA[2], 7: AT_FIRST_STIGMA[2] + 384}
 AT_DEALT_WG = {
     ("a", 4): AT_W3_CODES[0], ("a", 5): AT_W3_CODES[1], ("a", 6): AT_Z_CODES[0], ("a", 7): AT_LAST_WEATHER,
     ("b", 4): AT_WG2, ("b", 5): AT_LAST_WEATHER, ("b", 6): AT_Z_CODES[1], ("b", 7): AT_LAST_WEATHER,
@@ -86,7 +86,7 @@ def tile_list_cherry_pollination_scores_kernel(
         tab_s = shared.tile([P, T], U8, name="tab_s", offset=AT_TAB_S)
         w1_early = keep.tile([P, 4 * P], U8, name="w1_early", align_bytes=64)
         w1_late = shared.tile([P, 2 * H - 4 * P], U8, name="w1_late", offset=AT_W1_W_LATE, align_bytes=64)
-        planes = keep.tile([P, BANK + K], U8, name="planes", align_bytes=64)
+        planes = keep.tile([P, BANK + H], U8, name="planes", align_bytes=64)
         w1_s = planes[:, BANK : BANK + K]
         wg1_sb = [
             shared.tile([P, FIRST], F32, name="wg1_early", offset=AT_WG1),
@@ -98,17 +98,17 @@ def tile_list_cherry_pollination_scores_kernel(
             shared.tile([P, BANK], U8, name="picked_early", offset=AT_PICKED, align_bytes=64),
             shared.tile([P, BANK], U8, name="picked_late", offset=AT_PICKED, align_bytes=64),
         ]
-        v_s_late = keep.tile([P, BANK], U8, name="v_s_late", align_bytes=64)
-        v_s = [planes[:, 0:BANK], v_s_late[:]]
+        planes_late = keep.tile([P, BANK + K], U8, name="planes_late", align_bytes=64)
+        v_s = [planes[:, 0:BANK], planes_late[:, 0:BANK]]
         w2_c = keep.tile([P, H], U32, name="w2_c", align_bytes=64)
         w2_s = keep.tile([P, H], U8, name="w2_s", align_bytes=64)
 
         nc.vector.memset(tab_s[:].bitcast(I32)[0:ROWS_AT, :], 0)
-        nc.gpsimd.memset(w1_s.bitcast(I32)[0:ROWS_AT, :], 0)
+        nc.gpsimd.memset(planes[:, BANK : BANK + H].bitcast(I32)[0:ROWS_AT, :], 0)
         table = tab_words[0].rearrange("p t i -> p (t i)").bitcast(I32)
         nc.sync.dma_start(tab_s[:].bitcast(I32)[ROWS_AT:P, :], tab_scales[0].bitcast(I32))
         nc.sync.dma_start(list1[:], offs)
-        nc.sync.dma_start(w1_s.bitcast(I32)[ROWS_AT:P, :], w1_scales[0, :, 0:K].bitcast(I32))
+        nc.sync.dma_start(planes[:, BANK : BANK + H].bitcast(I32)[ROWS_AT:P, :], w1_scales[0].bitcast(I32))
         nc.sync.dma_start(tab_w[:, 0:EARLY], table[:, 0:EARLY])
         nc.sync.dma_start(list2[:], offs2)
         nc.sync.dma_start(w1_early[:].bitcast(I32), w1_words[0, :, 0 : 4 * P].bitcast(I32))
@@ -119,17 +119,16 @@ def tile_list_cherry_pollination_scores_kernel(
         for h in range(2):
             nc.vector.tensor_copy(picked_s[h][:], tab_s[:].indirect(list1[:, 32 * h : 32 * (h + 1)]))
             nc.vector.tensor_copy(v_s[h].bitcast(I32), picked_s[h][:].bitcast(I32))
-            rows = (planes, v_s_late)[h][:].bitcast(I32)
+            if h == 1:
+                nc.vector.tensor_copy(
+                    planes_late[:, BANK : BANK + K].rearrange("p (t q) -> p t q", t=4),
+                    planes[:, BANK + K : BANK + H].rearrange("p (q t) -> p t q", t=4),
+                )
+            rows = (planes, planes_late)[h][:, 0 : BANK + K].bitcast(I32)
             for r in range(4):
                 (nc.scalar, nc.sync)[h].dma_start(rows[r:P:32, :], rows[ROWS_AT + r : P : 4, :])
         nc.sync.dma_start(wg1_sb[1][:], wg1[:, FIRST:S])
         nc.sync.dma_start(w1_late[:].bitcast(I32), w1_words[0, :, 4 * P : 2 * H].bitcast(I32))
-        w1_s_late = shared.tile([P, K], U8, name="w1_s_late", offset=AT_W1_S_LATE, align_bytes=64)
-        nc.gpsimd.memset(w1_s_late[:].bitcast(I32), 0)
-        for q in range(4):
-            nc.sync.dma_start(
-                w1_s_late[:].bitcast(I32)[32 * q : 32 * q + 4, :], w1_scales[0, 4 * q : 4 * q + 4, K:H].bitcast(I32)
-            )
         page_a.append(shared.tile([P, T2], F32, name="page_a1", offset=AT_PAGE_A1))
         nc.vector.memset(page_a[1][:], 0.0)
         for lo, hi in ((0, FIRST), (FIRST, S)):
@@ -180,16 +179,15 @@ def tile_list_cherry_pollination_scores_kernel(
             for j in range((hi - lo) // P):
                 w3_blocks.append((codes[:, P * j : P * (j + 1)], scales[:, P * j : P * (j + 1)]))
 
-        w1_dealt = {}
+        w1_dealt = []
 
-        def deal_w1(s):
-            words = shared.tile([P, P, 2], U8, name="w1_dealt_w%d" % s, offset=AT_W1_DEALT[s], align_bytes=64)
-            scales = shared.tile([P, P], U8, name="w1_dealt_s%d" % s, offset=AT_W1_DEALT[s] + 2 * P, align_bytes=64)
-            src_w = w1_late[:, H - 4 * P : 2 * H - 4 * P].rearrange("p (q t b) -> p t q b", t=4, b=2)
-            src_s = w1_s_late[:].rearrange("p (q t) -> p t q", t=4)
-            nc.gpsimd.tensor_copy(words[:], src_w[:, DEALT[s], :, :])
-            nc.gpsimd.tensor_copy(scales[:], src_s[:, DEALT[s], :])
-            w1_dealt[s] = (words[:].rearrange("p q b -> p (q b)").bitcast(FP4X4), scales[:])
+        def deal_w1():
+            words = shared.tile([P, H], U8, name="w1_dealt", offset=AT_W1_DEALT, align_bytes=64)
+            nc.scalar.copy(
+                words[:].bitcast(U16).rearrange("p (t q) -> p t q", t=4),
+                w1_late[:, H - 4 * P : 2 * H - 4 * P].bitcast(U16).rearrange("p (q t) -> p t q", t=4),
+            )
+            w1_dealt.append(words)
 
         pollen, h2, placed, scaled, weather_sb, sums, z_rows, dealt_wg = {}, {}, {}, {}, {}, {}, {}, {}
 
@@ -204,7 +202,9 @@ def tile_list_cherry_pollination_scores_kernel(
             elif s < 4:
                 codes, scales = w1_late[:, 2 * P * (j - 2) : 2 * P * (j - 1)].bitcast(FP4X4), w1_s[:, P * j : P * (j + 1)]
             else:
-                codes, scales = w1_dealt[s]
+                t = DEALT[s]
+                codes = w1_dealt[0][:, 2 * P * t : 2 * P * (t + 1)].bitcast(FP4X4)
+                scales = planes_late[:, BANK + P * t : BANK + P * (t + 1)]
             for h in range(2):
                 acc = bank("s%d" % h)
                 nc.tensor.matmul_mx(
@@ -275,9 +275,14 @@ def tile_list_cherry_pollination_scores_kernel(
                 cols = slice(h * T2 // 2, (h + 1) * T2 // 2)
                 nc.scalar.activation(scaled[s][:, cols], scaled[s][:, cols], COPY, scale=gain_sb[:, j : j + 1])
 
+        rest = {}
+
         def add_last_page(s):
-            for cols in (slice(0, BANK), slice(BANK, 3 * BANK)):
-                nc.gpsimd.tensor_tensor(weather_sb[s][:, cols], weather_sb[s][:, cols], page_b[s % 2][:, cols], ADD)
+            for c in range(CHUNKS):
+                add_term(sums[s, c], page_b[s % 2], c, False, True)
+                rows = shared.tile([P, BANK], F32, name="rest_rows%d" % c, offset=AT_TURNED + 4096 * c)
+                nc.scalar.copy(rows[:], sums[s, c][:])
+                rest[c] = turn_back(rows[:], "z%d" % c)
 
         def pair_half(s, c):
             t = DEALT[s]
@@ -295,7 +300,7 @@ def tile_list_cherry_pollination_scores_kernel(
             for c in range(CHUNKS):
                 sums[s, c] = bank("z%d" % c)
                 add_term(sums[s, c], weather_sb[s], c, True, False)
-                if c < CHUNKS - 1 or s == 6:
+                if s < SLICES - 1 and (c < CHUNKS - 1 or s == 6):
                     add_term(sums[s, c], scaled[s], c, False, False)
 
         def close_sum(s, c):
@@ -305,18 +310,18 @@ def tile_list_cherry_pollination_scores_kernel(
             add_term(acc, page_b[s % 2], c, False, True)
             if s < 4:
                 if s == 0:
-                    z_rows[c] = work.tile([P, 4, 2, P, 2], BF16, name="z_rows", tag="z_rows%d" % c, bufs=1)
+                    z_rows[c] = shared.tile([P, 4, 2, P, 2], BF16, name="first_rows%d" % c, offset=AT_TURNED + 4096 * c)
                 nc.scalar.copy(
                     z_rows[c][:, :, :, 32 * s : 32 * (s + 1), :],
                     acc[:].rearrange("m (b p u e) -> m b u p e", b=4, u=2, e=2),
                 )
             elif s == 4:
-                z_rows[c] = work.tile([P, BANK], F32, name="z_rows", tag="z_rows%d" % c, bufs=1)
+                z_rows[c] = shared.tile([P, BANK], F32, name="single_rows%d" % c, offset=AT_TURNED + 4096 * c)
                 nc.scalar.copy(z_rows[c][:], acc[:])
                 nc.scalar.copy(pair_half(s, c), turn_back(z_rows[c][:], "x%d" % (c % 2))[:])
             else:
                 if DEALT[s] == 0:
-                    z_rows[c] = work.tile([P, BANK, 2], BF16, name="z_rows", tag="z_rows%d" % c, bufs=1)
+                    z_rows[c] = shared.tile([P, BANK, 2], BF16, name="pair_rows%d" % c, offset=AT_TURNED + 4096 * c)
                 nc.scalar.copy(z_rows[c][:, :, DEALT[s]], acc[:])
 
         def turn_back(words, tag):
@@ -372,7 +377,7 @@ def tile_list_cherry_pollination_scores_kernel(
                     nc.scalar.copy(pairs[c][:, 0, :], acc[:])
             if s == 3:
                 finish_first_pass()
-            if s + 1 < SLICES - 1:
+            if s + 1 < SLICES:
                 open_sums(s + 1)
                 if s + 3 < SLICES:
                     load_weather(s + 3)
@@ -428,6 +433,7 @@ def tile_list_cherry_pollination_scores_kernel(
         make_identity(nc, ident[:])
         ahead(3)
         ahead(4)
+        deal_w1()
         weigh(*order[3])
         ahead(5)
         weigh(*order[4])
@@ -443,16 +449,12 @@ def tile_list_cherry_pollination_scores_kernel(
                 z_first.extend(quantize_z(z_turned[0], 2, 0))
             if n + 3 < len(order):
                 weigh(*order[n + 3])
-                if order[n + 3][0] == "a" and order[n + 3][1] < SLICES - 1:
-                    deal_w1(order[n + 3][1] + 1)
             ahead(n + 4)
             after(*order[n])
         last = SLICES - 1
         scatter("a", last)
-        rest = shared.tile([P, BANK], F32, name="last_sum", offset=AT_Z_CODES[1] + 2048)
-        nc.vector.tensor_tensor(rest[:], weather_sb[last][:, chunk(3)], page_b[last % 2][:, chunk(3)], ADD)
 
-        gelu_last = {}
+        gelu_last = []
         outs, woven, z_last = {}, {}, {}
 
         def columns(i):
@@ -462,21 +464,21 @@ def tile_list_cherry_pollination_scores_kernel(
             lo, hi = PIECES[i]
             return lo // BANK, slice(lo % BANK, lo % BANK + hi - lo)
 
+        def gelu_of(i):
+            lo, hi = PIECES[i]
+            return gelu_last[lo // (2 * BANK)][:, lo % (2 * BANK) : lo % (2 * BANK) + hi - lo]
+
         def gelu(i):
             lo, hi = PIECES[i]
-            if i == 0:
-                gelu_last["early"] = work.tile([P, 2 * BANK], F32, name="last_gelu", tag="z_rows3", bufs=1)
-            if i < 3:
-                gelu_last[i] = gelu_last["early"][:, lo:hi]
-            else:
-                late = shared.tile([P, hi - lo], F32, name="last_gelu%d" % i, offset=AT_PAIRS + 4 * (lo - 2 * BANK))
-                gelu_last[i] = late[:]
-            nc.scalar.activation(gelu_last[i], page_a[last % 2][:, columns(i)], GELU)
+            if lo % (2 * BANK) == 0:
+                at = (AT_TURNED + 3 * 4096, AT_PAIRS)[lo // (2 * BANK)]
+                gelu_last.append(shared.tile([P, 2 * BANK], F32, name="last_gelu%d" % i, offset=at))
+            nc.scalar.activation(gelu_of(i), page_a[last % 2][:, columns(i)], GELU)
 
         def finish(i):
             c, cols = in_chunk(i)
             nc.vector.scalar_tensor_tensor(
-                pair_half(last, c)[:, cols], gelu_last[i], gain_sb[:, 11:12], rest[:, cols] if c == 3 else weather_sb[last][:, columns(i)], MULT, ADD
+                pair_half(last, c)[:, cols], gelu_of(i), gain_sb[:, 11:12], rest[c][:, cols], MULT, ADD
             )
 
         def copy_on(engine, dst, src):
@@ -519,7 +521,7 @@ def tile_list_cherry_pollination_scores_kernel(
                     )
 
         def quantize_first(c):
-            codes = shared.tile([P, BANK], U32, name="z_first%d" % c, offset=AT_PAIRS + 4096 * (c - 1), align_bytes=64)
+            codes = shared.tile([P, BANK], U32, name="z_first%d" % c, offset=(AT_Z_CODES[1] + 2048, AT_PAIRS + 2 * 4096)[c - 2], align_bytes=64)
             scales = keep.tile([P, BANK], U8, name="z_first_s%d" % c, align_bytes=64)
             nc.vector.quantize_mx(
                 out=codes[:].bitcast(FP8X4), scales=scales[:], in_=z_turned[1][:, 4 * BANK * (c - 2) : 4 * BANK * (c - 1)]
@@ -538,8 +540,9 @@ def tile_list_cherry_pollination_scores_kernel(
                 rows = out[P * blocks[0] : P * (blocks[-1] + 1), columns(i)]
                 nc.sync.dma_start(rows.rearrange("(a p) m -> p a m", p=P), result[:])
 
-        for i in range(3):
+        for i in range(2):
             last_product(i, 0)
+        quantize_first(2)
         for i in range(3):
             gelu(i)
             finish(i)
@@ -548,29 +551,32 @@ def tile_list_cherry_pollination_scores_kernel(
         for i in range(3, 6):
             gelu(i)
         quantize_last(0)
-        weave(2, "vector")
         quantize_last(1)
-        quantize_last(2)
-        for i in range(3):
-            last_product(i, 1)
-            leave(i, ("scalar",) * 3)
+        weave(2, "vector")
+        last_product(0, 1)
+        last_product(1, 1)
+        leave(0, ("scalar",) * 2)
+        last_product(2, 0)
         finish(3)
-        quantize_first(2)
+        quantize_last(2)
+        leave(1, ("scalar",) * 2)
+        last_product(2, 1)
         last_product(3, 0)
         weave(3, "vector")
         finish(4)
         quantize_last(3)
         finish(5)
-        weave(4, "scalar")
-        quantize_first(3)
-        weave(5, "vector")
         last_product(3, 1)
+        leave(2, ("scalar",) * 3)
+        quantize_first(3)
+        weave(4, "vector")
         last_product(4, 0)
+        weave(5, "vector")
         last_product(5, 0)
         quantize_last(4)
         quantize_last(5)
         leave(3, ("scalar",) * 3)
         last_product(4, 1)
         last_product(5, 1)
-        leave(4, ("vector", "vector"))
+        leave(4, ("vector", "scalar"))
         leave(5, ("scalar", "vector"))

@@ -25,15 +25,15 @@ SLICES = H // P
 CHUNKS = T2 // BANK
 NT = N // P
 FIRST = 256
-EARLY = 1024
-ROWS_AT = P - 16
+EARLY = 1280
+ROWS_AT = 4
 DEALT = {4: 2, 5: 0, 6: 1, 7: 3}
 AT_PAGE_B0 = 16384
 AT_TAB_S = 4608
 AT_W1_W_LATE = 3136
 AT_WG1_LATE = 5120
 AT_PAGE_A1 = 125280
-AT_PICKED = 133440
+AT_PICKED = 133504
 AT_W1_DEALT = 66112
 AT_TURNED = 152320
 AT_PAGE_B1 = 67136
@@ -86,7 +86,7 @@ def tile_list_cherry_pollination_scores_kernel(
         tab_s = shared.tile([P, T], U8, name="tab_s", offset=AT_TAB_S)
         w1_early = keep.tile([P, 4 * P], U8, name="w1_early", align_bytes=64)
         w1_late = shared.tile([P, 2 * H - 4 * P], U8, name="w1_late", offset=AT_W1_W_LATE, align_bytes=64)
-        planes = keep.tile([P, BANK + H], U8, name="planes", align_bytes=64)
+        planes = keep.tile([P, BANK + K], U8, name="planes", align_bytes=64)
         w1_s = planes[:, BANK : BANK + K]
         wg1_sb = [
             shared.tile([P, FIRST], F32, name="wg1_early", offset=AT_WG1),
@@ -98,39 +98,34 @@ def tile_list_cherry_pollination_scores_kernel(
             shared.tile([P, BANK], U8, name="picked_early", offset=AT_PICKED, align_bytes=64),
             shared.tile([P, BANK], U8, name="picked_late", offset=AT_PICKED, align_bytes=64),
         ]
-        planes_late = keep.tile([P, BANK + K], U8, name="planes_late", align_bytes=64)
+        planes_late = keep.tile([P, BANK], U8, name="planes_late", align_bytes=64)
         v_s = [planes[:, 0:BANK], planes_late[:, 0:BANK]]
         w2_c = keep.tile([P, H], U32, name="w2_c", align_bytes=64)
         w2_s = keep.tile([P, H], U8, name="w2_s", align_bytes=64)
 
-        nc.vector.memset(tab_s[:].bitcast(I32)[0:ROWS_AT, :], 0)
-        nc.gpsimd.memset(planes[:, BANK : BANK + H].bitcast(I32)[0:ROWS_AT, :], 0)
+        nc.vector.memset(tab_s[:].bitcast(I32), 0)
+        nc.vector.memset(w1_s.bitcast(I32), 0)
         table = tab_words[0].rearrange("p t i -> p (t i)").bitcast(I32)
-        nc.sync.dma_start(tab_s[:].bitcast(I32)[ROWS_AT:P, :], tab_scales[0].bitcast(I32))
-        nc.sync.dma_start(list1[:], offs)
-        nc.sync.dma_start(planes[:, BANK : BANK + H].bitcast(I32)[ROWS_AT:P, :], w1_scales[0].bitcast(I32))
         nc.sync.dma_start(tab_w[:, 0:EARLY], table[:, 0:EARLY])
-        nc.sync.dma_start(list2[:], offs2)
-        nc.sync.dma_start(w1_early[:].bitcast(I32), w1_words[0, :, 0 : 4 * P].bitcast(I32))
-        nc.sync.dma_start(wg1_sb[0][:], wg1[:, 0:FIRST])
+        nc.sync.dma_start(tab_s[:].bitcast(I32)[ROWS_AT:P:8, :], tab_scales[0].bitcast(I32))
+        nc.sync.dma_start(list1[:], offs)
+        nc.sync.dma_start(w1_s.bitcast(I32)[ROWS_AT:P:8, :], w1_scales[0, :, 0:K].bitcast(I32))
         nc.sync.dma_start(tab_w[:, EARLY:T], table[:, EARLY:T])
-        nc.vector.memset(page_a[0][:], 0.0)
+        nc.sync.dma_start(w1_early[:].bitcast(I32), w1_words[0, :, 0 : 4 * P].bitcast(I32))
+        nc.sync.dma_start(list2[:], offs2)
+        nc.sync.dma_start(wg1_sb[0][:], wg1[:, 0:FIRST])
+        page_a.append(shared.tile([P, T2], F32, name="page_a1", offset=AT_PAGE_A1))
+        for page in page_a:
+            nc.vector.memset(page[:], 0.0)
 
         for h in range(2):
             nc.vector.tensor_copy(picked_s[h][:], tab_s[:].indirect(list1[:, 32 * h : 32 * (h + 1)]))
             nc.vector.tensor_copy(v_s[h].bitcast(I32), picked_s[h][:].bitcast(I32))
-            if h == 1:
-                nc.vector.tensor_copy(
-                    planes_late[:, BANK : BANK + K].rearrange("p (t q) -> p t q", t=4),
-                    planes[:, BANK + K : BANK + H].rearrange("p (q t) -> p t q", t=4),
-                )
-            rows = (planes, planes_late)[h][:, 0 : BANK + K].bitcast(I32)
+            rows = (planes, planes_late)[h][:].bitcast(I32)
             for r in range(4):
-                (nc.scalar, nc.sync)[h].dma_start(rows[r:P:32, :], rows[ROWS_AT + r : P : 4, :])
+                (nc.scalar, nc.sync)[h].dma_start(rows[r:P:32, :], rows[ROWS_AT + 8 * r : P : 32, :])
         nc.sync.dma_start(wg1_sb[1][:], wg1[:, FIRST:S])
         nc.sync.dma_start(w1_late[:].bitcast(I32), w1_words[0, :, 4 * P : 2 * H].bitcast(I32))
-        page_a.append(shared.tile([P, T2], F32, name="page_a1", offset=AT_PAGE_A1))
-        nc.vector.memset(page_a[1][:], 0.0)
         for lo, hi in ((0, FIRST), (FIRST, S)):
             nc.vector.tensor_copy(v_w[:, lo:hi], tab_w[:].bitcast(U32).indirect(list1[:, lo // 16 : hi // 16]))
 
@@ -187,7 +182,13 @@ def tile_list_cherry_pollination_scores_kernel(
                 words[:].bitcast(U16).rearrange("p (t q) -> p t q", t=4),
                 w1_late[:, H - 4 * P : 2 * H - 4 * P].bitcast(U16).rearrange("p (q t) -> p t q", t=4),
             )
-            w1_dealt.append(words)
+            raw = shared.tile([P, K], U8, name="w1_s_late", offset=AT_WG1, align_bytes=64)
+            nc.gpsimd.memset(raw[:].bitcast(I32), 0)
+            for q in range(4):
+                nc.sync.dma_start(raw[:].bitcast(I32)[32 * q : 32 * q + 4, :], w1_scales[0, 4 * q : 4 * q + 4, K:H].bitcast(I32))
+            scales = keep.tile([P, K], U8, name="w1_dealt_s", align_bytes=64)
+            nc.gpsimd.tensor_copy(scales[:].rearrange("p (t q) -> p t q", t=4), raw[:].rearrange("p (q t) -> p t q", t=4))
+            w1_dealt.extend([words, scales])
 
         pollen, h2, placed, scaled, weather_sb, sums, z_rows, dealt_wg = {}, {}, {}, {}, {}, {}, {}, {}
 
@@ -204,7 +205,7 @@ def tile_list_cherry_pollination_scores_kernel(
             else:
                 t = DEALT[s]
                 codes = w1_dealt[0][:, 2 * P * t : 2 * P * (t + 1)].bitcast(FP4X4)
-                scales = planes_late[:, BANK + P * t : BANK + P * (t + 1)]
+                scales = w1_dealt[1][:, P * t : P * (t + 1)]
             for h in range(2):
                 acc = bank("s%d" % h)
                 nc.tensor.matmul_mx(

@@ -25,15 +25,15 @@ SLICES = H // P
 CHUNKS = T2 // BANK
 NT = N // P
 FIRST = 256
-EARLY = 1280
+EARLY = 768
 ROWS_AT = 4
 DEALT = {4: 2, 5: 0, 6: 1, 7: 3}
 AT_PAGE_B0 = 16384
-AT_TAB_S = 4608
-AT_W1_W_LATE = 3136
-AT_WG1_LATE = 5120
+AT_TAB_S = 133440
+AT_W1_W_LATE = 136576
+AT_WG1_LATE = 133504
 AT_PAGE_A1 = 125280
-AT_PICKED = 133504
+AT_PICKED = (8256, 4608)
 AT_W1_DEALT = 66112
 AT_TURNED = 152320
 AT_PAGE_B1 = 67136
@@ -95,8 +95,8 @@ def tile_list_cherry_pollination_scores_kernel(
         page_a = [keep.tile([P, T2], F32, name="page_a0")]
         v_w = keep.tile([P, S], U32, name="v_w", align_bytes=64)
         picked_s = [
-            shared.tile([P, BANK], U8, name="picked_early", offset=AT_PICKED, align_bytes=64),
-            shared.tile([P, BANK], U8, name="picked_late", offset=AT_PICKED, align_bytes=64),
+            shared.tile([P, BANK], U8, name="picked_early", offset=AT_PICKED[0], align_bytes=64),
+            shared.tile([P, BANK], U8, name="picked_late", offset=AT_PICKED[1], align_bytes=64),
         ]
         planes_late = keep.tile([P, BANK], U8, name="planes_late", align_bytes=64)
         v_s = [planes[:, 0:BANK], planes_late[:, 0:BANK]]
@@ -104,26 +104,28 @@ def tile_list_cherry_pollination_scores_kernel(
         w2_s = keep.tile([P, H], U8, name="w2_s", align_bytes=64)
 
         nc.vector.memset(tab_s[:].bitcast(I32), 0)
-        nc.vector.memset(w1_s.bitcast(I32), 0)
+        nc.vector.memset(planes[:].bitcast(I32), 0)
+        nc.vector.memset(planes_late[:].bitcast(I32), 0)
         table = tab_words[0].rearrange("p t i -> p (t i)").bitcast(I32)
         nc.sync.dma_start(tab_w[:, 0:EARLY], table[:, 0:EARLY])
         nc.sync.dma_start(tab_s[:].bitcast(I32)[ROWS_AT:P:8, :], tab_scales[0].bitcast(I32))
         nc.sync.dma_start(list1[:], offs)
-        nc.sync.dma_start(w1_s.bitcast(I32)[ROWS_AT:P:8, :], w1_scales[0, :, 0:K].bitcast(I32))
         nc.sync.dma_start(tab_w[:, EARLY:T], table[:, EARLY:T])
         nc.sync.dma_start(w1_early[:].bitcast(I32), w1_words[0, :, 0 : 4 * P].bitcast(I32))
         nc.sync.dma_start(list2[:], offs2)
         nc.sync.dma_start(wg1_sb[0][:], wg1[:, 0:FIRST])
-        page_a.append(shared.tile([P, T2], F32, name="page_a1", offset=AT_PAGE_A1))
-        for page in page_a:
-            nc.vector.memset(page[:], 0.0)
+        for q in range(4):
+            nc.scalar.dma_start(w1_s.bitcast(I32)[32 * q : 32 * q + 4, :], w1_scales[0, 4 * q : 4 * q + 4, 0:K].bitcast(I32))
+        nc.vector.memset(page_a[0][:], 0.0)
 
         for h in range(2):
             nc.vector.tensor_copy(picked_s[h][:], tab_s[:].indirect(list1[:, 32 * h : 32 * (h + 1)]))
-            nc.vector.tensor_copy(v_s[h].bitcast(I32), picked_s[h][:].bitcast(I32))
-            rows = (planes, planes_late)[h][:].bitcast(I32)
             for r in range(4):
-                (nc.scalar, nc.sync)[h].dma_start(rows[r:P:32, :], rows[ROWS_AT + 8 * r : P : 32, :])
+                (nc.scalar, nc.sync)[h].dma_start(
+                    v_s[h].bitcast(I32)[r:P:32, :], picked_s[h][:].bitcast(I32)[ROWS_AT + 8 * r : P : 32, :]
+                )
+        page_a.append(shared.tile([P, T2], F32, name="page_a1", offset=AT_PAGE_A1))
+        nc.vector.memset(page_a[1][:], 0.0)
         nc.sync.dma_start(wg1_sb[1][:], wg1[:, FIRST:S])
         nc.sync.dma_start(w1_late[:].bitcast(I32), w1_words[0, :, 4 * P : 2 * H].bitcast(I32))
         for lo, hi in ((0, FIRST), (FIRST, S)):

@@ -34,7 +34,7 @@ AT_W1_W_LATE = 136576
 AT_WG1_LATE = 133504
 AT_PAGE_A1 = 125280
 AT_PICKED = (8256, 4608)
-AT_W1_DEALT = 66112
+AT_W1_DEALT = 512
 AT_TURNED = 152320
 AT_PAGE_B1 = 67136
 AT_W2_RAW = (8224, 41024)
@@ -45,20 +45,20 @@ AT_Z_K = (53312, 117056)
 AT_W2_BF = 61440
 AT_W3_RAW = AT_W2_BF + 32 - 6144
 AT_WEATHER = (8192, 24576)
-AT_IDENT = 65600
+AT_IDENT = 0
 AT_LAST_WEATHER = 76096
 AT_PAIRS = 87616
 PIECES = ((0, 256), (256, 512), (512, 1024), (1024, 1536), (1536, 1792), (1792, 2048))
 OUT_BANKS = (("s0", "s1"), ("x0", "x1"), ("z0", "z1", "s0"), ("z2", "s1", "x0"), ("x1", "z3"), ("z0", "z1"))
-AT_WOVEN = (AT_ROWS[1], AT_ROWS[1] + 2048, AT_ROWS[1] + 4096, AT_Z_K[0], AT_Z_K[0] + 4096, AT_Z_K[0] + 6144)
+AT_WOVEN = (AT_ROWS[1], AT_ROWS[1] + 2048, AT_PAGE_B1, AT_Z_K[0], AT_Z_K[0] + 4096, AT_Z_K[0] + 6144)
 AT_RESULTS = (AT_ROWS[0], AT_PAGE_B0, AT_WEATHER[0], AT_WG2)
 AT_LATE_CODES = 134144
 AT_WG1 = 104000
 AT_W3_CODES = (61504, AT_WG1)
 AT_Z_CODES = (108480, 112960)
-AT_FIRST_STIGMA = (AT_Z_CODES[0] - 384, AT_Z_CODES[1] - 384, AT_LAST_WEATHER - 768)
+AT_FIRST_STIGMA = (AT_Z_CODES[0] - 384, AT_IDENT, AT_LAST_WEATHER - 768)
 AT_DEALT_WG = {
-    ("a", 4): AT_W3_CODES[0], ("a", 5): AT_W3_CODES[1], ("a", 6): AT_Z_CODES[0], ("a", 7): AT_LAST_WEATHER,
+    ("a", 4): AT_W3_CODES[0], ("a", 5): AT_W3_CODES[1], ("a", 6): AT_Z_CODES[0], ("a", 7): AT_W3_CODES[0],
     ("b", 4): AT_WG2, ("b", 5): AT_LAST_WEATHER, ("b", 6): AT_Z_CODES[1], ("b", 7): AT_LAST_WEATHER,
 }
 
@@ -171,7 +171,7 @@ def tile_list_cherry_pollination_scores_kernel(
         def quantize_w3(i):
             lo, hi = ((0, 512), (512, 768))[i]
             codes = shared.tile([P, hi - lo], U32, name="w3_c%d" % i, offset=AT_LATE_CODES + 4096 + 4 * lo, align_bytes=64)
-            scales = shared.tile([P, hi - lo], U8, name="w3_s%d" % i, offset=AT_LATE_CODES + 11264 + lo, align_bytes=64)
+            scales = shared.tile([P, hi - lo], U8, name="w3_s%d" % i, offset=AT_ROWS[1] + 4096 + lo, align_bytes=64)
             nc.vector.quantize_mx(out=codes[:].bitcast(FP8X4), scales=scales[:], in_=w3_bf[0][:, 4 * lo : 4 * hi])
             for j in range((hi - lo) // P):
                 w3_blocks.append((codes[:, P * j : P * (j + 1)], scales[:, P * j : P * (j + 1)]))
@@ -198,7 +198,10 @@ def tile_list_cherry_pollination_scores_kernel(
             return s if s < 4 else 4 + DEALT[s]
 
         def first_products(kind, s):
-            made = work.tile([P, S], F32, name="made", tag="made_" + kind, bufs=3 if kind == "a" else 2)
+            if (kind, s) == ("b", SLICES - 1):
+                made = shared.tile([P, S], F32, name="made_last", offset=AT_DEALT_WG["a", s])
+            else:
+                made = work.tile([P, S], F32, name="made", tag="made_" + kind, bufs=3 if kind == "a" else 2)
             j = column_block(s)
             if kind == "b":
                 codes, scales = w2_c[:, P * j : P * (j + 1)].bitcast(FP8X4), w2_s[:, P * j : P * (j + 1)]
@@ -236,7 +239,7 @@ def tile_list_cherry_pollination_scores_kernel(
             if (kind, s) == ("a", SLICES - 1):
                 placed[kind, s] = shared.tile([P, S], F32, name="placed_last", offset=AT_Z_CODES[1])
             elif (kind, s) == ("b", 6):
-                placed[kind, s] = shared.tile([P, S], F32, name="placed_b6", offset=AT_LATE_CODES + 4096 - 512)
+                placed[kind, s] = shared.tile([P, S], F32, name="placed_b6", offset=4608 - 512)
             else:
                 placed[kind, s] = work.tile([P, S], F32, name="placed", tag="placed", bufs=3)
             src = pollen[s]
@@ -342,7 +345,7 @@ def tile_list_cherry_pollination_scores_kernel(
                 z_c = shared.tile([P, 2 * BANK], U32, name="z_first%d" % i, offset=(AT_LATE_CODES, AT_Z_CODES[1])[i], align_bytes=64)
             else:
                 z_c = work.tile([P, BANK], U32, name="z_c", tag="z_c", bufs=4, align_bytes=64)
-            z_s = work.tile([P, chunks * BANK], U8, name="z_s", tag="z_s%d" % chunks, bufs=4 // chunks, align_bytes=64)
+            z_s = shared.tile([P, chunks * BANK], U8, name="z_s", offset=AT_ROWS[1] + 5120, align_bytes=64)
             nc.vector.quantize_mx(out=z_c[:].bitcast(FP8X4), scales=z_s[:], in_=z_k[:])
             return [(z_c[:, chunk(i)], z_s[:, chunk(i)]) for i in range(chunks)]
 
@@ -432,28 +435,28 @@ def tile_list_cherry_pollination_scores_kernel(
         for i in range(2):
             page_b.append(shared.tile([P, T2], F32, name="page_b%d" % i, offset=(AT_PAGE_B0, AT_PAGE_B1)[i]))
             nc.gpsimd.memset(page_b[i][:], 0.0)
-        ident = shared.tile([P, P], F32, name="ident", offset=AT_IDENT)
-        make_identity(nc, ident[:])
         ahead(3)
         ahead(4)
-        deal_w1()
         weigh(*order[3])
         ahead(5)
         weigh(*order[4])
+        ident = shared.tile([P, P], F32, name="ident", offset=AT_IDENT)
+        make_identity(nc, ident[:])
+        deal_w1()
         after("a", 0)
         after("a", 1)
         cast_w3()
         pairs = [shared.tile([P, 2, BANK], F32, name="pairs%d" % c, offset=AT_PAIRS + 4096 * c) for c in range(CHUNKS)]
         for n in range(2, len(order) - 1):
             scatter(*order[n])
-            if order[n] == ("b", 6):
-                for i in range(2):
-                    quantize_w3(i)
-                z_first.extend(quantize_z(z_turned[0], 2, 0))
             if n + 3 < len(order):
                 weigh(*order[n + 3])
             ahead(n + 4)
             after(*order[n])
+            if order[n] == ("b", 5):
+                for i in range(2):
+                    quantize_w3(i)
+                z_first.extend(quantize_z(z_turned[0], 2, 0))
         last = SLICES - 1
         scatter("a", last)
 
@@ -506,6 +509,8 @@ def tile_list_cherry_pollination_scores_kernel(
         def groups(i):
             lo, hi = PIECES[i]
             per = BANK // (hi - lo)
+            if i == 0:
+                return [range(0, 1), range(1, NT)]
             return [range(a, min(a + per, NT)) for a in range(0, NT, per)]
 
         def last_product(i, b):

from contextlib import ExitStack

import concourse.mybir as mybir
from concourse.masks import make_identity

K, H, N, T, S, T2 = 512, 1024, 384, 4096, 1024, 2048
FLOPS = 2 * (2 * K * H * S + H * N * T2)

F32 = mybir.dt.float32
BF16 = mybir.dt.bfloat16
I32 = mybir.dt.int32
U32 = mybir.dt.uint32
U16 = mybir.dt.uint16
U8 = mybir.dt.uint8
FP8X4 = mybir.dt.float8_e4m3fn_x4
FP4X4 = mybir.dt.float4_e2m1fn_x4
MULT = mybir.AluOpType.mult
ADD = mybir.AluOpType.add
GELU = mybir.ActivationFunctionType.Gelu_apprx_tanh
COPY = mybir.ActivationFunctionType.Copy

P = 128
BANK = 512
SLICES = H // P
CHUNKS = T2 // BANK
NT = N // P
FIRST = 256
EARLY = 768
ROWS_AT = 4
DEALT = {4: 2, 5: 0, 6: 1, 7: 3}
AT_PAGE_B0 = 16384
AT_TAB_S = 133440
AT_W1_W_LATE = 136576
AT_WG1_LATE = 133504
AT_PAGE_A1 = 125280
AT_PICKED = (8256, 4608)
AT_W1_DEALT = 512
AT_TURNED = 152320
AT_PAGE_B1 = 67136
AT_W2_RAW = (8224, 41024)
AT_TAB_W = 32736
AT_WG2 = 32768
AT_ROWS = (36928, 45120)
AT_Z_K = (53312, 117056)
AT_W2_BF = 61440
AT_W3_RAW = AT_W2_BF + 32 - 6144
AT_WEATHER = (8192, 24576)
AT_IDENT = 0
AT_LAST_WEATHER = 76096
AT_PAIRS = 87616
PIECES = ((0, 256), (256, 512), (512, 1024), (1024, 1536), (1536, 1792), (1792, 2048))
OUT_BANKS = (("s0", "s1"), ("x0", "x1"), ("z0", "z1", "s0"), ("z2", "s1", "x0"), ("x1", "z3"), ("z0", "z1"))
AT_WOVEN = (AT_ROWS[1], AT_ROWS[1] + 2048, AT_PAGE_B1, AT_Z_K[0], AT_Z_K[0] + 4096, AT_Z_K[0] + 6144)
AT_RESULTS = (AT_ROWS[0], AT_PAGE_B0, AT_WEATHER[0], AT_WG2)
AT_LATE_CODES = 134144
AT_WG1 = 104000
AT_W3_CODES = (61504, AT_WG1)
AT_Z_CODES = (108480, 112960)
AT_FIRST_STIGMA = (AT_Z_CODES[0] - 384, AT_IDENT, AT_LAST_WEATHER - 768)
AT_DEALT_WG = {
    ("a", 4): AT_W3_CODES[0], ("a", 5): AT_W3_CODES[1], ("a", 6): AT_Z_CODES[0], ("a", 7): AT_W3_CODES[0],
    ("b", 4): AT_WG2, ("b", 5): AT_LAST_WEATHER, ("b", 6): AT_Z_CODES[1], ("b", 7): AT_LAST_WEATHER,
}


def tile_list_cherry_pollination_scores_kernel(
    tc, tab_words, tab_scales, offs, offs2, offs3, w1_words, w1_scales, w2, wg1, wg2, gain, weather, w3, out
):
    nc = tc.nc
    with ExitStack() as ctx:
        keep = ctx.enter_context(tc.tile_pool(name="keep", bufs=1))
        work = ctx.enter_context(tc.tile_pool(name="work", bufs=2))
        shared = ctx.enter_context(tc.tile_pool(name="shared", bufs=1))
        psum = ctx.enter_context(tc.psum_pool(name="psum", bufs=1))

        def bank(tag):
            return psum.tile([P, BANK], F32, name=tag, tag=tag)

        def chunk(c):
            return slice(BANK * c, BANK * (c + 1))

        list1 = keep.tile([P, S // 16], U16, name="list1")
        list2 = keep.tile([P, S // 16], U16, name="list2")
        list3 = keep.tile([P, S // 16], U16, name="list3")
        tab_w = shared.tile([P, T], I32, name="tab_w", offset=AT_TAB_W)
        tab_s = shared.tile([P, T], U8, name="tab_s", offset=AT_TAB_S)
        w1_early = keep.tile([P, 4 * P], U8, name="w1_early", align_bytes=64)
        w1_late = shared.tile([P, 2 * H - 4 * P], U8, name="w1_late", offset=AT_W1_W_LATE, align_bytes=64)
        planes = keep.tile([P, BANK + K], U8, name="planes", align_bytes=64)
        w1_s = planes[:, BANK : BANK + K]
        wg1_sb = [
            shared.tile([P, FIRST], F32, name="wg1_early", offset=AT_WG1),
            shared.tile([P, S - FIRST], F32, name="wg1_late", offset=AT_WG1_LATE),
        ]
        page_a = [keep.tile([P, T2], F32, name="page_a0")]
        v_w = keep.tile([P, S], U32, name="v_w", align_bytes=64)
        picked_s = [
            shared.tile([P, BANK], U8, name="picked_early", offset=AT_PICKED[0], align_bytes=64),
            shared.tile([P, BANK], U8, name="picked_late", offset=AT_PICKED[1], align_bytes=64),
        ]
        planes_late = keep.tile([P, BANK], U8, name="planes_late", align_bytes=64)
        v_s = [planes[:, 0:BANK], planes_late[:, 0:BANK]]
        w2_c = keep.tile([P, H], U32, name="w2_c", align_bytes=64)
        w2_s = keep.tile([P, H], U8, name="w2_s", align_bytes=64)

        nc.vector.memset(tab_s[:].bitcast(I32), 0)
        nc.vector.memset(planes[:].bitcast(I32), 0)
        nc.vector.memset(planes_late[:].bitcast(I32), 0)
        table = tab_words[0].rearrange("p t i -> p (t i)").bitcast(I32)
        nc.sync.dma_start(tab_w[:, 0:EARLY], table[:, 0:EARLY])
        nc.sync.dma_start(tab_s[:].bitcast(I32)[ROWS_AT:P:8, :], tab_scales[0].bitcast(I32))
        nc.sync.dma_start(list1[:], offs)
        nc.sync.dma_start(tab_w[:, EARLY:T], table[:, EARLY:T])
        nc.sync.dma_start(w1_early[:].bitcast(I32), w1_words[0, :, 0 : 4 * P].bitcast(I32))
        nc.sync.dma_start(list2[:], offs2)
        nc.sync.dma_start(wg1_sb[0][:], wg1[:, 0:FIRST])
        for q in range(4):
            nc.scalar.dma_start(w1_s.bitcast(I32)[32 * q : 32 * q + 4, :], w1_scales[0, 4 * q : 4 * q + 4, 0:K].bitcast(I32))
        nc.vector.memset(page_a[0][:], 0.0)

        for h in range(2):
            nc.vector.tensor_copy(picked_s[h][:], tab_s[:].indirect(list1[:, 32 * h : 32 * (h + 1)]))
            for r in range(4):
                (nc.scalar, nc.sync)[h].dma_start(
                    v_s[h].bitcast(I32)[r:P:32, :], picked_s[h][:].bitcast(I32)[ROWS_AT + 8 * r : P : 32, :]
                )
        page_a.append(shared.tile([P, T2], F32, name="page_a1", offset=AT_PAGE_A1))
        nc.vector.memset(page_a[1][:], 0.0)
        nc.sync.dma_start(wg1_sb[1][:], wg1[:, FIRST:S])
        nc.sync.dma_start(w1_late[:].bitcast(I32), w1_words[0, :, 4 * P : 2 * H].bitcast(I32))
        for lo, hi in ((0, FIRST), (FIRST, S)):
            nc.vector.tensor_copy(v_w[:, lo:hi], tab_w[:].bitcast(U32).indirect(list1[:, lo // 16 : hi // 16]))

        w2_raw = [shared.tile([P, 4, BANK], F32, name="w2_raw%d" % h, offset=AT_W2_RAW[h]) for h in range(2)]
        for h in range(2):
            nc.sync.dma_start(w2_raw[h][:], w2[:, chunk(h)].rearrange("(p j) w -> p j w", j=4))
        wg2_sb = shared.tile([P, S], F32, name="wg2_sb", offset=AT_WG2)
        gain_sb = shared.tile([P, 16], F32, name="gain_sb", offset=AT_WG2 + 4 * S)
        nc.sync.dma_start(wg2_sb[:], wg2)
        nc.sync.dma_start(list3[:], offs3)
        with nc.allow_non_contiguous_dma(reason="one gain for each partition and slice"):
            nc.sync.dma_start(gain_sb[:, 0:4], gain[0:K].rearrange("(s p) -> p s", p=P))
            nc.sync.dma_start(gain_sb[:, 8:12], gain[K:H].rearrange("(p t) -> p t", t=4))

        def interleave(dst, raw):
            nc.scalar.copy(
                dst.rearrange("p (c i t) -> p c t i", i=4, t=4),
                raw.rearrange("p t (c i) -> p c t i", i=4),
            )

        def prepare_w2():
            w2_bf = shared.tile([P, 4 * H], BF16, name="w2_bf", offset=AT_W2_BF, align_bytes=64)
            interleave(w2_bf[:, 0 : 4 * BANK], w2_raw[0][:])
            nc.scalar.copy(
                w2_bf[:, 4 * BANK : 8 * BANK].rearrange("p (t q j) -> p q j t", t=4, j=4),
                w2_raw[1][:].rearrange("p j (q t) -> p q j t", t=4),
            )
            nc.vector.quantize_mx(out=w2_c[:].bitcast(FP8X4), scales=w2_s[:], in_=w2_bf[:])

        w3_bf = []
        w3_blocks = []

        def cast_w3():
            rounded = shared.tile([P, 2 * N * 4], BF16, name="w3_bf", offset=AT_LATE_CODES + 12032, align_bytes=64)
            for b in range(2):
                w3_raw = shared.tile([P, 4, N], F32, name="w3_raw%d" % b, offset=AT_W3_RAW)
                nc.sync.dma_start(w3_raw[:], w3[b * K : (b + 1) * K, :].rearrange("(p j) w -> p j w", j=4))
                interleave(rounded[:, b * 4 * N : (b + 1) * 4 * N], w3_raw[:])
            w3_bf.append(rounded)

        def quantize_w3(i):
            lo, hi = ((0, 512), (512, 768))[i]
            codes = shared.tile([P, hi - lo], U32, name="w3_c%d" % i, offset=AT_LATE_CODES + 4096 + 4 * lo, align_bytes=64)
            scales = shared.tile([P, hi - lo], U8, name="w3_s%d" % i, offset=AT_ROWS[1] + 4096 + lo, align_bytes=64)
            nc.vector.quantize_mx(out=codes[:].bitcast(FP8X4), scales=scales[:], in_=w3_bf[0][:, 4 * lo : 4 * hi])
            for j in range((hi - lo) // P):
                w3_blocks.append((codes[:, P * j : P * (j + 1)], scales[:, P * j : P * (j + 1)]))

        w1_dealt = []

        def deal_w1():
            words = shared.tile([P, H], U8, name="w1_dealt", offset=AT_W1_DEALT, align_bytes=64)
            nc.scalar.copy(
                words[:].bitcast(U16).rearrange("p (t q) -> p t q", t=4),
                w1_late[:, H - 4 * P : 2 * H - 4 * P].bitcast(U16).rearrange("p (q t) -> p t q", t=4),
            )
            raw = shared.tile([P, K], U8, name="w1_s_late", offset=AT_WG1, align_bytes=64)
            nc.gpsimd.memset(raw[:].bitcast(I32), 0)
            for q in range(4):
                nc.sync.dma_start(raw[:].bitcast(I32)[32 * q : 32 * q + 4, :], w1_scales[0, 4 * q : 4 * q + 4, K:H].bitcast(I32))
            scales = keep.tile([P, K], U8, name="w1_dealt_s", align_bytes=64)
            nc.gpsimd.tensor_copy(scales[:].rearrange("p (t q) -> p t q", t=4), raw[:].rearrange("p (q t) -> p t q", t=4))
            w1_dealt.extend([words, scales])

        pollen, h2, placed, scaled, weather_sb, sums, z_rows, dealt_wg = {}, {}, {}, {}, {}, {}, {}, {}

        def column_block(s):
            return s if s < 4 else 4 + DEALT[s]

        def first_products(kind, s):
            if (kind, s) == ("b", SLICES - 1):
                made = shared.tile([P, S], F32, name="made_last", offset=AT_DEALT_WG["a", s])
            else:
                made = work.tile([P, S], F32, name="made", tag="made_" + kind, bufs=3 if kind == "a" else 2)
            j = column_block(s)
            if kind == "b":
                codes, scales = w2_c[:, P * j : P * (j + 1)].bitcast(FP8X4), w2_s[:, P * j : P * (j + 1)]
            elif s < 4:
                codes, scales = w1_late[:, 2 * P * (j - 2) : 2 * P * (j - 1)].bitcast(FP4X4), w1_s[:, P * j : P * (j + 1)]
            else:
                t = DEALT[s]
                codes = w1_dealt[0][:, 2 * P * t : 2 * P * (t + 1)].bitcast(FP4X4)
                scales = w1_dealt[1][:, P * t : P * (t + 1)]
            for h in range(2):
                acc = bank("s%d" % h)
                nc.tensor.matmul_mx(
                    out=acc[:], lhsT=codes, lhsT_scale=scales, rhs=v_w[:, chunk(h)].bitcast(FP8X4),
                    rhs_scale=v_s[h], start=True, stop=True,
                )
                if kind == "a":
                    nc.scalar.copy(made[:, chunk(h)], acc[:])
                else:
                    nc.scalar.activation(made[:, chunk(h)], acc[:], COPY, scale=-1.0)
            (pollen if kind == "a" else h2)[s] = made

        def load_dealt_wg(kind, s):
            tile = shared.tile([P, S], F32, name="dealt_wg_%s%d" % (kind, s), offset=AT_DEALT_WG[kind, s])
            rows = (wg1 if kind == "a" else wg2).rearrange("(q t) j -> t q j", t=4)[DEALT[s]]
            for g in range(4):
                nc.sync.dma_start(tile[32 * g : 32 * (g + 1), :], rows)
            dealt_wg[kind, s] = tile

        def weigh(kind, s):
            if s >= 4:
                wg = dealt_wg[kind, s]
            else:
                wg = wg2_sb
            halves = [slice(0, S)]
            if (kind, s) == ("a", SLICES - 1):
                placed[kind, s] = shared.tile([P, S], F32, name="placed_last", offset=AT_Z_CODES[1])
            elif (kind, s) == ("b", 6):
                placed[kind, s] = shared.tile([P, S], F32, name="placed_b6", offset=4608 - 512)
            else:
                placed[kind, s] = work.tile([P, S], F32, name="placed", tag="placed", bufs=3)
            src = pollen[s]
            if kind == "b":
                if s < 3:
                    src = shared.tile([P, S], F32, name="stigma%d" % s, offset=AT_FIRST_STIGMA[s])
                else:
                    src = work.tile([P, S], F32, name="stigma", tag="stigma", bufs=1)
            if (kind, s) == ("b", 0):
                nc.gpsimd.tensor_tensor(src[:], pollen[s][:], wg[:], MULT)
                nc.gpsimd.tensor_tensor(placed[kind, s][:], src[:], h2[s][:], MULT)
                return
            if kind == "a" and s < 4:
                for cols, part in ((slice(0, FIRST), wg1_sb[0]), (slice(FIRST, S), wg1_sb[1])):
                    nc.gpsimd.tensor_tensor(placed[kind, s][:, cols], src[:, cols], part[:], MULT)
                return
            for cols in halves:
                if kind == "b":
                    nc.gpsimd.tensor_tensor(src[:, cols], h2[s][:, cols], pollen[s][:, cols], MULT)
                nc.gpsimd.tensor_tensor(placed[kind, s][:, cols], src[:, cols], wg[:, cols], MULT)

        def scatter(kind, s):
            page, offsets = (page_a[s % 2], list2) if kind == "a" else (page_b[s % 2], list3)
            nc.vector.tensor_copy(page[:].indirect(offsets[:]), placed[kind, s][:])

        def load_weather(s):
            weather_sb[s] = shared.tile([P, T2], F32, name="weather%d" % s, offset=AT_WEATHER[s % 2])
            if s < 4:
                rows = weather[P * s : P * (s + 1), :]
            else:
                rows = weather[K:H, :].rearrange("(p t) m -> t p m", t=4)[DEALT[s]]
            nc.sync.dma_start(weather_sb[s][:], rows)

        def gelu_gain(s):
            scaled[s] = shared.tile([P, T2], F32, name="scaled%d" % (s % 2), offset=AT_ROWS[s % 2])
            j = s if s < 4 else 8 + DEALT[s]
            nc.scalar.activation(scaled[s][:], page_a[s % 2][:], GELU)
            for h in range(2):
                cols = slice(h * T2 // 2, (h + 1) * T2 // 2)
                nc.scalar.activation(scaled[s][:, cols], scaled[s][:, cols], COPY, scale=gain_sb[:, j : j + 1])

        rest = {}

        def add_last_page(s):
            for c in range(CHUNKS):
                add_term(sums[s, c], page_b[s % 2], c, False, True)
                rows = shared.tile([P, BANK], F32, name="rest_rows%d" % c, offset=AT_TURNED + 4096 * c)
                nc.scalar.copy(rows[:], sums[s, c][:])
                rest[c] = turn_back(rows[:], "z%d" % c)

        def pair_half(s, c):
            t = DEALT[s]
            return pairs[c][:, t // 2, :].bitcast(BF16).rearrange("p (m e) -> p m e", e=2)[:, :, t % 2]

        def add_term(acc, src, c, start, stop):
            for mb in range(4):
                cols = slice(BANK * c + P * mb, BANK * c + P * (mb + 1))
                nc.tensor.matmul(
                    acc[:, P * mb : P * (mb + 1)], src[:, cols], ident[:],
                    start=(start and mb == 0), stop=(stop and mb == 3), is_transpose=True,
                )

        def open_sums(s):
            for c in range(CHUNKS):
                sums[s, c] = bank("z%d" % c)
                add_term(sums[s, c], weather_sb[s], c, True, False)
                if s < SLICES - 1 and (c < CHUNKS - 1 or s == 6):
                    add_term(sums[s, c], scaled[s], c, False, False)

        def close_sum(s, c):
            acc = sums[s, c]
            if c == CHUNKS - 1 and s < 6:
                add_term(acc, scaled[s], c, False, False)
            add_term(acc, page_b[s % 2], c, False, True)
            if s < 4:
                if s == 0:
                    z_rows[c] = shared.tile([P, 4, 2, P, 2], BF16, name="first_rows%d" % c, offset=AT_TURNED + 4096 * c)
                nc.scalar.copy(
                    z_rows[c][:, :, :, 32 * s : 32 * (s + 1), :],
                    acc[:].rearrange("m (b p u e) -> m b u p e", b=4, u=2, e=2),
                )
            elif s == 4:
                z_rows[c] = shared.tile([P, BANK], F32, name="single_rows%d" % c, offset=AT_TURNED + 4096 * c)
                nc.scalar.copy(z_rows[c][:], acc[:])
                nc.scalar.copy(pair_half(s, c), turn_back(z_rows[c][:], "x%d" % (c % 2))[:])
            else:
                if DEALT[s] == 0:
                    z_rows[c] = shared.tile([P, BANK, 2], BF16, name="pair_rows%d" % c, offset=AT_TURNED + 4096 * c)
                nc.scalar.copy(z_rows[c][:, :, DEALT[s]], acc[:])

        def turn_back(words, tag):
            acc = bank(tag)
            for i in range(4):
                nc.tensor.transpose(acc[:, P * i : P * (i + 1)], words[:, P * i : P * (i + 1)], ident[:])
            return acc

        def new_z_k(chunks, i):
            at = AT_Z_K[i] if chunks == 2 else AT_Z_K[i // 2] + 4096 * (i % 2)
            return shared.tile([P, chunks * 4 * BANK], BF16, name="z_k%d_%d" % (chunks, i), offset=at, align_bytes=64)

        def quantize_z(z_k, chunks, i):
            if chunks == 2:
                z_c = shared.tile([P, 2 * BANK], U32, name="z_first%d" % i, offset=(AT_LATE_CODES, AT_Z_CODES[1])[i], align_bytes=64)
            else:
                z_c = work.tile([P, BANK], U32, name="z_c", tag="z_c", bufs=4, align_bytes=64)
            z_s = shared.tile([P, chunks * BANK], U8, name="z_s", offset=AT_ROWS[1] + 5120, align_bytes=64)
            nc.vector.quantize_mx(out=z_c[:].bitcast(FP8X4), scales=z_s[:], in_=z_k[:])
            return [(z_c[:, chunk(i)], z_s[:, chunk(i)]) for i in range(chunks)]

        z_first = []
        z_turned = []

        def finish_first_pass():
            for pair in range(2):
                z_k = new_z_k(2, pair)
                for j in range(2):
                    words = z_rows[2 * pair + j][:].rearrange("m b u p e -> m (b u p e)").bitcast(F32)
                    for half in range(2):
                        acc = turn_back(words[:, chunk(half)], "x%d" % half)
                        nc.scalar.copy(
                            z_k[:].bitcast(F32)[:, chunk(2 * j + half)].rearrange("p (b m u) -> p b m u", b=2, u=2),
                            acc[:].rearrange("p (b u m) -> p b m u", b=2, u=2),
                        )
                z_turned.append(z_k)

        def after(kind, s):
            if kind == "a":
                gelu_gain(s)
                if s == 1:
                    open_sums(0)
                    load_weather(2)
                return
            if s == SLICES - 1:
                add_last_page(s)
                return
            for c in range(CHUNKS):
                close_sum(s, c)
                if s == 6:
                    words = z_rows[c][:].rearrange("m x e -> m (x e)").bitcast(F32)
                    acc = turn_back(words, ("s0", "s1", "x0", "x1")[c])
                    nc.scalar.copy(pairs[c][:, 0, :], acc[:])
            if s == 3:
                finish_first_pass()
            if s + 1 < SLICES:
                open_sums(s + 1)
                if s + 3 < SLICES:
                    load_weather(s + 3)

        order = [("a", 0), ("a", 1), ("a", 2), ("b", 0), ("b", 1)]
        for s in range(3, SLICES - 1):
            order.extend([("a", s), ("b", s - 1)])
        order.extend([("b", 6), ("b", 7), ("a", 7)])

        def ahead(n):
            if n < len(order):
                if order[n][1] >= 4:
                    load_dealt_wg(*order[n])
                if order[n] == ("b", 7):
                    first_products("a", 7)
                if order[n] != ("a", 7):
                    first_products(*order[n])

        for s in range(2):
            pollen[s] = work.tile([P, S], F32, name="made", tag="made_a", bufs=3)
            placed["a", s] = work.tile([P, S], F32, name="placed", tag="placed", bufs=3)

        def early_values(s, lo, hi, tag):
            h, at = lo // BANK, lo % BANK
            acc = bank(tag)
            nc.tensor.matmul_mx(
                out=acc[:, 0 : hi - lo], lhsT=w1_early[:, 2 * P * s : 2 * P * (s + 1)].bitcast(FP4X4),
                lhsT_scale=w1_s[:, P * s : P * (s + 1)], rhs=v_w[:, lo:hi].bitcast(FP8X4),
                rhs_scale=v_s[h][:, at : at + hi - lo], start=True, stop=True,
            )
            nc.scalar.copy(pollen[s][:, lo:hi], acc[:, 0 : hi - lo])
            wg = wg1_sb[0][:] if lo == 0 else wg1_sb[1][:, lo - FIRST : hi - FIRST]
            (nc.vector if lo == 0 else nc.gpsimd).tensor_tensor(placed["a", s][:, lo:hi], pollen[s][:, lo:hi], wg, MULT)

        for s in range(2):
            early_values(s, 0, FIRST, "s%d" % s)
        for s in range(2):
            nc.vector.tensor_copy(page_a[s][:].indirect(list2[:, 0 : FIRST // 16]), placed["a", s][:, 0:FIRST])
        for s in range(2):
            early_values(s, FIRST, BANK, ("x0", "s0")[s])
            early_values(s, BANK, S, ("x1", "s1")[s])
            nc.vector.tensor_copy(page_a[s][:].indirect(list2[:, FIRST // 16 : S // 16]), placed["a", s][:, FIRST:S])
        prepare_w2()
        load_weather(0)
        load_weather(1)
        first_products("a", 2)
        weigh("a", 2)
        page_b = []
        for i in range(2):
            page_b.append(shared.tile([P, T2], F32, name="page_b%d" % i, offset=(AT_PAGE_B0, AT_PAGE_B1)[i]))
            nc.gpsimd.memset(page_b[i][:], 0.0)
        ahead(3)
        ahead(4)
        weigh(*order[3])
        ahead(5)
        weigh(*order[4])
        ident = shared.tile([P, P], F32, name="ident", offset=AT_IDENT)
        make_identity(nc, ident[:])
        deal_w1()
        after("a", 0)
        after("a", 1)
        cast_w3()
        pairs = [shared.tile([P, 2, BANK], F32, name="pairs%d" % c, offset=AT_PAIRS + 4096 * c) for c in range(CHUNKS)]
        for n in range(2, len(order) - 1):
            scatter(*order[n])
            if n + 3 < len(order):
                weigh(*order[n + 3])
            ahead(n + 4)
            after(*order[n])
            if order[n] == ("b", 5):
                for i in range(2):
                    quantize_w3(i)
                z_first.extend(quantize_z(z_turned[0], 2, 0))
        last = SLICES - 1
        scatter("a", last)

        gelu_last = []
        outs, woven, z_last = {}, {}, {}

        def columns(i):
            return slice(*PIECES[i])

        def in_chunk(i):
            lo, hi = PIECES[i]
            return lo // BANK, slice(lo % BANK, lo % BANK + hi - lo)

        def gelu_of(i):
            lo, hi = PIECES[i]
            return gelu_last[lo // (2 * BANK)][:, lo % (2 * BANK) : lo % (2 * BANK) + hi - lo]

        def gelu(i):
            lo, hi = PIECES[i]
            if lo % (2 * BANK) == 0:
                at = (AT_TURNED + 3 * 4096, AT_PAIRS)[lo // (2 * BANK)]
                gelu_last.append(shared.tile([P, 2 * BANK], F32, name="last_gelu%d" % i, offset=at))
            nc.scalar.activation(gelu_of(i), page_a[last % 2][:, columns(i)], GELU)

        def finish(i):
            c, cols = in_chunk(i)
            nc.vector.scalar_tensor_tensor(
                pair_half(last, c)[:, cols], gelu_of(i), gain_sb[:, 11:12], rest[c][:, cols], MULT, ADD
            )

        def copy_on(engine, dst, src):
            if engine == "vector":
                nc.vector.tensor_copy(dst, src)
            else:
                nc.scalar.copy(dst, src)

        def weave(i, engine):
            lo, hi = PIECES[i]
            c, cols = in_chunk(i)
            woven[i] = shared.tile([P, 4 * (hi - lo)], BF16, name="woven%d" % i, offset=AT_WOVEN[i], align_bytes=64)
            copy_on(engine, woven[i][:].bitcast(F32).rearrange("p (m u) -> p m u", u=2), pairs[c][:, :, cols].rearrange("p u m -> p m u"))

        def quantize_last(i):
            lo, hi = PIECES[i]
            codes = shared.tile([P, hi - lo], U32, name="last_c%d" % i, offset=(AT_Z_CODES[0] if i < 4 else AT_LATE_CODES + 12032 - 6144) + 4 * lo, align_bytes=64)
            scales = keep.tile([P, hi - lo], U8, name="last_s%d" % i, align_bytes=64)
            nc.vector.quantize_mx(out=codes[:].bitcast(FP8X4), scales=scales[:], in_=woven[i][:])
            z_last[i] = (codes[:], scales[:])

        def groups(i):
            lo, hi = PIECES[i]
            per = BANK // (hi - lo)
            if i == 0:
                return [range(0, 1), range(1, NT)]
            return [range(a, min(a + per, NT)) for a in range(0, NT, per)]

        def last_product(i, b):
            lo, hi = PIECES[i]
            c, cols = in_chunk(i)
            z = (z_first[c][0][:, cols], z_first[c][1][:, cols]) if b == 0 else z_last[i]
            for g, blocks in enumerate(groups(i)):
                if b == 0:
                    outs[i, g] = bank(OUT_BANKS[i][g])
                for j, a in enumerate(blocks):
                    codes, scales = w3_blocks[NT * b + a]
                    nc.tensor.matmul_mx(
                        out=outs[i, g][:, j * (hi - lo) : (j + 1) * (hi - lo)], lhsT=codes.bitcast(FP8X4), lhsT_scale=scales,
                        rhs=z[0].bitcast(FP8X4), rhs_scale=z[1],
                        start=(b == 0 and j == 0), stop=(b == 1 and j == len(blocks) - 1),
                    )

        def quantize_first(c):
            codes = shared.tile([P, BANK], U32, name="z_first%d" % c, offset=(AT_Z_CODES[1] + 2048, AT_PAIRS + 2 * 4096)[c - 2], align_bytes=64)
            scales = keep.tile([P, BANK], U8, name="z_first_s%d" % c, align_bytes=64)
            nc.vector.quantize_mx(
                out=codes[:].bitcast(FP8X4), scales=scales[:], in_=z_turned[1][:, 4 * BANK * (c - 2) : 4 * BANK * (c - 1)]
            )
            z_first.append((codes[:], scales[:]))

        stored = []

        def leave(i, engines):
            lo, hi = PIECES[i]
            for g, blocks in enumerate(groups(i)):
                n = len(stored)
                result = shared.tile([P, len(blocks), hi - lo], F32, name="result%d" % n, offset=AT_RESULTS[n // 4] + 2048 * (n % 4))
                stored.append(result)
                copy_on(engines[g], result[:].rearrange("p a m -> p (a m)"), outs[i, g][:, 0 : len(blocks) * (hi - lo)])
                rows = out[P * blocks[0] : P * (blocks[-1] + 1), columns(i)]
                nc.sync.dma_start(rows.rearrange("(a p) m -> p a m", p=P), result[:])

        for i in range(2):
            last_product(i, 0)
        quantize_first(2)
        for i in range(3):
            gelu(i)
            finish(i)
        weave(0, "scalar")
        weave(1, "scalar")
        for i in range(3, 6):
            gelu(i)
        quantize_last(0)
        quantize_last(1)
        weave(2, "vector")
        last_product(0, 1)
        last_product(1, 1)
        leave(0, ("scalar",) * 2)
        last_product(2, 0)
        finish(3)
        quantize_last(2)
        leave(1, ("scalar",) * 2)
        last_product(2, 1)
        last_product(3, 0)
        weave(3, "vector")
        finish(4)
        quantize_last(3)
        finish(5)
        last_product(3, 1)
        leave(2, ("scalar",) * 3)
        quantize_first(3)
        weave(4, "vector")
        last_product(4, 0)
        weave(5, "vector")
        last_product(5, 0)
        quantize_last(4)
        quantize_last(5)
        leave(3, ("scalar",) * 3)
        last_product(4, 1)
        last_product(5, 1)
        leave(4, ("vector", "scalar"))
        leave(5, ("scalar", "vector"))
